import numpy as np
import ml_dtypes


def mxq(x, axis, fmt="e4m3"):
    dtype, down = {"e4m3": (ml_dtypes.float8_e4m3fn, 7), "e5m2": (ml_dtypes.float8_e5m2, 14)}[fmt]
    v = np.moveaxis(np.asarray(x, np.float32).astype(ml_dtypes.bfloat16).astype(np.float64), axis, -1)
    blocks = v.reshape(v.shape[:-1] + (-1, 32))
    amax = np.abs(blocks).max(-1, keepdims=True)
    byte = np.maximum(np.where(amax > 0, np.frexp(amax)[1] - 1 + 127, 0) - down, 1)
    scale = np.exp2(byte - 127.0)
    codes = (blocks / scale).astype(np.float32).astype(dtype).astype(np.float64)
    return np.moveaxis((codes * scale).reshape(v.shape), -1, axis)


WIDE = False


def mx_kscale(k):
    if not WIDE:
        return np.ones(k)
    levels = np.array([10, -10, 5, -5, 0])
    if k % 512:
        return np.exp2(np.random.permutation(np.resize(levels, k // 32))).repeat(32)
    a = np.empty((k // 512, 16))
    for p in range(k // 512):
        a[p, :8] = np.random.permutation(np.resize(levels, 8))
        for g in range(8):
            far = levels[np.abs(levels - a[p, g]) >= 10]
            a[p, g + 8] = far[np.random.randint(len(far))]
    return np.exp2(a.ravel()).repeat(32)


def f64(x):
    return np.asarray(x).astype(np.float64)


def striped(idx):
    return np.tile(idx.reshape(-1, 16).T, (8, 1)).astype(np.uint16)


def unstriped(offs):
    return offs[:16].T.reshape(-1).astype(np.int64)


E2M1 = np.array([0.0, 0.5, 1.0, 1.5, 2.0, 3.0, 4.0, 6.0, -0.0, -0.5, -1.0, -1.5, -2.0, -3.0, -4.0, -6.0])


def pack_weight(w, fmt):
    k, n = w.shape
    w = f64(np.asarray(w, np.float32).astype(ml_dtypes.bfloat16)).reshape(k // 32, 32, n)
    amax = np.abs(w).max(1)
    if fmt == "e4m3":
        byte = np.frexp(amax)[1] - 1 + 127 - 7
    else:
        mant, ex = np.frexp(amax / 6.0)
        byte = np.where(mant > 0.5, ex, ex - 1) + 127
    byte = np.clip(np.where(amax > 0, byte, 1), 1, 254)
    scaled = (w * np.exp2(127.0 - byte)[:, None, :]).reshape(k, n).astype(np.float32)
    by_word = np.ascontiguousarray(scaled.reshape(k // 512, 128, 4, n).transpose(0, 1, 3, 2))
    if fmt == "e4m3":
        words = by_word.astype(ml_dtypes.float8_e4m3fn).view(np.uint8)
    else:
        c = by_word.astype(ml_dtypes.float4_e2m1fn).view(np.uint8) & 0xF
        words = (c[..., 0::2] | (c[..., 1::2] << 4)).reshape(k // 512, 128, 2 * n)
    return np.ascontiguousarray(words), np.ascontiguousarray(byte.astype(np.uint8).reshape(k // 512, 16, n))


def unpack_weight(words, scales, fmt):
    g, _, n = scales.shape
    words = np.ascontiguousarray(words).reshape(g, 128, n, -1)
    if fmt == "e4m3":
        vals = words.view(ml_dtypes.float8_e4m3fn).astype(np.float64)
    else:
        nib = np.empty((g, 128, n, 4), np.uint8)
        nib[..., 0::2] = words & 0xF
        nib[..., 1::2] = words >> 4
        vals = E2M1[nib]
    vals = vals * np.repeat(np.exp2(scales.astype(np.float64) - 127.0), 8, axis=1)[..., None]
    return vals.transpose(0, 1, 3, 2).reshape(g * 512, n)


def gelu(v):
    return 0.5 * v * (1.0 + np.tanh(np.sqrt(2.0 / np.pi) * (v + 0.044715 * v**3)))


K, T, S, H, T2, P, N = 1024, 2048, 1024, 1024, 2048, 1024, 512

def setup_inputs():
    n = np.random.standard_normal
    s = mx_kscale(K)[:, None]
    u = mx_kscale(H)[:, None]
    tab_words, tab_scales = pack_weight(n((K, T)) * s, "e4m3")
    w1_words, w1_scales = pack_weight(n((K, H)) / np.sqrt(K) / s * u.T, "e2m1")
    return {
        "tab_words": tab_words, "tab_scales": tab_scales,
        "offs": striped(np.random.permutation(T)[:S]),
        "w1_words": w1_words, "w1_scales": w1_scales,
        "wgs": np.exp(0.3 * n((128, S))).astype(np.float32),
        "page0": (n((H, T2)) * u).astype(np.float32),
        "offs2": striped(np.random.permutation(T2)[:S]),
        "offs3": striped(np.random.permutation(T2)[:P]),
        "low": ((0.6 * n((H, P)) - 0.3) * u).astype(np.float32),
        "bias": (0.5 * n(H) * u[:, 0]).astype(np.float32),
        "w2": (n((H, N)) / np.sqrt(H) / u).astype(np.float32),
    }

def reference(tab_words, tab_scales, offs, w1_words, w1_scales, wgs, page0, offs2, offs3, low, bias, w2):
    v = unpack_weight(tab_words, tab_scales, "e4m3")[:, unstriped(offs)]
    w1 = unpack_weight(w1_words, w1_scales, "e2m1")
    h = w1.T @ v
    page = f64(page0).copy()
    page[:, unstriped(offs2)] = np.tile(f64(wgs), (H // 128, 1)) * h
    x = page[:, unstriped(offs3)]
    z = np.maximum(x, f64(low)) - f64(bias)[:, None]
    zq = mxq(z, 0, "e4m3")
    w2q = mxq(f64(w2), 0, "e4m3")
    return w2q.T @ zq

@@ -1,0 +1,334 @@
+from contextlib import ExitStack
+
+import concourse.mybir as mybir
+from concourse.masks import make_identity
+
+K, T, S, H, T2, M, N = 1024, 2048, 1024, 1024, 2048, 1024, 512
+FLOPS = 2 * K * H * S + 2 * H * N * M
+
+F32 = mybir.dt.float32
+BF16 = mybir.dt.bfloat16
+I32 = mybir.dt.int32
+U32 = mybir.dt.uint32
+U16 = mybir.dt.uint16
+U8 = mybir.dt.uint8
+FP8X4 = mybir.dt.float8_e4m3fn_x4
+FP4X4 = mybir.dt.float4_e2m1fn_x4
+ALU = mybir.AluOpType
+IDENT = mybir.ActivationFunctionType.Identity
+
+P = 128
+HALF = 512
+PIECE = 256
+TILES = H // P
+PASSES = 2
+
+
+def tile_list_fetal_slice_mosaic_kernel(
+    tc, tab_words, tab_scales, offs, w1_words, w1_scales, wgs, page0, offs2, offs3, low, bias, w2, out
+):
+    nc = tc.nc
+    with ExitStack() as ctx:
+        keep = ctx.enter_context(tc.tile_pool(name="keep", bufs=1))
+        big = ctx.enter_context(tc.tile_pool(name="big", bufs=4))
+        xs = ctx.enter_context(tc.tile_pool(name="xs", bufs=1))
+        ring = ctx.enter_context(tc.tile_pool(name="ring", bufs=2))
+        stage = ctx.enter_context(tc.tile_pool(name="stage", bufs=10))
+        acc_pool = ctx.enter_context(tc.psum_pool(name="acc", bufs=6))
+        turn_pool = ctx.enter_context(tc.psum_pool(name="turn", bufs=1))
+
+        idx = keep.tile([P, S // 16], U16, name="idx")
+        idx2 = keep.tile([P, S // 16], U16, name="idx2")
+        idx3 = keep.tile([P, M // 16], U16, name="idx3")
+
+        nc.sync.dma_start(idx[:], offs)
+        nc.sync.dma_start(idx2[:], offs2)
+        nc.sync.dma_start(idx3[:], offs3)
+        w1_view = w1_words.rearrange("a p c -> p a c")
+        w1_first = keep.tile([P, PASSES, 2 * P], U8, name="w1_first", tag="w1_first", align_bytes=64)
+        nc.sync.dma_start(out=w1_first[:].bitcast(I32), in_=w1_view[:, :, 0 : 2 * P].bitcast(I32))
+        tab_sc = big.tile([P, T], U8, name="tab_sc", tag="big", align_bytes=64)
+        nc.vector.memset(tab_sc[:].bitcast(I32), 0)
+        tab_w = []
+
+        def load_tab_words(a):
+            t = big.tile([P, T], I32, name=f"tab_w{a}", tag="big", align_bytes=64)
+            nc.sync.dma_start(out=t[:], in_=tab_words[a].rearrange("p t i -> p (t i)").bitcast(I32))
+            tab_w.append(t)
+
+        load_tab_words(0)
+        for q in range(4):
+            nc.scalar.dma_start(
+                out=tab_sc[32 * q : 32 * q + 8, :].bitcast(I32),
+                in_=tab_scales[:, 4 * q : 4 * q + 4, :].bitcast(I32),
+            )
+        load_tab_words(1)
+        w1_sc = keep.tile([P, PASSES, H], U8, name="w1_sc", align_bytes=64)
+        nc.gpsimd.memset(w1_sc[:].bitcast(I32), 0)
+        for q in range(4):
+            nc.gpsimd.dma_start(
+                out=w1_sc[32 * q : 32 * q + 4, :, :].bitcast(I32),
+                in_=w1_scales[:, 4 * q : 4 * q + 4, :].rearrange("a r c -> r a c").bitcast(I32),
+            )
+        ident_f32 = keep.tile([P, P], F32, name="ident_f32")
+        make_identity(nc, ident_f32[:])
+        ident_bf = keep.tile([P, P], BF16, name="ident_bf")
+        nc.scalar.activation(out=ident_bf[:], in_=ident_f32[:], func=IDENT)
+        wgs_sb = keep.tile([P, S], F32, name="wgs_sb")
+        nc.sync.dma_start(out=wgs_sb[:, 0:HALF], in_=wgs[:, 0:HALF])
+        pages = []
+
+        def rows_of(matrix, c):
+            if c < 4:
+                return matrix[c * P : (c + 1) * P, :]
+            return matrix[HALF:, :].rearrange("(b t q) m -> t b q m", t=4, q=8)[c - 4]
+
+        def load_page(c):
+            page = big.tile([P, T2], F32, name=f"page{c}", tag="big", align_bytes=64)
+            nc.sync.dma_start(out=page[:], in_=rows_of(page0, c))
+            pages.append(page)
+
+        load_page(0)
+        nc.sync.dma_start(out=wgs_sb[:, HALF:S], in_=wgs[:, HALF:S])
+
+        v_sc0 = keep.tile([P, S], U8, name="v_sc0", align_bytes=64)
+        v_sc1 = keep.tile([P, S], U8, name="v_sc1", align_bytes=64)
+        nc.vector.memset(v_sc1[:].bitcast(I32), 0)
+        v_sc = [v_sc0, v_sc1]
+        v_w = [keep.tile([P, S], U32, name=f"v_w{a}", tag=f"v_w{a}", align_bytes=64) for a in range(PASSES)]
+        for s in range(2):
+            cols = slice(s * HALF, (s + 1) * HALF)
+            part = idx[:, s * 32 : (s + 1) * 32]
+            nc.vector.tensor_copy(v_w[0][:, cols], tab_w[0][:].bitcast(U32).indirect(part))
+            nc.vector.tensor_copy(v_sc0[:, cols], tab_sc[:].indirect(part))
+            nc.scalar.dma_start(out=v_sc1[0:112, cols].bitcast(I32), in_=v_sc0[4:116, cols].bitcast(I32))
+            nc.vector.tensor_copy(v_w[1][:, cols], tab_w[1][:].bitcast(U32).indirect(part))
+        w1_rest = big.tile([P, PASSES, 2 * (H - P)], U8, name="w1_rest", tag="big", align_bytes=64)
+        nc.sync.dma_start(out=w1_rest[:].bitcast(I32), in_=w1_view[:, :, 2 * P :].bitcast(I32))
+
+        h_sb = [keep.tile([P, S], F32, name=f"h{c}", tag=f"h{c}", align_bytes=64) for c in range(TILES)]
+
+        def first_product(c, late_codes, late_sc):
+            for s in range(2):
+                cols = slice(s * HALF, (s + 1) * HALF)
+                acc = acc_pool.tile([P, HALF], F32, name="acc", tag="acc")
+                for a in range(PASSES):
+                    if c == 0:
+                        codes, scales = w1_first[:, a, :], w1_sc[:, a, 0:P]
+                    elif c < 4:
+                        codes, scales = w1_rest[:, a, 2 * P * (c - 1) : 2 * P * c], w1_sc[:, a, c * P : (c + 1) * P]
+                    else:
+                        codes, scales = late_codes[:, a, c - 4, :], late_sc[:, a, c - 4, :]
+                    nc.tensor.matmul_mx(
+                        out=acc[:],
+                        lhsT=codes.bitcast(FP4X4),
+                        lhsT_scale=scales,
+                        rhs=v_w[a][:, cols].bitcast(FP8X4),
+                        rhs_scale=v_sc[a][:, cols],
+                        start=(a == 0),
+                        stop=(a == PASSES - 1),
+                    )
+                nc.scalar.copy(out=h_sb[c][:, cols], in_=acc[:])
+
+        for c in range(4):
+            first_product(c, None, None)
+        load_page(1)
+        bias_rows = big.tile([P, P], F32, name="bias_rows", tag="big", align_bytes=64)
+        nc.gpsimd.memset(bias_rows[:], 0.0)
+        nc.sync.dma_start(out=bias_rows[0:4, :], in_=bias[0:HALF].rearrange("(c p) -> c p", p=P))
+        nc.sync.dma_start(
+            out=bias_rows[4:TILES, :].rearrange("t (b q) -> t b q", q=8),
+            in_=bias[HALF:].rearrange("(b t q) -> t b q", t=4, q=8),
+        )
+        bias_turned = turn_pool.tile([P, P], F32, name="bias_turned", tag="back")
+        nc.tensor.transpose(bias_turned[:], bias_rows[:], ident_f32[:])
+        neg_bias = keep.tile([P, TILES], F32, name="neg_bias")
+        nc.scalar.activation(out=neg_bias[:], in_=bias_turned[:, 0:TILES], func=IDENT, scale=-1.0)
+
+        floor = [keep.tile([P, M], F32, name=f"floor{c}") for c in range(TILES)]
+
+        def load_floor(c):
+            raw = big.tile([P, M], F32, name="low_raw", tag="big", align_bytes=64)
+            nc.sync.dma_start(out=raw[:], in_=rows_of(low, c))
+            nc.scalar.activation(out=floor[c][:], in_=raw[:], func=IDENT, bias=neg_bias[:, c : c + 1])
+
+        w2_codes = keep.tile([P, PASSES, N], U32, name="w2_codes", align_bytes=64)
+        w2_sc = keep.tile([P, PASSES, N], U8, name="w2_sc", align_bytes=64)
+        w2_bf = keep.tile([P, PASSES, N, 4], BF16, name="w2_bf", align_bytes=64)
+
+        def load_w2(g):
+            raw = big.tile([P, 4, N], F32, name="w2_raw", tag="big", align_bytes=64)
+            if g == 0:
+                nc.sync.dma_start(out=raw[:], in_=w2[0:HALF, :].rearrange("(p j) n -> p j n", j=4))
+            else:
+                for t in range(4):
+                    nc.sync.dma_start(out=raw[:, t, :], in_=rows_of(w2, 4 + t))
+            nc.scalar.copy(out=w2_bf[:, g, :, :], in_=raw[:].rearrange("p j n -> p n j"))
+
+        weights = [wgs_sb] * 4
+
+        def load_weights(t):
+            if t < PASSES:
+                tile = keep.tile([P, S], F32, name="wgs_late", tag=f"v_w{t}", align_bytes=64)
+            else:
+                tile = keep.tile([P, S], F32, name="wgs_late", tag=f"h{t - 1}", align_bytes=64)
+            for rep in range(4):
+                nc.sync.dma_start(
+                    out=tile[32 * rep : 32 * rep + 32, :],
+                    in_=wgs.rearrange("(b t q) s -> t b q s", t=4, q=8)[t],
+                )
+            weights.append(tile)
+
+        def scatter(c, lo, hi):
+            nc.vector.tensor_tensor(
+                pages[c][:].indirect(idx2[:, lo // 16 : hi // 16]), h_sb[c][:, lo:hi], weights[c][:, lo:hi], ALU.mult
+            )
+
+        z_t = keep.tile([P, M // P, 2, P], F32, name="z_t")
+        z_late = keep.tile([P, M // PIECE, 4, PIECE], BF16, name="z_late")
+        z_codes = {}
+        z_sc = [keep.tile([P, M], U8, name=f"z_sc{g}", align_bytes=64) for g in range(PASSES)]
+
+        def gather(c, x, lo, hi):
+            nc.vector.tensor_copy(x, pages[c][:].indirect(idx3[:, lo // 16 : hi // 16]))
+
+        def apply_floor(c, z, x, bound):
+            nc.vector.scalar_tensor_tensor(z, x, neg_bias[:, c : c + 1], bound, ALU.add, ALU.max)
+
+        def floor_whole(c, x):
+            if c >= 4:
+                by_piece = "p (q m) -> p q m"
+                apply_floor(
+                    c, z_late[:, :, c - 4, :], x[:].rearrange(by_piece, m=PIECE), floor[c][:].rearrange(by_piece, m=PIECE)
+                )
+                return
+            z = ring.tile([P, M], BF16, name="z", tag="z")
+            apply_floor(c, z[:], x[:], floor[c][:])
+            turned = turn_pool.tile([P, M // P, P], BF16, name="turned", tag="turned")
+            for b in range(M // P):
+                nc.tensor.transpose(turned[:, b, :], z[:, b * P : (b + 1) * P], ident_bf[:])
+            nc.scalar.copy(
+                out=z_t[:, :, :, 32 * c : 32 * (c + 1)],
+                in_=turned[:].bitcast(F32).rearrange("m b (l u) -> m b u l", u=2),
+            )
+
+        def turn_back(lo, words):
+            back = turn_pool.tile([P, 2, 2, P], F32, name="back", tag="back")
+            for b in range(2):
+                for u in range(2):
+                    nc.tensor.transpose(back[:, b, u, :], z_t[:, lo // P + b, u, :], ident_f32[:])
+            nc.scalar.copy(
+                out=words.rearrange("p (b m u) -> p b m u", b=2, u=2),
+                in_=back[:].rearrange("p b u m -> p b m u"),
+            )
+
+        def quantise_z(g, lo, hi, woven):
+            tag = f"h{5 + lo // HALF}" if g == 0 else f"codes{lo}"
+            codes = keep.tile([P, hi - lo], U32, name="z_codes", tag=tag, align_bytes=64)
+            nc.vector.quantize_mx(out=codes[:].bitcast(FP8X4), scales=z_sc[g][:, lo:hi], in_=woven[:])
+            z_codes[(g, lo)] = codes
+
+        out_view = out.rearrange("(j p) m -> p j m", p=P)
+
+        def product(lo, hi, shared):
+            start = lo // HALF * HALF
+            moving = [z_codes[(0, start)][:, lo - start : hi - start], z_codes[(1, lo)][:]]
+            for pair in range(2):
+                acc = acc_pool.tile([P, 2, hi - lo], F32, name="acc_out", tag="acc")
+                for g in range(PASSES):
+                    for j in range(2):
+                        n_cols = slice((2 * pair + j) * P, (2 * pair + j + 1) * P)
+                        nc.tensor.matmul_mx(
+                            out=acc[:, j, :],
+                            lhsT=w2_codes[:, g, n_cols].bitcast(FP8X4),
+                            lhsT_scale=w2_sc[:, g, n_cols],
+                            rhs=moving[g].bitcast(FP8X4),
+                            rhs_scale=z_sc[g][:, lo:hi],
+                            start=(g == 0 and j == 0),
+                            stop=(g == PASSES - 1 and j == 1),
+                        )
+                res = stage.tile([P, 2, hi - lo], F32, name="res", tag="res")
+                if shared and pair == 1:
+                    nc.vector.tensor_copy(out=res[:], in_=acc[:])
+                else:
+                    nc.scalar.copy(out=res[:], in_=acc[:])
+                nc.sync.dma_start(out=out_view[:, 2 * pair : 2 * pair + 2, lo:hi], in_=res[:])
+
+        scatter(0, 0, HALF)
+        scatter(0, HALF, S)
+        late_codes = keep.tile([P, PASSES, 4, 2 * P], U8, name="late_codes", tag="h0", align_bytes=64)
+        nc.vector.tensor_copy(
+            out=late_codes[:].bitcast(I32).rearrange("p a t (b w) -> p a t b w", w=4),
+            in_=w1_rest[:, :, 2 * (HALF - P) :].bitcast(I32).rearrange("p a (b t w) -> p a t b w", t=4, w=4),
+        )
+        late_sc = keep.tile([P, PASSES, 4, P], U8, name="late_sc", tag="w1_first", align_bytes=64)
+        nc.vector.tensor_copy(
+            out=late_sc[:].bitcast(I32).rearrange("p a t (b w) -> p a t b w", w=2),
+            in_=w1_sc[:, :, HALF:].bitcast(I32).rearrange("p a (b t w) -> p a t b w", t=4, w=2),
+        )
+        x = xs.tile([P, M], F32, name="x", tag="x")
+        gather(0, x[:], 0, M)
+        for c in range(1, TILES - 1):
+            if c > 1:
+                load_page(c)
+            load_floor(c - 1)
+            if c in (2, 3):
+                load_w2(c - 2)
+            if c >= 3:
+                load_weights(c - 3)
+            scatter(c, 0, S)
+            floor_whole(c - 1, x)
+            if c <= 2:
+                first_product(2 * c + 2, late_codes, late_sc)
+                first_product(2 * c + 3, late_codes, late_sc)
+            if c < TILES - 2:
+                x = xs.tile([P, M], F32, name="x", tag="x")
+                gather(c, x[:], 0, M)
+            if c == 4:
+                nc.vector.quantize_mx(
+                    out=w2_codes[:].rearrange("p g n -> p (g n)").bitcast(FP8X4),
+                    scales=w2_sc[:].rearrange("p g n -> p (g n)"),
+                    in_=w2_bf[:].rearrange("p g n j -> p (g n j)"),
+                )
+            if c >= 5:
+                lo = (c - 5) * HALF
+                woven = ring.tile([P, HALF * 4], BF16, name="woven", tag="woven", align_bytes=64)
+                for at in (0, PIECE):
+                    turn_back(lo + at, woven[:, at * 4 : (at + PIECE) * 4].bitcast(F32))
+                quantise_z(0, lo, lo + HALF, woven)
+        last = TILES - 1
+        load_floor(last - 1)
+        load_page(last)
+        load_floor(last)
+        scatter(last, 0, S)
+        x_before = keep.tile([P, M], F32, name="x_before", tag=f"h{last}", align_bytes=64)
+        x_last = {}
+
+        def gather_pair(q):
+            lo, hi = q * PIECE, (q + 1) * PIECE
+            gather(last - 1, x_before[:, lo:hi], lo, hi)
+            x_last[q] = keep.tile([P, PIECE], F32, name="x_last", tag=f"tail{q}", align_bytes=64)
+            gather(last, x_last[q][:], lo, hi)
+
+        def finish(q, lo, hi, tag):
+            inner = slice(lo - q * PIECE, hi - q * PIECE)
+            apply_floor(last - 1, z_late[:, q, 2, inner], x_before[:, lo:hi], floor[last - 1][:, lo:hi])
+            apply_floor(last, z_late[:, q, 3, inner], x_last[q][:, inner], floor[last][:, lo:hi])
+            woven = keep.tile([P, (hi - lo) * 4], BF16, name="woven_late", tag=tag, align_bytes=64)
+            target = woven[:].rearrange("p (m t) -> p m t", t=4)
+            source = z_late[:, q, :, inner].rearrange("p t m -> p m t")
+            if q == 3:
+                nc.vector.tensor_copy(out=target, in_=source)
+            else:
+                nc.scalar.copy(out=target, in_=source)
+            quantise_z(1, lo, hi, woven)
+            product(lo, hi, q >= 2)
+
+        gather_pair(0)
+        gather_pair(1)
+        for q in range(2):
+            finish(q, q * PIECE, (q + 1) * PIECE, f"tail{q + 2}")
+            gather_pair(q + 2)
+        finish(2, 2 * PIECE, 3 * PIECE, "tail0")
+        finish(3, 3 * PIECE, 3 * PIECE + P, "tail1")
+        finish(3, 3 * PIECE + P, M, "tail4")

@@ -34,8 +34,8 @@ def tile_list_fetal_slice_mosaic_kernel(
         xs = ctx.enter_context(tc.tile_pool(name="xs", bufs=1))
         ring = ctx.enter_context(tc.tile_pool(name="ring", bufs=2))
         stage = ctx.enter_context(tc.tile_pool(name="stage", bufs=10))
-        acc_pool = ctx.enter_context(tc.psum_pool(name="acc", bufs=6))
-        turn_pool = ctx.enter_context(tc.psum_pool(name="turn", bufs=1))
+        acc_pool = ctx.enter_context(tc.psum_pool(name="acc", bufs=4))
+        turn_pool = ctx.enter_context(tc.psum_pool(name="turn", bufs=2))
 
         idx = keep.tile([P, S // 16], U16, name="idx")
         idx2 = keep.tile([P, S // 16], U16, name="idx2")
@@ -45,7 +45,7 @@ def tile_list_fetal_slice_mosaic_kernel(
         nc.sync.dma_start(idx2[:], offs2)
         nc.sync.dma_start(idx3[:], offs3)
         w1_view = w1_words.rearrange("a p c -> p a c")
-        w1_first = keep.tile([P, PASSES, 2 * P], U8, name="w1_first", tag="w1_first", align_bytes=64)
+        w1_first = keep.tile([P, PASSES, 2 * P], U8, name="w1_first", align_bytes=64)
         nc.sync.dma_start(out=w1_first[:].bitcast(I32), in_=w1_view[:, :, 0 : 2 * P].bitcast(I32))
         tab_sc = big.tile([P, T], U8, name="tab_sc", tag="big", align_bytes=64)
         nc.vector.memset(tab_sc[:].bitcast(I32), 0)
@@ -78,14 +78,9 @@ def tile_list_fetal_slice_mosaic_kernel(
         nc.sync.dma_start(out=wgs_sb[:, 0:HALF], in_=wgs[:, 0:HALF])
         pages = []
 
-        def rows_of(matrix, c):
-            if c < 4:
-                return matrix[c * P : (c + 1) * P, :]
-            return matrix[HALF:, :].rearrange("(b t q) m -> t b q m", t=4, q=8)[c - 4]
-
         def load_page(c):
             page = big.tile([P, T2], F32, name=f"page{c}", tag="big", align_bytes=64)
-            nc.sync.dma_start(out=page[:], in_=rows_of(page0, c))
+            nc.sync.dma_start(out=page[:], in_=page0[c * P : (c + 1) * P, :])
             pages.append(page)
 
         load_page(0)
@@ -95,7 +90,7 @@ def tile_list_fetal_slice_mosaic_kernel(
         v_sc1 = keep.tile([P, S], U8, name="v_sc1", align_bytes=64)
         nc.vector.memset(v_sc1[:].bitcast(I32), 0)
         v_sc = [v_sc0, v_sc1]
-        v_w = [keep.tile([P, S], U32, name=f"v_w{a}", tag=f"v_w{a}", align_bytes=64) for a in range(PASSES)]
+        v_w = [keep.tile([P, S], U32, name=f"v_w{a}", align_bytes=64) for a in range(PASSES)]
         for s in range(2):
             cols = slice(s * HALF, (s + 1) * HALF)
             part = idx[:, s * 32 : (s + 1) * 32]
@@ -106,23 +101,20 @@ def tile_list_fetal_slice_mosaic_kernel(
         w1_rest = big.tile([P, PASSES, 2 * (H - P)], U8, name="w1_rest", tag="big", align_bytes=64)
         nc.sync.dma_start(out=w1_rest[:].bitcast(I32), in_=w1_view[:, :, 2 * P :].bitcast(I32))
 
-        h_sb = [keep.tile([P, S], F32, name=f"h{c}", tag=f"h{c}", align_bytes=64) for c in range(TILES)]
-
-        def first_product(c, late_codes, late_sc):
+        h_sb = [keep.tile([P, S], F32, name=f"h{c}", tag=f"h{c}") for c in range(TILES)]
+        for c in range(TILES):
             for s in range(2):
                 cols = slice(s * HALF, (s + 1) * HALF)
                 acc = acc_pool.tile([P, HALF], F32, name="acc", tag="acc")
                 for a in range(PASSES):
                     if c == 0:
-                        codes, scales = w1_first[:, a, :], w1_sc[:, a, 0:P]
-                    elif c < 4:
-                        codes, scales = w1_rest[:, a, 2 * P * (c - 1) : 2 * P * c], w1_sc[:, a, c * P : (c + 1) * P]
+                        codes = w1_first[:, a, :]
                     else:
-                        codes, scales = late_codes[:, a, c - 4, :], late_sc[:, a, c - 4, :]
+                        codes = w1_rest[:, a, 2 * P * (c - 1) : 2 * P * c]
                     nc.tensor.matmul_mx(
                         out=acc[:],
                         lhsT=codes.bitcast(FP4X4),
-                        lhsT_scale=scales,
+                        lhsT_scale=w1_sc[:, a, c * P : (c + 1) * P],
                         rhs=v_w[a][:, cols].bitcast(FP8X4),
                         rhs_scale=v_sc[a][:, cols],
                         start=(a == 0),
@@ -130,16 +122,10 @@ def tile_list_fetal_slice_mosaic_kernel(
                     )
                 nc.scalar.copy(out=h_sb[c][:, cols], in_=acc[:])
 
-        for c in range(4):
-            first_product(c, None, None)
         load_page(1)
         bias_rows = big.tile([P, P], F32, name="bias_rows", tag="big", align_bytes=64)
         nc.gpsimd.memset(bias_rows[:], 0.0)
-        nc.sync.dma_start(out=bias_rows[0:4, :], in_=bias[0:HALF].rearrange("(c p) -> c p", p=P))
-        nc.sync.dma_start(
-            out=bias_rows[4:TILES, :].rearrange("t (b q) -> t b q", q=8),
-            in_=bias[HALF:].rearrange("(b t q) -> t b q", t=4, q=8),
-        )
+        nc.sync.dma_start(out=bias_rows[0:TILES, :], in_=bias.rearrange("(c p) -> c p", p=P))
         bias_turned = turn_pool.tile([P, P], F32, name="bias_turned", tag="back")
         nc.tensor.transpose(bias_turned[:], bias_rows[:], ident_f32[:])
         neg_bias = keep.tile([P, TILES], F32, name="neg_bias")
@@ -149,7 +135,7 @@ def tile_list_fetal_slice_mosaic_kernel(
 
         def load_floor(c):
             raw = big.tile([P, M], F32, name="low_raw", tag="big", align_bytes=64)
-            nc.sync.dma_start(out=raw[:], in_=rows_of(low, c))
+            nc.sync.dma_start(out=raw[:], in_=low[c * P : (c + 1) * P, :])
             nc.scalar.activation(out=floor[c][:], in_=raw[:], func=IDENT, bias=neg_bias[:, c : c + 1])
 
         w2_codes = keep.tile([P, PASSES, N], U32, name="w2_codes", align_bytes=64)
@@ -158,81 +144,59 @@ def tile_list_fetal_slice_mosaic_kernel(
 
         def load_w2(g):
             raw = big.tile([P, 4, N], F32, name="w2_raw", tag="big", align_bytes=64)
-            if g == 0:
-                nc.sync.dma_start(out=raw[:], in_=w2[0:HALF, :].rearrange("(p j) n -> p j n", j=4))
-            else:
-                for t in range(4):
-                    nc.sync.dma_start(out=raw[:, t, :], in_=rows_of(w2, 4 + t))
+            nc.sync.dma_start(out=raw[:], in_=w2[g * 512 : (g + 1) * 512, :].rearrange("(p j) n -> p j n", j=4))
             nc.scalar.copy(out=w2_bf[:, g, :, :], in_=raw[:].rearrange("p j n -> p n j"))
-
-        weights = [wgs_sb] * 4
-
-        def load_weights(t):
-            if t < PASSES:
-                tile = keep.tile([P, S], F32, name="wgs_late", tag=f"v_w{t}", align_bytes=64)
-            else:
-                tile = keep.tile([P, S], F32, name="wgs_late", tag=f"h{t - 1}", align_bytes=64)
-            for rep in range(4):
-                nc.sync.dma_start(
-                    out=tile[32 * rep : 32 * rep + 32, :],
-                    in_=wgs.rearrange("(b t q) s -> t b q s", t=4, q=8)[t],
-                )
-            weights.append(tile)
 
         def scatter(c, lo, hi):
             nc.vector.tensor_tensor(
-                pages[c][:].indirect(idx2[:, lo // 16 : hi // 16]), h_sb[c][:, lo:hi], weights[c][:, lo:hi], ALU.mult
+                pages[c][:].indirect(idx2[:, lo // 16 : hi // 16]), h_sb[c][:, lo:hi], wgs_sb[:, lo:hi], ALU.mult
             )
 
-        z_t = keep.tile([P, M // P, 2, P], F32, name="z_t")
-        z_late = keep.tile([P, M // PIECE, 4, PIECE], BF16, name="z_late")
-        z_codes = {}
+        z_t = [keep.tile([P, M // P, 2, P], F32, name=f"z_t{g}") for g in range(PASSES)]
+        z_codes = [keep.tile([P, M], U32, name=f"z_codes{g}", align_bytes=64) for g in range(PASSES)]
         z_sc = [keep.tile([P, M], U8, name=f"z_sc{g}", align_bytes=64) for g in range(PASSES)]
 
         def gather(c, x, lo, hi):
             nc.vector.tensor_copy(x, pages[c][:].indirect(idx3[:, lo // 16 : hi // 16]))
 
-        def apply_floor(c, z, x, bound):
-            nc.vector.scalar_tensor_tensor(z, x, neg_bias[:, c : c + 1], bound, ALU.add, ALU.max)
+        def apply_floor(c, x, lo, hi):
+            z = ring.tile([P, hi - lo], BF16, name="z", tag="z", bufs=5)
+            nc.vector.scalar_tensor_tensor(
+                z[:], x, neg_bias[:, c : c + 1], floor[c][:, lo:hi], ALU.add, ALU.max
+            )
+            return z
 
-        def floor_whole(c, x):
-            if c >= 4:
-                by_piece = "p (q m) -> p q m"
-                apply_floor(
-                    c, z_late[:, :, c - 4, :], x[:].rearrange(by_piece, m=PIECE), floor[c][:].rearrange(by_piece, m=PIECE)
-                )
-                return
-            z = ring.tile([P, M], BF16, name="z", tag="z")
-            apply_floor(c, z[:], x[:], floor[c][:])
-            turned = turn_pool.tile([P, M // P, P], BF16, name="turned", tag="turned")
-            for b in range(M // P):
-                nc.tensor.transpose(turned[:, b, :], z[:, b * P : (b + 1) * P], ident_bf[:])
+        def turn(c, zs, lo, hi):
+            g, first = divmod(c, 4)
+            blocks = (hi - lo) // P
+            turned = turn_pool.tile([P, blocks, len(zs) * P], BF16, name="turned", tag="turned")
+            for i, z in enumerate(zs):
+                for b in range(blocks):
+                    nc.tensor.transpose(turned[:, b, i * P : (i + 1) * P], z[:, b * P : (b + 1) * P], ident_bf[:])
             nc.scalar.copy(
-                out=z_t[:, :, :, 32 * c : 32 * (c + 1)],
+                out=z_t[g][:, lo // P : hi // P, :, 32 * first : 32 * (first + len(zs))],
                 in_=turned[:].bitcast(F32).rearrange("m b (l u) -> m b u l", u=2),
             )
 
-        def turn_back(lo, words):
-            back = turn_pool.tile([P, 2, 2, P], F32, name="back", tag="back")
-            for b in range(2):
+        def turn_back(g, lo, blocks, words):
+            back = turn_pool.tile([P, blocks, 2, P], F32, name="back", tag="back")
+            for b in range(blocks):
                 for u in range(2):
-                    nc.tensor.transpose(back[:, b, u, :], z_t[:, lo // P + b, u, :], ident_f32[:])
+                    nc.tensor.transpose(back[:, b, u, :], z_t[g][:, lo // P + b, u, :], ident_f32[:])
             nc.scalar.copy(
-                out=words.rearrange("p (b m u) -> p b m u", b=2, u=2),
+                out=words.rearrange("p (b m u) -> p b m u", b=blocks, u=2),
                 in_=back[:].rearrange("p b u m -> p b m u"),
             )
 
         def quantise_z(g, lo, hi, woven):
-            tag = f"h{5 + lo // HALF}" if g == 0 else f"codes{lo}"
-            codes = keep.tile([P, hi - lo], U32, name="z_codes", tag=tag, align_bytes=64)
-            nc.vector.quantize_mx(out=codes[:].bitcast(FP8X4), scales=z_sc[g][:, lo:hi], in_=woven[:])
-            z_codes[(g, lo)] = codes
+            step = min(PIECE, hi - lo)
+            for at in range(0, hi - lo, step):
+                turn_back(g, lo + at, step // P, woven[:, at * 4 : (at + step) * 4].bitcast(F32))
+            nc.vector.quantize_mx(out=z_codes[g][:, lo:hi].bitcast(FP8X4), scales=z_sc[g][:, lo:hi], in_=woven[:])
 
         out_view = out.rearrange("(j p) m -> p j m", p=P)
 
         def product(lo, hi, shared):
-            start = lo // HALF * HALF
-            moving = [z_codes[(0, start)][:, lo - start : hi - start], z_codes[(1, lo)][:]]
             for pair in range(2):
                 acc = acc_pool.tile([P, 2, hi - lo], F32, name="acc_out", tag="acc")
                 for g in range(PASSES):
@@ -242,7 +206,7 @@ def tile_list_fetal_slice_mosaic_kernel(
                             out=acc[:, j, :],
                             lhsT=w2_codes[:, g, n_cols].bitcast(FP8X4),
                             lhsT_scale=w2_sc[:, g, n_cols],
-                            rhs=moving[g].bitcast(FP8X4),
+                            rhs=z_codes[g][:, lo:hi].bitcast(FP8X4),
                             rhs_scale=z_sc[g][:, lo:hi],
                             start=(g == 0 and j == 0),
                             stop=(g == PASSES - 1 and j == 1),
@@ -256,16 +220,6 @@ def tile_list_fetal_slice_mosaic_kernel(
 
         scatter(0, 0, HALF)
         scatter(0, HALF, S)
-        late_codes = keep.tile([P, PASSES, 4, 2 * P], U8, name="late_codes", tag="h0", align_bytes=64)
-        nc.vector.tensor_copy(
-            out=late_codes[:].bitcast(I32).rearrange("p a t (b w) -> p a t b w", w=4),
-            in_=w1_rest[:, :, 2 * (HALF - P) :].bitcast(I32).rearrange("p a (b t w) -> p a t b w", t=4, w=4),
-        )
-        late_sc = keep.tile([P, PASSES, 4, P], U8, name="late_sc", tag="w1_first", align_bytes=64)
-        nc.vector.tensor_copy(
-            out=late_sc[:].bitcast(I32).rearrange("p a t (b w) -> p a t b w", w=2),
-            in_=w1_sc[:, :, HALF:].bitcast(I32).rearrange("p a (b t w) -> p a t b w", t=4, w=2),
-        )
         x = xs.tile([P, M], F32, name="x", tag="x")
         gather(0, x[:], 0, M)
         for c in range(1, TILES - 1):
@@ -274,61 +228,42 @@ def tile_list_fetal_slice_mosaic_kernel(
             load_floor(c - 1)
             if c in (2, 3):
                 load_w2(c - 2)
-            if c >= 3:
-                load_weights(c - 3)
             scatter(c, 0, S)
-            floor_whole(c - 1, x)
-            if c <= 2:
-                first_product(2 * c + 2, late_codes, late_sc)
-                first_product(2 * c + 3, late_codes, late_sc)
-            if c < TILES - 2:
-                x = xs.tile([P, M], F32, name="x", tag="x")
-                gather(c, x[:], 0, M)
+            turn(c - 1, [apply_floor(c - 1, x[:], 0, M)], 0, M)
+            x = xs.tile([P, M], F32, name="x", tag="x")
+            gather(c, x[:], 0, M)
             if c == 4:
                 nc.vector.quantize_mx(
                     out=w2_codes[:].rearrange("p g n -> p (g n)").bitcast(FP8X4),
                     scales=w2_sc[:].rearrange("p g n -> p (g n)"),
                     in_=w2_bf[:].rearrange("p g n j -> p (g n j)"),
                 )
-            if c >= 5:
-                lo = (c - 5) * HALF
-                woven = ring.tile([P, HALF * 4], BF16, name="woven", tag="woven", align_bytes=64)
-                for at in (0, PIECE):
-                    turn_back(lo + at, woven[:, at * 4 : (at + PIECE) * 4].bitcast(F32))
-                quantise_z(0, lo, lo + HALF, woven)
+            if c == 5:
+                for lo in (0, HALF):
+                    woven = ring.tile([P, HALF * 4], BF16, name="woven", tag="woven", align_bytes=64)
+                    quantise_z(0, lo, lo + HALF, woven)
         last = TILES - 1
         load_floor(last - 1)
-        load_page(last)
         load_floor(last)
+        load_page(last)
+        turn(last - 1, [apply_floor(last - 1, x[:], 0, M)], 0, M)
         scatter(last, 0, S)
-        x_before = keep.tile([P, M], F32, name="x_before", tag=f"h{last}", align_bytes=64)
         x_last = {}
 
-        def gather_pair(q):
-            lo, hi = q * PIECE, (q + 1) * PIECE
-            gather(last - 1, x_before[:, lo:hi], lo, hi)
-            x_last[q] = keep.tile([P, PIECE], F32, name="x_last", tag=f"tail{q}", align_bytes=64)
-            gather(last, x_last[q][:], lo, hi)
+        def gather_last(q):
+            x_last[q] = ring.tile([P, PIECE], F32, name="x_last", tag="x_last")
+            gather(last, x_last[q][:], q * PIECE, (q + 1) * PIECE)
 
-        def finish(q, lo, hi, tag):
-            inner = slice(lo - q * PIECE, hi - q * PIECE)
-            apply_floor(last - 1, z_late[:, q, 2, inner], x_before[:, lo:hi], floor[last - 1][:, lo:hi])
-            apply_floor(last, z_late[:, q, 3, inner], x_last[q][:, inner], floor[last][:, lo:hi])
-            woven = keep.tile([P, (hi - lo) * 4], BF16, name="woven_late", tag=tag, align_bytes=64)
-            target = woven[:].rearrange("p (m t) -> p m t", t=4)
-            source = z_late[:, q, :, inner].rearrange("p t m -> p m t")
-            if q == 3:
-                nc.vector.tensor_copy(out=target, in_=source)
-            else:
-                nc.scalar.copy(out=target, in_=source)
+        def finish(q, lo, hi):
+            z = apply_floor(last, x_last[q][:, lo - q * PIECE : hi - q * PIECE], lo, hi)
+            turn(last, [z], lo, hi)
+            woven = stage.tile([P, (hi - lo) * 4], BF16, name="woven_last", tag="woven_last", bufs=5, align_bytes=64)
             quantise_z(1, lo, hi, woven)
-            product(lo, hi, q >= 2)
+            product(lo, hi, True)
 
-        gather_pair(0)
-        gather_pair(1)
-        for q in range(2):
-            finish(q, q * PIECE, (q + 1) * PIECE, f"tail{q + 2}")
-            gather_pair(q + 2)
-        finish(2, 2 * PIECE, 3 * PIECE, "tail0")
-        finish(3, 3 * PIECE, 3 * PIECE + P, "tail1")
-        finish(3, 3 * PIECE + P, M, "tail4")
+        gather_last(0)
+        for q in range(3):
+            gather_last(q + 1)
+            finish(q, q * PIECE, (q + 1) * PIECE)
+        finish(3, 3 * PIECE, 3 * PIECE + P)
+        finish(3, 3 * PIECE + P, M)

@@ -15,13 +15,21 @@ U8 = mybir.dt.uint8
 FP8X4 = mybir.dt.float8_e4m3fn_x4
 FP4X4 = mybir.dt.float4_e2m1fn_x4
 ALU = mybir.AluOpType
-IDENT = mybir.ActivationFunctionType.Identity
+IDENTITY = mybir.ActivationFunctionType.Identity
 
 P = 128
-HALF = 512
-PIECE = 256
-TILES = H // P
+PACK = 4
+QUADRANT = 32
+QUADRANTS = P // QUADRANT
+PER_COLUMN = 16
+BANK = 512
 PASSES = 2
+ROW_TILES = H // P
+TILES_A_PASS = ROW_TILES // PASSES
+LAST = ROW_TILES - 1
+PIECE = 256
+SHIFTED_ROWS = 112
+LAST_SPANS = [(0, PIECE), (PIECE, 2 * PIECE), (2 * PIECE, 3 * PIECE), (3 * PIECE, M - P), (M - P, M)]
 
 
 def tile_list_fetal_slice_mosaic_kernel(
@@ -30,16 +38,19 @@ def tile_list_fetal_slice_mosaic_kernel(
     nc = tc.nc
     with ExitStack() as ctx:
         keep = ctx.enter_context(tc.tile_pool(name="keep", bufs=1))
-        big = ctx.enter_context(tc.tile_pool(name="big", bufs=4))
-        xs = ctx.enter_context(tc.tile_pool(name="xs", bufs=1))
+        loads = ctx.enter_context(tc.tile_pool(name="loads", bufs=4))
+        picked = ctx.enter_context(tc.tile_pool(name="picked", bufs=1))
         ring = ctx.enter_context(tc.tile_pool(name="ring", bufs=2))
-        stage = ctx.enter_context(tc.tile_pool(name="stage", bufs=10))
-        acc_pool = ctx.enter_context(tc.psum_pool(name="acc", bufs=4))
-        turn_pool = ctx.enter_context(tc.psum_pool(name="turn", bufs=2))
+        stage = ctx.enter_context(tc.tile_pool(name="stage", bufs=2 * len(LAST_SPANS)))
+        sums = ctx.enter_context(tc.psum_pool(name="sums", bufs=4))
+        turns = ctx.enter_context(tc.psum_pool(name="turns", bufs=2))
 
-        idx = keep.tile([P, S // 16], U16, name="idx")
-        idx2 = keep.tile([P, S // 16], U16, name="idx2")
-        idx3 = keep.tile([P, M // 16], U16, name="idx3")
+        idx = keep.tile([P, S // PER_COLUMN], U16, name="idx")
+        idx2 = keep.tile([P, S // PER_COLUMN], U16, name="idx2")
+        idx3 = keep.tile([P, M // PER_COLUMN], U16, name="idx3")
+
+        def entries(listed, lo, hi):
+            return listed[:, lo // PER_COLUMN : hi // PER_COLUMN]
 
         nc.sync.dma_start(idx[:], offs)
         nc.sync.dma_start(idx2[:], offs2)
@@ -47,223 +58,230 @@ def tile_list_fetal_slice_mosaic_kernel(
         w1_view = w1_words.rearrange("a p c -> p a c")
         w1_first = keep.tile([P, PASSES, 2 * P], U8, name="w1_first", align_bytes=64)
         nc.sync.dma_start(out=w1_first[:].bitcast(I32), in_=w1_view[:, :, 0 : 2 * P].bitcast(I32))
-        tab_sc = big.tile([P, T], U8, name="tab_sc", tag="big", align_bytes=64)
+        tab_sc = loads.tile([P, T], U8, name="tab_sc", tag="load", align_bytes=64)
         nc.vector.memset(tab_sc[:].bitcast(I32), 0)
         tab_w = []
 
         def load_tab_words(a):
-            t = big.tile([P, T], I32, name=f"tab_w{a}", tag="big", align_bytes=64)
-            nc.sync.dma_start(out=t[:], in_=tab_words[a].rearrange("p t i -> p (t i)").bitcast(I32))
-            tab_w.append(t)
+            words = loads.tile([P, T], I32, name=f"tab_w{a}", tag="load", align_bytes=64)
+            nc.sync.dma_start(out=words[:], in_=tab_words[a].rearrange("p t i -> p (t i)").bitcast(I32))
+            tab_w.append(words)
 
         load_tab_words(0)
-        for q in range(4):
+        for quad in range(QUADRANTS):
             nc.scalar.dma_start(
-                out=tab_sc[32 * q : 32 * q + 8, :].bitcast(I32),
-                in_=tab_scales[:, 4 * q : 4 * q + 4, :].bitcast(I32),
+                out=tab_sc[QUADRANT * quad : QUADRANT * quad + PASSES * PACK, :].bitcast(I32),
+                in_=tab_scales[:, PACK * quad : PACK * (quad + 1), :].bitcast(I32),
             )
         load_tab_words(1)
         w1_sc = keep.tile([P, PASSES, H], U8, name="w1_sc", align_bytes=64)
         nc.gpsimd.memset(w1_sc[:].bitcast(I32), 0)
-        for q in range(4):
+        for quad in range(QUADRANTS):
             nc.gpsimd.dma_start(
-                out=w1_sc[32 * q : 32 * q + 4, :, :].bitcast(I32),
-                in_=w1_scales[:, 4 * q : 4 * q + 4, :].rearrange("a r c -> r a c").bitcast(I32),
+                out=w1_sc[QUADRANT * quad : QUADRANT * quad + PACK, :, :].bitcast(I32),
+                in_=w1_scales[:, PACK * quad : PACK * (quad + 1), :].rearrange("a r c -> r a c").bitcast(I32),
             )
         ident_f32 = keep.tile([P, P], F32, name="ident_f32")
         make_identity(nc, ident_f32[:])
         ident_bf = keep.tile([P, P], BF16, name="ident_bf")
-        nc.scalar.activation(out=ident_bf[:], in_=ident_f32[:], func=IDENT)
-        wgs_sb = keep.tile([P, S], F32, name="wgs_sb")
-        nc.sync.dma_start(out=wgs_sb[:, 0:HALF], in_=wgs[:, 0:HALF])
+        nc.scalar.activation(out=ident_bf[:], in_=ident_f32[:], func=IDENTITY)
+        wgs_sb = keep.tile([P, S], F32, name="wgs_sb", tag="wgs", align_bytes=64)
+        nc.sync.dma_start(out=wgs_sb[:], in_=wgs)
         pages = []
 
         def load_page(c):
-            page = big.tile([P, T2], F32, name=f"page{c}", tag="big", align_bytes=64)
+            page = loads.tile([P, T2], F32, name=f"page{c}", tag="load", align_bytes=64)
             nc.sync.dma_start(out=page[:], in_=page0[c * P : (c + 1) * P, :])
             pages.append(page)
 
         load_page(0)
-        nc.sync.dma_start(out=wgs_sb[:, HALF:S], in_=wgs[:, HALF:S])
 
         v_sc0 = keep.tile([P, S], U8, name="v_sc0", align_bytes=64)
         v_sc1 = keep.tile([P, S], U8, name="v_sc1", align_bytes=64)
         nc.vector.memset(v_sc1[:].bitcast(I32), 0)
         v_sc = [v_sc0, v_sc1]
         v_w = [keep.tile([P, S], U32, name=f"v_w{a}", align_bytes=64) for a in range(PASSES)]
-        for s in range(2):
-            cols = slice(s * HALF, (s + 1) * HALF)
-            part = idx[:, s * 32 : (s + 1) * 32]
+        for lo in range(0, S, BANK):
+            cols = slice(lo, lo + BANK)
+            part = entries(idx, lo, lo + BANK)
             nc.vector.tensor_copy(v_w[0][:, cols], tab_w[0][:].bitcast(U32).indirect(part))
             nc.vector.tensor_copy(v_sc0[:, cols], tab_sc[:].indirect(part))
-            nc.scalar.dma_start(out=v_sc1[0:112, cols].bitcast(I32), in_=v_sc0[4:116, cols].bitcast(I32))
+            nc.scalar.dma_start(
+                out=v_sc1[0:SHIFTED_ROWS, cols].bitcast(I32),
+                in_=v_sc0[PACK : PACK + SHIFTED_ROWS, cols].bitcast(I32),
+            )
             nc.vector.tensor_copy(v_w[1][:, cols], tab_w[1][:].bitcast(U32).indirect(part))
-        w1_rest = big.tile([P, PASSES, 2 * (H - P)], U8, name="w1_rest", tag="big", align_bytes=64)
+        w1_rest = loads.tile([P, PASSES, 2 * (H - P)], U8, name="w1_rest", tag="load", align_bytes=64)
         nc.sync.dma_start(out=w1_rest[:].bitcast(I32), in_=w1_view[:, :, 2 * P :].bitcast(I32))
 
-        h_sb = [keep.tile([P, S], F32, name=f"h{c}", tag=f"h{c}") for c in range(TILES)]
-        for c in range(TILES):
-            for s in range(2):
-                cols = slice(s * HALF, (s + 1) * HALF)
-                acc = acc_pool.tile([P, HALF], F32, name="acc", tag="acc")
+        h_sb = [keep.tile([P, S], F32, name=f"h{c}", tag=f"h{c}", align_bytes=64) for c in range(ROW_TILES)]
+        for c in range(ROW_TILES):
+            for lo in range(0, S, BANK):
+                cols = slice(lo, lo + BANK)
+                h_sum = sums.tile([P, BANK], F32, name="h_sum", tag="sum")
                 for a in range(PASSES):
                     if c == 0:
-                        codes = w1_first[:, a, :]
+                        w1_codes = w1_first[:, a, :]
                     else:
-                        codes = w1_rest[:, a, 2 * P * (c - 1) : 2 * P * c]
+                        w1_codes = w1_rest[:, a, 2 * P * (c - 1) : 2 * P * c]
                     nc.tensor.matmul_mx(
-                        out=acc[:],
-                        lhsT=codes.bitcast(FP4X4),
+                        out=h_sum[:],
+                        lhsT=w1_codes.bitcast(FP4X4),
                         lhsT_scale=w1_sc[:, a, c * P : (c + 1) * P],
                         rhs=v_w[a][:, cols].bitcast(FP8X4),
                         rhs_scale=v_sc[a][:, cols],
                         start=(a == 0),
                         stop=(a == PASSES - 1),
                     )
-                nc.scalar.copy(out=h_sb[c][:, cols], in_=acc[:])
+                nc.scalar.copy(out=h_sb[c][:, cols], in_=h_sum[:])
 
         load_page(1)
-        bias_rows = big.tile([P, P], F32, name="bias_rows", tag="big", align_bytes=64)
+        bias_rows = loads.tile([P, P], F32, name="bias_rows", tag="load", align_bytes=64)
         nc.gpsimd.memset(bias_rows[:], 0.0)
-        nc.sync.dma_start(out=bias_rows[0:TILES, :], in_=bias.rearrange("(c p) -> c p", p=P))
-        bias_turned = turn_pool.tile([P, P], F32, name="bias_turned", tag="back")
+        nc.sync.dma_start(out=bias_rows[0:ROW_TILES, :], in_=bias.rearrange("(c p) -> c p", p=P))
+        bias_turned = turns.tile([P, P], F32, name="bias_turned", tag="back")
         nc.tensor.transpose(bias_turned[:], bias_rows[:], ident_f32[:])
-        neg_bias = keep.tile([P, TILES], F32, name="neg_bias")
-        nc.scalar.activation(out=neg_bias[:], in_=bias_turned[:, 0:TILES], func=IDENT, scale=-1.0)
+        neg_bias = keep.tile([P, ROW_TILES], F32, name="neg_bias")
+        nc.scalar.activation(out=neg_bias[:], in_=bias_turned[:, 0:ROW_TILES], func=IDENTITY, scale=-1.0)
 
-        floor = [keep.tile([P, M], F32, name=f"floor{c}") for c in range(TILES)]
+        floor = [keep.tile([P, M], F32, name=f"floor{c}") for c in range(ROW_TILES)]
 
         def load_floor(c):
-            raw = big.tile([P, M], F32, name="low_raw", tag="big", align_bytes=64)
-            nc.sync.dma_start(out=raw[:], in_=low[c * P : (c + 1) * P, :])
-            nc.scalar.activation(out=floor[c][:], in_=raw[:], func=IDENT, bias=neg_bias[:, c : c + 1])
+            low_rows = loads.tile([P, M], F32, name="low_rows", tag="load", align_bytes=64)
+            nc.sync.dma_start(out=low_rows[:], in_=low[c * P : (c + 1) * P, :])
+            nc.scalar.activation(out=floor[c][:], in_=low_rows[:], func=IDENTITY, bias=neg_bias[:, c : c + 1])
 
-        w2_codes = keep.tile([P, PASSES, N], U32, name="w2_codes", align_bytes=64)
+        w2_codes = {}
         w2_sc = keep.tile([P, PASSES, N], U8, name="w2_sc", align_bytes=64)
-        w2_bf = keep.tile([P, PASSES, N, 4], BF16, name="w2_bf", align_bytes=64)
+        w2_bf = keep.tile([P, PASSES, N, PACK], BF16, name="w2_bf", align_bytes=64)
 
         def load_w2(g):
-            raw = big.tile([P, 4, N], F32, name="w2_raw", tag="big", align_bytes=64)
-            nc.sync.dma_start(out=raw[:], in_=w2[g * 512 : (g + 1) * 512, :].rearrange("(p j) n -> p j n", j=4))
-            nc.scalar.copy(out=w2_bf[:, g, :, :], in_=raw[:].rearrange("p j n -> p n j"))
+            w2_rows = loads.tile([P, PACK, N], F32, name="w2_rows", tag="load", align_bytes=64)
+            rows = w2[g * P * PACK : (g + 1) * P * PACK, :]
+            nc.sync.dma_start(out=w2_rows[:], in_=rows.rearrange("(p t) n -> p t n", t=PACK))
+            nc.scalar.copy(out=w2_bf[:, g, :, :], in_=w2_rows[:].rearrange("p t n -> p n t"))
+
+        def quantise_w2(g, tag):
+            w2_codes[g] = keep.tile([P, N], U32, name="w2_codes", tag=tag, align_bytes=64)
+            nc.vector.quantize_mx(
+                out=w2_codes[g][:].bitcast(FP8X4),
+                scales=w2_sc[:, g, :],
+                in_=w2_bf[:, g, :, :].rearrange("p n t -> p (n t)"),
+            )
 
         def scatter(c, lo, hi):
             nc.vector.tensor_tensor(
-                pages[c][:].indirect(idx2[:, lo // 16 : hi // 16]), h_sb[c][:, lo:hi], wgs_sb[:, lo:hi], ALU.mult
+                pages[c][:].indirect(entries(idx2, lo, hi)), h_sb[c][:, lo:hi], wgs_sb[:, lo:hi], ALU.mult
             )
-
-        z_t = [keep.tile([P, M // P, 2, P], F32, name=f"z_t{g}") for g in range(PASSES)]
-        z_codes = [keep.tile([P, M], U32, name=f"z_codes{g}", align_bytes=64) for g in range(PASSES)]
-        z_sc = [keep.tile([P, M], U8, name=f"z_sc{g}", align_bytes=64) for g in range(PASSES)]
 
         def gather(c, x, lo, hi):
-            nc.vector.tensor_copy(x, pages[c][:].indirect(idx3[:, lo // 16 : hi // 16]))
+            nc.vector.tensor_copy(x, pages[c][:].indirect(entries(idx3, lo, hi)))
 
-        def apply_floor(c, x, lo, hi):
-            z = ring.tile([P, hi - lo], BF16, name="z", tag="z", bufs=5)
-            nc.vector.scalar_tensor_tensor(
-                z[:], x, neg_bias[:, c : c + 1], floor[c][:, lo:hi], ALU.add, ALU.max
-            )
-            return z
+        z_t = [keep.tile([P, M // P, 2, P], F32, name=f"z_t{g}") for g in range(PASSES)]
+        z_codes = {}
+        z_sc = [keep.tile([P, M], U8, name=f"z_sc{g}", align_bytes=64) for g in range(PASSES)]
 
-        def turn(c, zs, lo, hi):
-            g, first = divmod(c, 4)
+        def floor_and_turn(c, x, lo, hi):
+            z = ring.tile([P, hi - lo], BF16, name="z", tag="z", bufs=len(LAST_SPANS))
+            nc.vector.scalar_tensor_tensor(z[:], x, neg_bias[:, c : c + 1], floor[c][:, lo:hi], ALU.add, ALU.max)
+            g, within = divmod(c, TILES_A_PASS)
             blocks = (hi - lo) // P
-            turned = turn_pool.tile([P, blocks, len(zs) * P], BF16, name="turned", tag="turned")
-            for i, z in enumerate(zs):
-                for b in range(blocks):
-                    nc.tensor.transpose(turned[:, b, i * P : (i + 1) * P], z[:, b * P : (b + 1) * P], ident_bf[:])
+            turned = turns.tile([P, blocks, P], BF16, name="turned", tag="turned")
+            for b in range(blocks):
+                nc.tensor.transpose(turned[:, b, :], z[:, b * P : (b + 1) * P], ident_bf[:])
+            share = P // PACK
             nc.scalar.copy(
-                out=z_t[g][:, lo // P : hi // P, :, 32 * first : 32 * (first + len(zs))],
+                out=z_t[g][:, lo // P : hi // P, :, share * within : share * (within + 1)],
                 in_=turned[:].bitcast(F32).rearrange("m b (l u) -> m b u l", u=2),
             )
 
-        def turn_back(g, lo, blocks, words):
-            back = turn_pool.tile([P, blocks, 2, P], F32, name="back", tag="back")
-            for b in range(blocks):
-                for u in range(2):
-                    nc.tensor.transpose(back[:, b, u, :], z_t[g][:, lo // P + b, u, :], ident_f32[:])
-            nc.scalar.copy(
-                out=words.rearrange("p (b m u) -> p b m u", b=blocks, u=2),
-                in_=back[:].rearrange("p b u m -> p b m u"),
-            )
-
-        def quantise_z(g, lo, hi, woven):
+        def weave(g, lo, hi):
+            woven = keep.tile([P, (hi - lo) * PACK], BF16, name="woven", tag=f"woven{g}_{lo}", align_bytes=64)
             step = min(PIECE, hi - lo)
+            blocks = step // P
             for at in range(0, hi - lo, step):
-                turn_back(g, lo + at, step // P, woven[:, at * 4 : (at + step) * 4].bitcast(F32))
-            nc.vector.quantize_mx(out=z_codes[g][:, lo:hi].bitcast(FP8X4), scales=z_sc[g][:, lo:hi], in_=woven[:])
+                back = turns.tile([P, blocks, 2, P], F32, name="back", tag="back")
+                for b in range(blocks):
+                    for u in range(2):
+                        nc.tensor.transpose(back[:, b, u, :], z_t[g][:, (lo + at) // P + b, u, :], ident_f32[:])
+                pairs = woven[:, at * PACK : (at + step) * PACK].bitcast(F32)
+                nc.scalar.copy(
+                    out=pairs.rearrange("p (b m u) -> p b m u", b=blocks, u=2),
+                    in_=back[:].rearrange("p b u m -> p b m u"),
+                )
+            return woven
+
+        def quantise_z(g, lo, hi, woven, tag):
+            z_codes[(g, lo)] = keep.tile([P, hi - lo], U32, name="z_codes", tag=tag, align_bytes=64)
+            nc.vector.quantize_mx(out=z_codes[(g, lo)][:].bitcast(FP8X4), scales=z_sc[g][:, lo:hi], in_=woven[:])
 
         out_view = out.rearrange("(j p) m -> p j m", p=P)
 
-        def product(lo, hi, shared):
-            for pair in range(2):
-                acc = acc_pool.tile([P, 2, hi - lo], F32, name="acc_out", tag="acc")
+        def product(lo, hi):
+            half_start = lo // BANK * BANK
+            moving = [z_codes[(0, half_start)][:, lo - half_start : hi - half_start], z_codes[(1, lo)][:]]
+            for pair in range(N // (2 * P)):
+                out_sum = sums.tile([P, 2, hi - lo], F32, name="out_sum", tag="sum")
                 for g in range(PASSES):
                     for j in range(2):
                         n_cols = slice((2 * pair + j) * P, (2 * pair + j + 1) * P)
                         nc.tensor.matmul_mx(
-                            out=acc[:, j, :],
-                            lhsT=w2_codes[:, g, n_cols].bitcast(FP8X4),
+                            out=out_sum[:, j, :],
+                            lhsT=w2_codes[g][:, n_cols].bitcast(FP8X4),
                             lhsT_scale=w2_sc[:, g, n_cols],
-                            rhs=z_codes[g][:, lo:hi].bitcast(FP8X4),
+                            rhs=moving[g].bitcast(FP8X4),
                             rhs_scale=z_sc[g][:, lo:hi],
                             start=(g == 0 and j == 0),
                             stop=(g == PASSES - 1 and j == 1),
                         )
-                res = stage.tile([P, 2, hi - lo], F32, name="res", tag="res")
-                if shared and pair == 1:
-                    nc.vector.tensor_copy(out=res[:], in_=acc[:])
+                result = stage.tile([P, 2, hi - lo], F32, name="result", tag="result")
+                if pair == 0:
+                    nc.scalar.copy(out=result[:], in_=out_sum[:])
                 else:
-                    nc.scalar.copy(out=res[:], in_=acc[:])
-                nc.sync.dma_start(out=out_view[:, 2 * pair : 2 * pair + 2, lo:hi], in_=res[:])
+                    nc.vector.tensor_copy(out=result[:], in_=out_sum[:])
+                nc.sync.dma_start(out=out_view[:, 2 * pair : 2 * pair + 2, lo:hi], in_=result[:])
 
-        scatter(0, 0, HALF)
-        scatter(0, HALF, S)
-        x = xs.tile([P, M], F32, name="x", tag="x")
+        scatter(0, 0, BANK)
+        scatter(0, BANK, S)
+        x = picked.tile([P, M], F32, name="x", tag="x")
         gather(0, x[:], 0, M)
-        for c in range(1, TILES - 1):
+        first_w2_step = 2
+        for c in range(1, LAST):
             if c > 1:
                 load_page(c)
             load_floor(c - 1)
-            if c in (2, 3):
-                load_w2(c - 2)
+            if first_w2_step <= c < first_w2_step + PASSES:
+                load_w2(c - first_w2_step)
             scatter(c, 0, S)
-            turn(c - 1, [apply_floor(c - 1, x[:], 0, M)], 0, M)
-            x = xs.tile([P, M], F32, name="x", tag="x")
+            floor_and_turn(c - 1, x[:], 0, M)
+            x = picked.tile([P, M], F32, name="x", tag="x")
             gather(c, x[:], 0, M)
-            if c == 4:
-                nc.vector.quantize_mx(
-                    out=w2_codes[:].rearrange("p g n -> p (g n)").bitcast(FP8X4),
-                    scales=w2_sc[:].rearrange("p g n -> p (g n)"),
-                    in_=w2_bf[:].rearrange("p g n j -> p (g n j)"),
-                )
-            if c == 5:
-                for lo in (0, HALF):
-                    woven = ring.tile([P, HALF * 4], BF16, name="woven", tag="woven", align_bytes=64)
-                    quantise_z(0, lo, lo + HALF, woven)
-        last = TILES - 1
-        load_floor(last - 1)
-        load_floor(last)
-        load_page(last)
-        turn(last - 1, [apply_floor(last - 1, x[:], 0, M)], 0, M)
-        scatter(last, 0, S)
+            if c == TILES_A_PASS:
+                quantise_w2(0, "w2_codes0")
+            if c == TILES_A_PASS + 1:
+                quantise_z(0, 0, BANK, weave(0, 0, BANK), "z_codes0")
+                woven_upper = weave(0, BANK, M)
+        load_floor(LAST - 1)
+        load_floor(LAST)
+        load_page(LAST)
+        floor_and_turn(LAST - 1, x[:], 0, M)
+        scatter(LAST, 0, S)
+
         x_last = {}
 
-        def gather_last(q):
-            x_last[q] = ring.tile([P, PIECE], F32, name="x_last", tag="x_last")
-            gather(last, x_last[q][:], q * PIECE, (q + 1) * PIECE)
-
-        def finish(q, lo, hi):
-            z = apply_floor(last, x_last[q][:, lo - q * PIECE : hi - q * PIECE], lo, hi)
-            turn(last, [z], lo, hi)
-            woven = stage.tile([P, (hi - lo) * 4], BF16, name="woven_last", tag="woven_last", bufs=5, align_bytes=64)
-            quantise_z(1, lo, hi, woven)
-            product(lo, hi, True)
+        def gather_last(piece):
+            x_last[piece] = ring.tile([P, PIECE], F32, name="x_last", tag="x_last")
+            gather(LAST, x_last[piece][:], piece * PIECE, (piece + 1) * PIECE)
 
         gather_last(0)
-        for q in range(3):
-            gather_last(q + 1)
-            finish(q, q * PIECE, (q + 1) * PIECE)
-        finish(3, 3 * PIECE, 3 * PIECE + P)
-        finish(3, 3 * PIECE + P, M)
+        for lo, hi in LAST_SPANS:
+            piece = lo // PIECE
+            if piece + 1 < M // PIECE:
+                gather_last(piece + 1)
+            floor_and_turn(LAST, x_last[piece][:, lo - piece * PIECE : hi - piece * PIECE], lo, hi)
+        quantise_w2(1, "wgs")
+        for lo, hi in LAST_SPANS:
+            if lo == PIECE:
+                quantise_z(0, BANK, M, woven_upper, f"h{LAST}")
+            quantise_z(1, lo, hi, weave(1, lo, hi), f"z_codes1_{lo}")
+            product(lo, hi)

@@ -28,8 +28,11 @@ ROW_TILES = H // P
 TILES_A_PASS = ROW_TILES // PASSES
 LAST = ROW_TILES - 1
 PIECE = 256
-SHIFTED_ROWS = 112
-LAST_SPANS = [(0, PIECE), (PIECE, 2 * PIECE), (2 * PIECE, 3 * PIECE), (3 * PIECE, M - P), (M - P, M)]
+SCALE_ROW = 24
+LIVE_ROWS = 100
+SLOTS = 3
+STEADY = 4
+SPANS = [(0, PIECE), (PIECE, 2 * PIECE), (2 * PIECE, 3 * PIECE), (3 * PIECE, M - P), (M - P, M)]
 
 
 def tile_list_fetal_slice_mosaic_kernel(
@@ -37,88 +40,89 @@ def tile_list_fetal_slice_mosaic_kernel(
 ):
     nc = tc.nc
     with ExitStack() as ctx:
+        lists = ctx.enter_context(tc.tile_pool(name="lists", bufs=1))
         keep = ctx.enter_context(tc.tile_pool(name="keep", bufs=1))
-        loads = ctx.enter_context(tc.tile_pool(name="loads", bufs=4))
-        picked = ctx.enter_context(tc.tile_pool(name="picked", bufs=1))
-        ring = ctx.enter_context(tc.tile_pool(name="ring", bufs=2))
-        stage = ctx.enter_context(tc.tile_pool(name="stage", bufs=2 * len(LAST_SPANS)))
-        sums = ctx.enter_context(tc.psum_pool(name="sums", bufs=4))
+        banks = ctx.enter_context(tc.psum_pool(name="banks", bufs=1))
         turns = ctx.enter_context(tc.psum_pool(name="turns", bufs=2))
 
-        idx = keep.tile([P, S // PER_COLUMN], U16, name="idx")
-        idx2 = keep.tile([P, S // PER_COLUMN], U16, name="idx2")
-        idx3 = keep.tile([P, M // PER_COLUMN], U16, name="idx3")
+        def sbuf(shape, dtype, name, tag=None):
+            return keep.tile(shape, dtype, name=name, tag=tag or name, align_bytes=64)
+
+        idx = lists.tile([P, S // PER_COLUMN], U16, name="idx")
+        idx2 = lists.tile([P, S // PER_COLUMN], U16, name="idx2")
+        idx3 = lists.tile([P, M // PER_COLUMN], U16, name="idx3")
 
         def entries(listed, lo, hi):
             return listed[:, lo // PER_COLUMN : hi // PER_COLUMN]
 
         nc.sync.dma_start(idx[:], offs)
-        nc.sync.dma_start(idx2[:], offs2)
-        nc.sync.dma_start(idx3[:], offs3)
-        w1_view = w1_words.rearrange("a p c -> p a c")
-        w1_first = keep.tile([P, PASSES, 2 * P], U8, name="w1_first", align_bytes=64)
-        nc.sync.dma_start(out=w1_first[:].bitcast(I32), in_=w1_view[:, :, 0 : 2 * P].bitcast(I32))
-        tab_sc = loads.tile([P, T], U8, name="tab_sc", tag="load", align_bytes=64)
-        nc.vector.memset(tab_sc[:].bitcast(I32), 0)
-        tab_w = []
-
-        def load_tab_words(a):
-            words = loads.tile([P, T], I32, name=f"tab_w{a}", tag="load", align_bytes=64)
-            nc.sync.dma_start(out=words[:], in_=tab_words[a].rearrange("p t i -> p (t i)").bitcast(I32))
-            tab_w.append(words)
-
-        load_tab_words(0)
+        tab_sc = sbuf([P, T], U8, "tab_sc", "page_slot0")
         for quad in range(QUADRANTS):
-            nc.scalar.dma_start(
-                out=tab_sc[QUADRANT * quad : QUADRANT * quad + PASSES * PACK, :].bitcast(I32),
+            nc.sync.dma_start(
+                out=tab_sc[QUADRANT * quad + SCALE_ROW : QUADRANT * (quad + 1), :].bitcast(I32),
                 in_=tab_scales[:, PACK * quad : PACK * (quad + 1), :].bitcast(I32),
             )
-        load_tab_words(1)
-        w1_sc = keep.tile([P, PASSES, H], U8, name="w1_sc", align_bytes=64)
+            nc.vector.memset(tab_sc[QUADRANT * quad : QUADRANT * quad + SCALE_ROW, :].bitcast(I32), 0)
+        tab_w = [sbuf([P, T], I32, "tab_w0", "wgs_slot"), sbuf([P, T], I32, "tab_w1", "page_slot1")]
+        for a in range(PASSES):
+            nc.sync.dma_start(out=tab_w[a][:], in_=tab_words[a].rearrange("p t i -> p (t i)").bitcast(I32))
+        w1_view = w1_words.rearrange("a p c -> p a c")
+        w1_first = sbuf([P, PASSES, 2 * P], U8, "w1_first", "row_slot0")
+        nc.sync.dma_start(out=w1_first[:].bitcast(I32), in_=w1_view[:, :, 0 : 2 * P].bitcast(I32))
+        nc.sync.dma_start(idx2[:], offs2)
+        wgs_first = sbuf([P, BANK], F32, "wgs_first", "page_slot2")
+        nc.sync.dma_start(out=wgs_first[:], in_=wgs[:, 0:BANK])
+        nc.sync.dma_start(idx3[:], offs3)
+        pages = {}
+
+        def load_page(c):
+            pages[c] = sbuf([P, T2], F32, f"page{c}", f"page_slot{c % SLOTS}" if c < LAST else "row_slot2")
+            nc.sync.dma_start(out=pages[c][:], in_=page0[c * P : (c + 1) * P, :])
+
+        w1_sc = sbuf([P, PASSES, H], U8, "w1_sc")
         nc.gpsimd.memset(w1_sc[:].bitcast(I32), 0)
         for quad in range(QUADRANTS):
             nc.gpsimd.dma_start(
                 out=w1_sc[QUADRANT * quad : QUADRANT * quad + PACK, :, :].bitcast(I32),
                 in_=w1_scales[:, PACK * quad : PACK * (quad + 1), :].rearrange("a r c -> r a c").bitcast(I32),
             )
-        ident_f32 = keep.tile([P, P], F32, name="ident_f32")
+        ident_f32 = sbuf([P, P], F32, "ident_f32")
         make_identity(nc, ident_f32[:])
-        ident_bf = keep.tile([P, P], BF16, name="ident_bf")
+        ident_bf = sbuf([P, P], BF16, "ident_bf")
         nc.scalar.activation(out=ident_bf[:], in_=ident_f32[:], func=IDENTITY)
-        wgs_sb = keep.tile([P, S], F32, name="wgs_sb", tag="wgs", align_bytes=64)
-        nc.sync.dma_start(out=wgs_sb[:], in_=wgs)
-        pages = []
+        bias_rows = sbuf([P, P], F32, "bias_rows")
+        nc.gpsimd.memset(bias_rows[:], 0.0)
+        nc.gpsimd.dma_start(out=bias_rows[0:ROW_TILES, :], in_=bias.rearrange("(c p) -> c p", p=P))
 
-        def load_page(c):
-            page = loads.tile([P, T2], F32, name=f"page{c}", tag="load", align_bytes=64)
-            nc.sync.dma_start(out=page[:], in_=page0[c * P : (c + 1) * P, :])
-            pages.append(page)
-
-        load_page(0)
-
-        v_sc0 = keep.tile([P, S], U8, name="v_sc0", align_bytes=64)
-        v_sc1 = keep.tile([P, S], U8, name="v_sc1", align_bytes=64)
-        nc.vector.memset(v_sc1[:].bitcast(I32), 0)
-        v_sc = [v_sc0, v_sc1]
-        v_w = [keep.tile([P, S], U32, name=f"v_w{a}", align_bytes=64) for a in range(PASSES)]
-        for lo in range(0, S, BANK):
-            cols = slice(lo, lo + BANK)
-            part = entries(idx, lo, lo + BANK)
-            nc.vector.tensor_copy(v_w[0][:, cols], tab_w[0][:].bitcast(U32).indirect(part))
-            nc.vector.tensor_copy(v_sc0[:, cols], tab_sc[:].indirect(part))
-            nc.scalar.dma_start(
-                out=v_sc1[0:SHIFTED_ROWS, cols].bitcast(I32),
-                in_=v_sc0[PACK : PACK + SHIFTED_ROWS, cols].bitcast(I32),
+        v_sc = [sbuf([P, S], U8, f"v_sc{a}") for a in range(PASSES)]
+        for a in range(PASSES):
+            nc.vector.memset(v_sc[a][P - QUADRANT : P, :].bitcast(I32), 0)
+        picked_sc = sbuf([P, S], U8, "picked_sc", "weights_slot")
+        nc.vector.tensor_copy(picked_sc[:], tab_sc[:].indirect(idx[:]))
+        for a in range(PASSES):
+            first = SCALE_ROW + PACK * a
+            nc.sync.dma_start(
+                out=v_sc[a][0:LIVE_ROWS, :].bitcast(I32), in_=picked_sc[first : first + LIVE_ROWS, :].bitcast(I32)
             )
-            nc.vector.tensor_copy(v_w[1][:, cols], tab_w[1][:].bitcast(U32).indirect(part))
-        w1_rest = loads.tile([P, PASSES, 2 * (H - P)], U8, name="w1_rest", tag="load", align_bytes=64)
+        load_page(0)
+        v_w = [sbuf([P, S], U32, "v_w0", "row_slot2"), sbuf([P, S], U32, "v_w1")]
+        nc.vector.tensor_copy(v_w[0][:], tab_w[0][:].bitcast(U32).indirect(idx[:]))
+        wgs_sb = sbuf([P, S], F32, "wgs_sb", "wgs_slot")
+        nc.sync.dma_start(out=wgs_sb[:], in_=wgs)
+        for lo in range(0, S, BANK):
+            part = entries(idx, lo, lo + BANK)
+            nc.vector.tensor_copy(v_w[1][:, lo : lo + BANK], tab_w[1][:].bitcast(U32).indirect(part))
+        w1_rest = sbuf([P, PASSES, 2 * (H - P)], U8, "w1_rest", "weights_slot")
         nc.sync.dma_start(out=w1_rest[:].bitcast(I32), in_=w1_view[:, :, 2 * P :].bitcast(I32))
+        load_page(1)
 
-        h_sb = [keep.tile([P, S], F32, name=f"h{c}", tag=f"h{c}", align_bytes=64) for c in range(ROW_TILES)]
-        for c in range(ROW_TILES):
-            for lo in range(0, S, BANK):
-                cols = slice(lo, lo + BANK)
-                h_sum = sums.tile([P, BANK], F32, name="h_sum", tag="sum")
+        h_sb = {}
+
+        def first_product(c):
+            h_sb[c] = sbuf([P, S], F32, f"h{c}", "row_slot1" if c == 0 else None)
+            for half in range(S // BANK):
+                cols = slice(half * BANK, (half + 1) * BANK)
+                h_sum = banks.tile([P, BANK], F32, name="h_sum", tag=f"bank{(2 * c + half) % 4}")
                 for a in range(PASSES):
                     if c == 0:
                         w1_codes = w1_first[:, a, :]
@@ -135,153 +139,164 @@ def tile_list_fetal_slice_mosaic_kernel(
                     )
                 nc.scalar.copy(out=h_sb[c][:, cols], in_=h_sum[:])
 
-        load_page(1)
-        bias_rows = loads.tile([P, P], F32, name="bias_rows", tag="load", align_bytes=64)
-        nc.gpsimd.memset(bias_rows[:], 0.0)
-        nc.sync.dma_start(out=bias_rows[0:ROW_TILES, :], in_=bias.rearrange("(c p) -> c p", p=P))
-        bias_turned = turns.tile([P, P], F32, name="bias_turned", tag="back")
+        first_product(0)
+        first_product(1)
+        bias_turned = banks.tile([P, P], F32, name="bias_turned", tag="bank0")
         nc.tensor.transpose(bias_turned[:], bias_rows[:], ident_f32[:])
-        neg_bias = keep.tile([P, ROW_TILES], F32, name="neg_bias")
+        neg_bias = sbuf([P, ROW_TILES], F32, "neg_bias")
         nc.scalar.activation(out=neg_bias[:], in_=bias_turned[:, 0:ROW_TILES], func=IDENTITY, scale=-1.0)
+        for c in range(2, ROW_TILES):
+            first_product(c)
 
-        floor = [keep.tile([P, M], F32, name=f"floor{c}") for c in range(ROW_TILES)]
+        floor = {}
 
-        def load_floor(c):
-            low_rows = loads.tile([P, M], F32, name="low_rows", tag="load", align_bytes=64)
-            nc.sync.dma_start(out=low_rows[:], in_=low[c * P : (c + 1) * P, :])
-            nc.scalar.activation(out=floor[c][:], in_=low_rows[:], func=IDENTITY, bias=neg_bias[:, c : c + 1])
+        def load_floors(c, count):
+            rows = sbuf([P, count, M], F32, f"low{c}", f"row_slot{c % SLOTS}" if count == 1 else f"floor{c - 1}")
+            nc.sync.dma_start(out=rows[:], in_=low[c * P : (c + count) * P, :].rearrange("(i p) m -> p i m", p=P))
+            for i in range(count):
+                floor[c + i] = sbuf([P, M], F32, f"floor{c + i}")
+                nc.scalar.activation(
+                    out=floor[c + i][:], in_=rows[:, i, :], func=IDENTITY, bias=neg_bias[:, c + i : c + i + 1]
+                )
 
-        w2_codes = {}
-        w2_sc = keep.tile([P, PASSES, N], U8, name="w2_sc", align_bytes=64)
-        w2_bf = keep.tile([P, PASSES, N, PACK], BF16, name="w2_bf", align_bytes=64)
+        w2_codes = sbuf([P, PASSES, N], U32, "w2_codes")
+        w2_sc = sbuf([P, PASSES, N], U8, "w2_sc")
 
-        def load_w2(g):
-            w2_rows = loads.tile([P, PACK, N], F32, name="w2_rows", tag="load", align_bytes=64)
+        def prepare_w2(g):
+            w2_rows = sbuf([P, PACK, N], F32, f"w2_rows{g}", "weights_slot")
             rows = w2[g * P * PACK : (g + 1) * P * PACK, :]
             nc.sync.dma_start(out=w2_rows[:], in_=rows.rearrange("(p t) n -> p t n", t=PACK))
-            nc.scalar.copy(out=w2_bf[:, g, :, :], in_=w2_rows[:].rearrange("p t n -> p n t"))
-
-        def quantise_w2(g, tag):
-            w2_codes[g] = keep.tile([P, N], U32, name="w2_codes", tag=tag, align_bytes=64)
+            w2_bf = sbuf([P, N, PACK], BF16, f"w2_bf{g}")
+            nc.scalar.copy(out=w2_bf[:], in_=w2_rows[:].rearrange("p t n -> p n t"))
             nc.vector.quantize_mx(
-                out=w2_codes[g][:].bitcast(FP8X4),
+                out=w2_codes[:, g, :].bitcast(FP8X4),
                 scales=w2_sc[:, g, :],
-                in_=w2_bf[:, g, :, :].rearrange("p n t -> p (n t)"),
+                in_=w2_bf[:].rearrange("p n t -> p (n t)"),
             )
 
-        def scatter(c, lo, hi):
+        def scatter(c, lo, hi, weights):
             nc.vector.tensor_tensor(
-                pages[c][:].indirect(entries(idx2, lo, hi)), h_sb[c][:, lo:hi], wgs_sb[:, lo:hi], ALU.mult
+                pages[c][:].indirect(entries(idx2, lo, hi)), h_sb[c][:, lo:hi], weights[:, lo:hi], ALU.mult
             )
 
         def gather(c, x, lo, hi):
             nc.vector.tensor_copy(x, pages[c][:].indirect(entries(idx3, lo, hi)))
 
-        z_t = [keep.tile([P, M // P, 2, P], F32, name=f"z_t{g}") for g in range(PASSES)]
-        z_codes = {}
-        z_sc = [keep.tile([P, M], U8, name=f"z_sc{g}", align_bytes=64) for g in range(PASSES)]
+        def floored(z, x, c, lo, hi):
+            nc.vector.scalar_tensor_tensor(z, x, neg_bias[:, c : c + 1], floor[c][:, lo:hi], ALU.add, ALU.max)
 
-        def floor_and_turn(c, x, lo, hi):
-            z = ring.tile([P, hi - lo], BF16, name="z", tag="z", bufs=len(LAST_SPANS))
-            nc.vector.scalar_tensor_tensor(z[:], x, neg_bias[:, c : c + 1], floor[c][:, lo:hi], ALU.add, ALU.max)
+        spans = {0: [(0, BANK), (BANK, M)], 1: SPANS}
+        z_t = {}
+        for g in range(PASSES):
+            for lo, hi in spans[g]:
+                z_t[(g, lo)] = sbuf([P, (hi - lo) // P, 2, P], F32, f"z_t{g}_{lo}")
+        share = P // PACK
+
+        def turn(c, count, z, lo, hi):
             g, within = divmod(c, TILES_A_PASS)
             blocks = (hi - lo) // P
-            turned = turns.tile([P, blocks, P], BF16, name="turned", tag="turned")
-            for b in range(blocks):
-                nc.tensor.transpose(turned[:, b, :], z[:, b * P : (b + 1) * P], ident_bf[:])
-            share = P // PACK
-            nc.scalar.copy(
-                out=z_t[g][:, lo // P : hi // P, :, share * within : share * (within + 1)],
-                in_=turned[:].bitcast(F32).rearrange("m b (l u) -> m b u l", u=2),
-            )
+            turned = turns.tile([P, count, blocks, P], BF16, name="turned", tag="turned")
+            for i in range(count):
+                for b in range(blocks):
+                    nc.tensor.transpose(turned[:, i, b, :], z[:, i, b * P : (b + 1) * P], ident_bf[:])
+            for at, end in spans[g]:
+                if lo <= at and end <= hi:
+                    words = turned[:, :, (at - lo) // P : (end - lo) // P, :].bitcast(F32)
+                    nc.scalar.copy(
+                        out=z_t[(g, at)][:, :, :, share * within : share * (within + count)].rearrange(
+                            "m b u (i l) -> m i b u l", i=count
+                        ),
+                        in_=words.rearrange("m i b (l u) -> m i b u l", u=2),
+                    )
 
-        def weave(g, lo, hi):
-            woven = keep.tile([P, (hi - lo) * PACK], BF16, name="woven", tag=f"woven{g}_{lo}", align_bytes=64)
+        z_codes = {}
+        z_sc = [sbuf([P, M], U8, f"z_sc{g}") for g in range(PASSES)]
+
+        def weave_and_quantise(g, lo, hi):
+            woven = sbuf([P, (hi - lo) * PACK], BF16, f"woven{g}_{lo}")
             step = min(PIECE, hi - lo)
             blocks = step // P
             for at in range(0, hi - lo, step):
                 back = turns.tile([P, blocks, 2, P], F32, name="back", tag="back")
                 for b in range(blocks):
                     for u in range(2):
-                        nc.tensor.transpose(back[:, b, u, :], z_t[g][:, (lo + at) // P + b, u, :], ident_f32[:])
+                        nc.tensor.transpose(back[:, b, u, :], z_t[(g, lo)][:, at // P + b, u, :], ident_f32[:])
                 pairs = woven[:, at * PACK : (at + step) * PACK].bitcast(F32)
                 nc.scalar.copy(
                     out=pairs.rearrange("p (b m u) -> p b m u", b=blocks, u=2),
                     in_=back[:].rearrange("p b u m -> p b m u"),
                 )
-            return woven
-
-        def quantise_z(g, lo, hi, woven, tag):
-            z_codes[(g, lo)] = keep.tile([P, hi - lo], U32, name="z_codes", tag=tag, align_bytes=64)
+            z_codes[(g, lo)] = sbuf([P, hi - lo], U32, f"z_codes{g}_{lo}")
             nc.vector.quantize_mx(out=z_codes[(g, lo)][:].bitcast(FP8X4), scales=z_sc[g][:, lo:hi], in_=woven[:])
 
         out_view = out.rearrange("(j p) m -> p j m", p=P)
 
-        def product(lo, hi):
+        def product(span, on_vector):
+            lo, hi = SPANS[span]
             half_start = lo // BANK * BANK
             moving = [z_codes[(0, half_start)][:, lo - half_start : hi - half_start], z_codes[(1, lo)][:]]
             for pair in range(N // (2 * P)):
-                out_sum = sums.tile([P, 2, hi - lo], F32, name="out_sum", tag="sum")
+                out_sum = banks.tile([P, 2, hi - lo], F32, name="out_sum", tag=f"bank{(2 * span + pair) % 4}")
                 for g in range(PASSES):
                     for j in range(2):
                         n_cols = slice((2 * pair + j) * P, (2 * pair + j + 1) * P)
                         nc.tensor.matmul_mx(
                             out=out_sum[:, j, :],
-                            lhsT=w2_codes[g][:, n_cols].bitcast(FP8X4),
+                            lhsT=w2_codes[:, g, n_cols].bitcast(FP8X4),
                             lhsT_scale=w2_sc[:, g, n_cols],
                             rhs=moving[g].bitcast(FP8X4),
                             rhs_scale=z_sc[g][:, lo:hi],
                             start=(g == 0 and j == 0),
                             stop=(g == PASSES - 1 and j == 1),
                         )
-                result = stage.tile([P, 2, hi - lo], F32, name="result", tag="result")
-                if pair == 0:
-                    nc.scalar.copy(out=result[:], in_=out_sum[:])
-                else:
+                result = sbuf([P, 2, hi - lo], F32, f"result{span}_{pair}")
+                if pair in on_vector:
                     nc.vector.tensor_copy(out=result[:], in_=out_sum[:])
+                else:
+                    nc.scalar.copy(out=result[:], in_=out_sum[:])
                 nc.sync.dma_start(out=out_view[:, 2 * pair : 2 * pair + 2, lo:hi], in_=result[:])
 
-        scatter(0, 0, BANK)
-        scatter(0, BANK, S)
-        x = picked.tile([P, M], F32, name="x", tag="x")
+        scatter(0, 0, BANK, wgs_first)
+        scatter(0, BANK, S, wgs_sb)
+        x = sbuf([P, M], F32, "x0", "row_slot2")
         gather(0, x[:], 0, M)
-        first_w2_step = 2
-        for c in range(1, LAST):
-            if c > 1:
-                load_page(c)
-            load_floor(c - 1)
-            if first_w2_step <= c < first_w2_step + PASSES:
-                load_w2(c - first_w2_step)
-            scatter(c, 0, S)
-            floor_and_turn(c - 1, x[:], 0, M)
-            x = picked.tile([P, M], F32, name="x", tag="x")
-            gather(c, x[:], 0, M)
+        for c in range(1, STEADY + 1):
+            load_floors(c - 1, 1)
+            load_page(c + 1)
+            scatter(c, 0, S, wgs_sb)
+            z = sbuf([P, 1, M], BF16, f"z{c - 1}", f"z_slot{c % 2}")
+            floored(z[:, 0, :], x[:], c - 1, 0, M)
+            turn(c - 1, 1, z, 0, M)
+            if c < STEADY:
+                x = sbuf([P, M], F32, f"x{c}", f"row_slot{c - 1}")
+                gather(c, x[:], 0, M)
+            if c <= PASSES:
+                prepare_w2(c - 1)
             if c == TILES_A_PASS:
-                quantise_w2(0, "w2_codes0")
-            if c == TILES_A_PASS + 1:
-                quantise_z(0, 0, BANK, weave(0, 0, BANK), "z_codes0")
-                woven_upper = weave(0, BANK, M)
-        load_floor(LAST - 1)
-        load_floor(LAST)
-        load_page(LAST)
-        floor_and_turn(LAST - 1, x[:], 0, M)
-        scatter(LAST, 0, S)
+                for lo, hi in spans[0]:
+                    weave_and_quantise(0, lo, hi)
+        for c in range(STEADY + 2, ROW_TILES):
+            load_page(c)
+        late = ROW_TILES - STEADY
+        load_floors(STEADY, late)
+        for c in range(STEADY + 1, ROW_TILES):
+            scatter(c, 0, S, wgs_sb)
 
-        x_last = {}
-
-        def gather_last(piece):
-            x_last[piece] = ring.tile([P, PIECE], F32, name="x_last", tag="x_last")
-            gather(LAST, x_last[piece][:], piece * PIECE, (piece + 1) * PIECE)
-
-        gather_last(0)
-        for lo, hi in LAST_SPANS:
-            piece = lo // PIECE
-            if piece + 1 < M // PIECE:
-                gather_last(piece + 1)
-            floor_and_turn(LAST, x_last[piece][:, lo - piece * PIECE : hi - piece * PIECE], lo, hi)
-        quantise_w2(1, "wgs")
-        for lo, hi in LAST_SPANS:
-            if lo == PIECE:
-                quantise_z(0, BANK, M, woven_upper, f"h{LAST}")
-            quantise_z(1, lo, hi, weave(1, lo, hi), f"z_codes1_{lo}")
-            product(lo, hi)
+        x = sbuf([P, late, PIECE], F32, "x_late", f"floor{STEADY - 1}")
+        for piece in range(M // PIECE):
+            lo, hi = piece * PIECE, (piece + 1) * PIECE
+            for i in range(late):
+                gather(STEADY + i, x[:, i, :], lo, hi)
+            z = sbuf([P, late, PIECE], BF16, f"z_late{piece}", f"z_t1_{lo - PIECE}" if piece else None)
+            for i in range(late - 1):
+                floored(z[:, i, :], x[:, i, :], STEADY + i, lo, hi)
+            mine = [s for s, (at, end) in enumerate(SPANS) if lo <= at and end <= hi]
+            turn(STEADY, late - 1, z[:, 0 : late - 1, :], lo, hi)
+            for s in mine:
+                at, end = SPANS[s]
+                floored(z[:, late - 1, at - lo : end - lo], x[:, late - 1, at - lo : end - lo], LAST, at, end)
+                turn(LAST, 1, z[:, late - 1 : late, at - lo : end - lo], at, end)
+            for s in mine:
+                weave_and_quantise(1, *SPANS[s])
+            for s in mine:
+                product(s, [[], [], [0, 1], [1], [1]][s])

@@ -42,6 +42,7 @@ def tile_list_fetal_slice_mosaic_kernel(
     with ExitStack() as ctx:
         lists = ctx.enter_context(tc.tile_pool(name="lists", bufs=1))
         keep = ctx.enter_context(tc.tile_pool(name="keep", bufs=1))
+        ending = ctx.enter_context(tc.tile_pool(name="ending", bufs=1))
         banks = ctx.enter_context(tc.psum_pool(name="banks", bufs=1))
         turns = ctx.enter_context(tc.psum_pool(name="turns", bufs=2))
 
@@ -56,6 +57,8 @@ def tile_list_fetal_slice_mosaic_kernel(
             return listed[:, lo // PER_COLUMN : hi // PER_COLUMN]
 
         nc.sync.dma_start(idx[:], offs)
+        w1_sc = sbuf([P, PASSES, H], U8, "w1_sc")
+        nc.vector.memset(w1_sc[:].bitcast(I32), 0)
         tab_sc = sbuf([P, T], U8, "tab_sc", "page_slot0")
         for quad in range(QUADRANTS):
             nc.sync.dma_start(
@@ -63,40 +66,39 @@ def tile_list_fetal_slice_mosaic_kernel(
                 in_=tab_scales[:, PACK * quad : PACK * (quad + 1), :].bitcast(I32),
             )
             nc.vector.memset(tab_sc[QUADRANT * quad : QUADRANT * quad + SCALE_ROW, :].bitcast(I32), 0)
-        tab_w = [sbuf([P, T], I32, "tab_w0", "wgs_slot"), sbuf([P, T], I32, "tab_w1", "page_slot1")]
-        for a in range(PASSES):
-            nc.sync.dma_start(out=tab_w[a][:], in_=tab_words[a].rearrange("p t i -> p (t i)").bitcast(I32))
+        nc.sync.dma_start(idx2[:], offs2)
+        nc.sync.dma_start(idx3[:], offs3)
         w1_view = w1_words.rearrange("a p c -> p a c")
         w1_first = sbuf([P, PASSES, 2 * P], U8, "w1_first", "row_slot0")
         nc.sync.dma_start(out=w1_first[:].bitcast(I32), in_=w1_view[:, :, 0 : 2 * P].bitcast(I32))
-        nc.sync.dma_start(idx2[:], offs2)
+        tab_w = [sbuf([P, T], I32, "tab_w0", "wgs_slot"), sbuf([P, T], I32, "tab_w1", "page_slot1")]
+        for a in range(PASSES):
+            nc.sync.dma_start(out=tab_w[a][:], in_=tab_words[a].rearrange("p t i -> p (t i)").bitcast(I32))
+        for quad in range(QUADRANTS):
+            nc.sync.dma_start(
+                out=w1_sc[QUADRANT * quad : QUADRANT * quad + PACK, :, :].bitcast(I32),
+                in_=w1_scales[:, PACK * quad : PACK * (quad + 1), :].rearrange("a r c -> r a c").bitcast(I32),
+            )
         wgs_first = sbuf([P, BANK], F32, "wgs_first", "page_slot2")
         nc.sync.dma_start(out=wgs_first[:], in_=wgs[:, 0:BANK])
-        nc.sync.dma_start(idx3[:], offs3)
         pages = {}
 
         def load_page(c):
             pages[c] = sbuf([P, T2], F32, f"page{c}", f"page_slot{c % SLOTS}" if c < LAST else "row_slot2")
-            nc.sync.dma_start(out=pages[c][:], in_=page0[c * P : (c + 1) * P, :])
+            if c < STEADY:
+                rows = page0[c * P : (c + 1) * P, :]
+            else:
+                rows = page0[STEADY * P :, :].rearrange("(p t) c -> t p c", t=PACK)[c - STEADY]
+            nc.sync.dma_start(out=pages[c][:], in_=rows)
 
-        w1_sc = sbuf([P, PASSES, H], U8, "w1_sc")
-        nc.gpsimd.memset(w1_sc[:].bitcast(I32), 0)
-        for quad in range(QUADRANTS):
-            nc.gpsimd.dma_start(
-                out=w1_sc[QUADRANT * quad : QUADRANT * quad + PACK, :, :].bitcast(I32),
-                in_=w1_scales[:, PACK * quad : PACK * (quad + 1), :].rearrange("a r c -> r a c").bitcast(I32),
-            )
         ident_f32 = sbuf([P, P], F32, "ident_f32")
         make_identity(nc, ident_f32[:])
         ident_bf = sbuf([P, P], BF16, "ident_bf")
         nc.scalar.activation(out=ident_bf[:], in_=ident_f32[:], func=IDENTITY)
-        bias_rows = sbuf([P, P], F32, "bias_rows")
-        nc.gpsimd.memset(bias_rows[:], 0.0)
-        nc.gpsimd.dma_start(out=bias_rows[0:ROW_TILES, :], in_=bias.rearrange("(c p) -> c p", p=P))
 
         v_sc = [sbuf([P, S], U8, f"v_sc{a}") for a in range(PASSES)]
         for a in range(PASSES):
-            nc.vector.memset(v_sc[a][P - QUADRANT : P, :].bitcast(I32), 0)
+            nc.gpsimd.memset(v_sc[a][P - QUADRANT : P, :].bitcast(I32), 0)
         picked_sc = sbuf([P, S], U8, "picked_sc", "weights_slot")
         nc.vector.tensor_copy(picked_sc[:], tab_sc[:].indirect(idx[:]))
         for a in range(PASSES):
@@ -105,7 +107,7 @@ def tile_list_fetal_slice_mosaic_kernel(
                 out=v_sc[a][0:LIVE_ROWS, :].bitcast(I32), in_=picked_sc[first : first + LIVE_ROWS, :].bitcast(I32)
             )
         load_page(0)
-        v_w = [sbuf([P, S], U32, "v_w0", "row_slot2"), sbuf([P, S], U32, "v_w1")]
+        v_w = [sbuf([P, S], U32, "v_w0"), sbuf([P, S], U32, "v_w1")]
         nc.vector.tensor_copy(v_w[0][:], tab_w[0][:].bitcast(U32).indirect(idx[:]))
         wgs_sb = sbuf([P, S], F32, "wgs_sb", "wgs_slot")
         nc.sync.dma_start(out=wgs_sb[:], in_=wgs)
@@ -141,18 +143,58 @@ def tile_list_fetal_slice_mosaic_kernel(
 
         first_product(0)
         first_product(1)
-        bias_turned = banks.tile([P, P], F32, name="bias_turned", tag="bank0")
-        nc.tensor.transpose(bias_turned[:], bias_rows[:], ident_f32[:])
+        bias_sb = sbuf([P, PASSES, 2 * PACK], F32, "bias_sb", "row_slot0")
+        with nc.allow_non_contiguous_dma(reason="one value of the bias for each partition and row tile"):
+            nc.sync.dma_start(out=bias_sb[:, 0, 0:PACK], in_=bias[0 : STEADY * P].rearrange("(c p) -> p c", p=P))
+        nc.sync.dma_start(out=bias_sb[:, 1, 0:PACK], in_=bias[STEADY * P :].rearrange("(p t) -> p t", t=PACK))
         neg_bias = sbuf([P, ROW_TILES], F32, "neg_bias")
-        nc.scalar.activation(out=neg_bias[:], in_=bias_turned[:, 0:ROW_TILES], func=IDENTITY, scale=-1.0)
-        for c in range(2, ROW_TILES):
-            first_product(c)
+        nc.scalar.activation(
+            out=neg_bias[:].rearrange("p (g t) -> p g t", t=PACK), in_=bias_sb[:, :, 0:PACK], func=IDENTITY, scale=-1.0
+        )
+        h_turned = sbuf([P, S // P, PACK, P], F32, "h_turned")
+        upper = STEADY * P
+
+        def upper_product():
+            for b in range(S // P):
+                cols = slice(b * P, (b + 1) * P)
+                h_sum = banks.tile([P, BANK], F32, name="h_sum", tag=f"bank{b % 4}")
+                for a in range(PASSES):
+                    nc.tensor.matmul_mx(
+                        out=h_sum[:],
+                        lhsT=v_w[a][:, cols].bitcast(FP8X4),
+                        lhsT_scale=v_sc[a][:, cols],
+                        rhs=w1_rest[:, a, 2 * (upper - P) :].bitcast(FP4X4),
+                        rhs_scale=w1_sc[:, a, upper:],
+                        start=(a == 0),
+                        stop=(a == PASSES - 1),
+                    )
+                nc.scalar.copy(out=h_turned[:, b, :, :], in_=h_sum[:].rearrange("j (p t) -> j t p", t=PACK))
+
+        wgs_dealt = {}
+
+        def load_wgs_dealt(t, slot):
+            wgs_dealt[t] = sbuf([P, S], F32, f"wgs_dealt{t}", slot)
+            for quad in range(QUADRANTS):
+                nc.sync.dma_start(
+                    out=wgs_dealt[t][QUADRANT * quad : QUADRANT * (quad + 1), :],
+                    in_=wgs.rearrange("(q t) j -> t q j", t=PACK)[t],
+                )
+
+        def turn_h_back(t):
+            h_sb[STEADY + t] = sbuf([P, S], F32, f"h{STEADY + t}")
+            for half in range(S // BANK):
+                back = turns.tile([P, BANK // P, P], F32, name="back", tag="back")
+                for b in range(BANK // P):
+                    nc.tensor.transpose(back[:, b, :], h_turned[:, half * BANK // P + b, t, :], ident_f32[:])
+                nc.scalar.copy(
+                    out=h_sb[STEADY + t][:, half * BANK : (half + 1) * BANK], in_=back[:].rearrange("p b j -> p (b j)")
+                )
 
         floor = {}
 
         def load_floors(c, count):
             rows = sbuf([P, count, M], F32, f"low{c}", f"row_slot{c % SLOTS}" if count == 1 else f"floor{c - 1}")
-            nc.sync.dma_start(out=rows[:], in_=low[c * P : (c + count) * P, :].rearrange("(i p) m -> p i m", p=P))
+            nc.sync.dma_start(out=rows[:], in_=low[c * P : (c + count) * P, :].rearrange("(p i) m -> p i m", p=P))
             for i in range(count):
                 floor[c + i] = sbuf([P, M], F32, f"floor{c + i}")
                 nc.scalar.activation(
@@ -163,7 +205,7 @@ def tile_list_fetal_slice_mosaic_kernel(
         w2_sc = sbuf([P, PASSES, N], U8, "w2_sc")
 
         def prepare_w2(g):
-            w2_rows = sbuf([P, PACK, N], F32, f"w2_rows{g}", "weights_slot")
+            w2_rows = sbuf([P, PACK, N], F32, f"w2_rows{g}", f"floor{g + 1}")
             rows = w2[g * P * PACK : (g + 1) * P * PACK, :]
             nc.sync.dma_start(out=w2_rows[:], in_=rows.rearrange("(p t) n -> p t n", t=PACK))
             w2_bf = sbuf([P, N, PACK], BF16, f"w2_bf{g}")
@@ -185,9 +227,9 @@ def tile_list_fetal_slice_mosaic_kernel(
         def floored(z, x, c, lo, hi):
             nc.vector.scalar_tensor_tensor(z, x, neg_bias[:, c : c + 1], floor[c][:, lo:hi], ALU.add, ALU.max)
 
-        spans = {0: [(0, BANK), (BANK, M)], 1: SPANS}
+        spans = {0: [(0, BANK), (BANK, M)]}
         z_t = {}
-        for g in range(PASSES):
+        for g in range(1):
             for lo, hi in spans[g]:
                 z_t[(g, lo)] = sbuf([P, (hi - lo) // P, 2, P], F32, f"z_t{g}_{lo}")
         share = P // PACK
@@ -226,17 +268,26 @@ def tile_list_fetal_slice_mosaic_kernel(
                     out=pairs.rearrange("p (b m u) -> p b m u", b=blocks, u=2),
                     in_=back[:].rearrange("p b u m -> p b m u"),
                 )
+            quantise(g, lo, hi, woven[:])
+
+        def quantise(g, lo, hi, woven):
             z_codes[(g, lo)] = sbuf([P, hi - lo], U32, f"z_codes{g}_{lo}")
-            nc.vector.quantize_mx(out=z_codes[(g, lo)][:].bitcast(FP8X4), scales=z_sc[g][:, lo:hi], in_=woven[:])
+            nc.vector.quantize_mx(out=z_codes[(g, lo)][:].bitcast(FP8X4), scales=z_sc[g][:, lo:hi], in_=woven)
 
         out_view = out.rearrange("(j p) m -> p j m", p=P)
 
-        def product(span, on_vector):
+        sums = {}
+
+        def product(span):
             lo, hi = SPANS[span]
             half_start = lo // BANK * BANK
             moving = [z_codes[(0, half_start)][:, lo - half_start : hi - half_start], z_codes[(1, lo)][:]]
             for pair in range(N // (2 * P)):
-                out_sum = banks.tile([P, 2, hi - lo], F32, name="out_sum", tag=f"bank{(2 * span + pair) % 4}")
+                bank = (2 * span + pair) % 8
+                if bank < 4:
+                    out_sum = banks.tile([P, 2, hi - lo], F32, name="out_sum", tag=f"bank{bank}")
+                else:
+                    out_sum = turns.tile([P, 2, hi - lo], F32, name="out_sum", tag="turned" if bank < 6 else "back")
                 for g in range(PASSES):
                     for j in range(2):
                         n_cols = slice((2 * pair + j) * P, (2 * pair + j + 1) * P)
@@ -249,12 +300,12 @@ def tile_list_fetal_slice_mosaic_kernel(
                             start=(g == 0 and j == 0),
                             stop=(g == PASSES - 1 and j == 1),
                         )
-                result = sbuf([P, 2, hi - lo], F32, f"result{span}_{pair}")
-                if pair in on_vector:
-                    nc.vector.tensor_copy(out=result[:], in_=out_sum[:])
-                else:
-                    nc.scalar.copy(out=result[:], in_=out_sum[:])
-                nc.sync.dma_start(out=out_view[:, 2 * pair : 2 * pair + 2, lo:hi], in_=result[:])
+                sums[(span, pair)] = out_sum
+
+        def store(span, pair, engine_copy, result):
+            lo, hi = SPANS[span]
+            engine_copy(out=result, in_=sums[(span, pair)][:])
+            nc.sync.dma_start(out=out_view[:, 2 * pair : 2 * pair + 2, lo:hi], in_=result)
 
         scatter(0, 0, BANK, wgs_first)
         scatter(0, BANK, S, wgs_sb)
@@ -263,40 +314,68 @@ def tile_list_fetal_slice_mosaic_kernel(
         for c in range(1, STEADY + 1):
             load_floors(c - 1, 1)
             load_page(c + 1)
-            scatter(c, 0, S, wgs_sb)
+            if c + 1 < STEADY:
+                first_product(c + 1)
+            scatter(c, 0, S, wgs_sb if c < STEADY else wgs_dealt[0])
             z = sbuf([P, 1, M], BF16, f"z{c - 1}", f"z_slot{c % 2}")
             floored(z[:, 0, :], x[:], c - 1, 0, M)
             turn(c - 1, 1, z, 0, M)
             if c < STEADY:
                 x = sbuf([P, M], F32, f"x{c}", f"row_slot{c - 1}")
                 gather(c, x[:], 0, M)
-            if c <= PASSES:
-                prepare_w2(c - 1)
+            if c == 2:
+                upper_product()
+            load_wgs_dealt(c - 1, f"h{c}" if c < STEADY else "wgs_slot")
+            if c >= 2:
+                turn_h_back(c - 2)
+            if 2 <= c < 2 + PASSES:
+                prepare_w2(c - 2)
             if c == TILES_A_PASS:
                 for lo, hi in spans[0]:
                     weave_and_quantise(0, lo, hi)
         for c in range(STEADY + 2, ROW_TILES):
             load_page(c)
+        turn_h_back(PACK - 1)
         late = ROW_TILES - STEADY
         load_floors(STEADY, late)
         for c in range(STEADY + 1, ROW_TILES):
-            scatter(c, 0, S, wgs_sb)
+            scatter(c, 0, S, wgs_dealt[c - STEADY])
 
         x = sbuf([P, late, PIECE], F32, "x_late", f"floor{STEADY - 1}")
         for piece in range(M // PIECE):
             lo, hi = piece * PIECE, (piece + 1) * PIECE
             for i in range(late):
                 gather(STEADY + i, x[:, i, :], lo, hi)
-            z = sbuf([P, late, PIECE], BF16, f"z_late{piece}", f"z_t1_{lo - PIECE}" if piece else None)
-            for i in range(late - 1):
-                floored(z[:, i, :], x[:, i, :], STEADY + i, lo, hi)
+            last_piece = hi == M
+            if piece < 2:
+                z = sbuf([P, late, PIECE], BF16, f"z_late{piece}")
+            else:
+                z = ending.tile([P, late, PIECE], BF16, name=f"z_late{piece}", offset=1024 * (piece + 1))
             mine = [s for s, (at, end) in enumerate(SPANS) if lo <= at and end <= hi]
-            turn(STEADY, late - 1, z[:, 0 : late - 1, :], lo, hi)
+            woven = {}
             for s in mine:
                 at, end = SPANS[s]
-                floored(z[:, late - 1, at - lo : end - lo], x[:, late - 1, at - lo : end - lo], LAST, at, end)
-                turn(LAST, 1, z[:, late - 1 : late, at - lo : end - lo], at, end)
+                for i in range(late):
+                    floored(z[:, i, at - lo : end - lo], x[:, i, at - lo : end - lo], STEADY + i, at, end)
+                woven[s] = sbuf([P, end - at, PACK], BF16, f"woven1_{at}")
+                nc.scalar.copy(out=woven[s][:], in_=z[:, :, at - lo : end - lo].rearrange("p t m -> p m t"))
+            if last_piece:
+                result = sbuf([P, 2, PIECE], F32, "result_before_last", "h4")
+                store(piece - 1, 0, nc.vector.tensor_copy, result[:])
+                result = ending.tile([P, 2, PIECE], F32, name="result_before_last1", offset=4096)
+                store(piece - 1, 1, nc.scalar.copy, result[:])
+            elif piece > 0:
+                if piece == 1:
+                    result = sbuf([P, 2, 2, PIECE], F32, "result0", "z_late1")
+                else:
+                    result = ending.tile([P, 2, 2, PIECE], F32, name="result1", offset=0)
+                for pair in range(2):
+                    store(piece - 1, pair, nc.scalar.copy, result[:, pair, :, :])
             for s in mine:
-                weave_and_quantise(1, *SPANS[s])
+                quantise(1, *SPANS[s], woven[s][:].rearrange("p m t -> p (m t)"))
             for s in mine:
-                product(s, [[], [], [0, 1], [1], [1]][s])
+                product(s)
+        for s in mine:
+            for pair, engine_copy in enumerate((nc.scalar.copy, nc.vector.tensor_copy)):
+                result = sbuf([P, 2, P], F32, f"result{s}_{pair}", f"h{5 + pair}" if s == 3 else None)
+                store(s, pair, engine_copy, result[:])

@@ -28,9 +28,10 @@ ROW_TILES = H // P
 TILES_A_PASS = ROW_TILES // PASSES
 LAST = ROW_TILES - 1
 PIECE = 256
-SCALE_ROW = 24
-LIVE_ROWS = 100
+HALF = P // 2
+SCALE_ROW = 16
 SLOTS = 3
+FIRST = 256
 STEADY = 4
 SPANS = [(0, PIECE), (PIECE, 2 * PIECE), (2 * PIECE, 3 * PIECE), (3 * PIECE, M - P), (M - P, M)]
 
@@ -43,6 +44,7 @@ def tile_list_fetal_slice_mosaic_kernel(
         lists = ctx.enter_context(tc.tile_pool(name="lists", bufs=1))
         keep = ctx.enter_context(tc.tile_pool(name="keep", bufs=1))
         ending = ctx.enter_context(tc.tile_pool(name="ending", bufs=1))
+        reused = ctx.enter_context(tc.tile_pool(name="reused", bufs=1))
         banks = ctx.enter_context(tc.psum_pool(name="banks", bufs=1))
         turns = ctx.enter_context(tc.psum_pool(name="turns", bufs=2))
 
@@ -57,30 +59,43 @@ def tile_list_fetal_slice_mosaic_kernel(
             return listed[:, lo // PER_COLUMN : hi // PER_COLUMN]
 
         nc.sync.dma_start(idx[:], offs)
-        w1_sc = sbuf([P, PASSES, H], U8, "w1_sc")
-        nc.vector.memset(w1_sc[:].bitcast(I32), 0)
         tab_sc = sbuf([P, T], U8, "tab_sc", "page_slot0")
-        for quad in range(QUADRANTS):
+        rows_by_parity = tab_scales.rearrange("a (h o r) c -> o (a h) r c", o=2, r=PACK)
+        for o in range(2):
+            base = QUADRANT * o
             nc.sync.dma_start(
-                out=tab_sc[QUADRANT * quad + SCALE_ROW : QUADRANT * (quad + 1), :].bitcast(I32),
-                in_=tab_scales[:, PACK * quad : PACK * (quad + 1), :].bitcast(I32),
+                out=tab_sc[base + SCALE_ROW : base + QUADRANT, :].bitcast(I32), in_=rows_by_parity[o].bitcast(I32)
             )
-            nc.vector.memset(tab_sc[QUADRANT * quad : QUADRANT * quad + SCALE_ROW, :].bitcast(I32), 0)
+            nc.vector.memset(tab_sc[base : base + SCALE_ROW, :].bitcast(I32), 0)
+        nc.vector.memset(tab_sc[HALF:P, :].bitcast(I32), 0)
+        v_sc_both = sbuf([P, PASSES, S], U8, "v_sc")
+        v_sc = [v_sc_both[:, a, :] for a in range(PASSES)]
+        w1_sc_first = sbuf([P, PASSES, P], U8, "w1_sc_first")
+        nc.vector.memset(w1_sc_first[:].bitcast(I32), 0)
+
+        def load_w1_scales(planes, cols):
+            for quad in range(QUADRANTS):
+                rows = w1_scales[:, PACK * quad : PACK * (quad + 1), cols]
+                nc.sync.dma_start(
+                    out=planes[QUADRANT * quad : QUADRANT * quad + PACK, :, :].bitcast(I32),
+                    in_=rows.rearrange("a r c -> r a c").bitcast(I32),
+                )
+
+        tab_w = [reused.tile([P, T], I32, name="tab_w0", align_bytes=64, offset=0), sbuf([P, T], I32, "tab_w1", "page_slot1")]
+
+        def load_words(a):
+            nc.sync.dma_start(out=tab_w[a][:], in_=tab_words[a].rearrange("p t i -> p (t i)").bitcast(I32))
+
+        load_words(0)
         nc.sync.dma_start(idx2[:], offs2)
         nc.sync.dma_start(idx3[:], offs3)
         w1_view = w1_words.rearrange("a p c -> p a c")
         w1_first = sbuf([P, PASSES, 2 * P], U8, "w1_first", "row_slot0")
         nc.sync.dma_start(out=w1_first[:].bitcast(I32), in_=w1_view[:, :, 0 : 2 * P].bitcast(I32))
-        tab_w = [sbuf([P, T], I32, "tab_w0", "wgs_slot"), sbuf([P, T], I32, "tab_w1", "page_slot1")]
-        for a in range(PASSES):
-            nc.sync.dma_start(out=tab_w[a][:], in_=tab_words[a].rearrange("p t i -> p (t i)").bitcast(I32))
-        for quad in range(QUADRANTS):
-            nc.sync.dma_start(
-                out=w1_sc[QUADRANT * quad : QUADRANT * quad + PACK, :, :].bitcast(I32),
-                in_=w1_scales[:, PACK * quad : PACK * (quad + 1), :].rearrange("a r c -> r a c").bitcast(I32),
-            )
-        wgs_first = sbuf([P, BANK], F32, "wgs_first", "page_slot2")
-        nc.sync.dma_start(out=wgs_first[:], in_=wgs[:, 0:BANK])
+        wgs_first = sbuf([P, FIRST], F32, "wgs_first", "page_slot2")
+        nc.sync.dma_start(out=wgs_first[:], in_=wgs[:, 0:FIRST])
+        load_words(1)
+        load_w1_scales(w1_sc_first, slice(0, P))
         pages = {}
 
         def load_page(c):
@@ -91,55 +106,63 @@ def tile_list_fetal_slice_mosaic_kernel(
                 rows = page0[STEADY * P :, :].rearrange("(p t) c -> t p c", t=PACK)[c - STEADY]
             nc.sync.dma_start(out=pages[c][:], in_=rows)
 
-        ident_f32 = sbuf([P, P], F32, "ident_f32")
-        make_identity(nc, ident_f32[:])
-        ident_bf = sbuf([P, P], BF16, "ident_bf")
-        nc.scalar.activation(out=ident_bf[:], in_=ident_f32[:], func=IDENTITY)
 
-        v_sc = [sbuf([P, S], U8, f"v_sc{a}") for a in range(PASSES)]
-        for a in range(PASSES):
-            nc.gpsimd.memset(v_sc[a][P - QUADRANT : P, :].bitcast(I32), 0)
         picked_sc = sbuf([P, S], U8, "picked_sc", "weights_slot")
         nc.vector.tensor_copy(picked_sc[:], tab_sc[:].indirect(idx[:]))
         for a in range(PASSES):
-            first = SCALE_ROW + PACK * a
-            nc.sync.dma_start(
-                out=v_sc[a][0:LIVE_ROWS, :].bitcast(I32), in_=picked_sc[first : first + LIVE_ROWS, :].bitcast(I32)
-            )
+            for h in range(2):
+                first = SCALE_ROW + PACK * (2 * a + h)
+                nc.sync.dma_start(
+                    out=v_sc_both[HALF * h : HALF * (h + 1), a, :].bitcast(I32),
+                    in_=picked_sc[first : first + HALF, :].bitcast(I32),
+                )
         load_page(0)
         v_w = [sbuf([P, S], U32, "v_w0"), sbuf([P, S], U32, "v_w1")]
         nc.vector.tensor_copy(v_w[0][:], tab_w[0][:].bitcast(U32).indirect(idx[:]))
-        wgs_sb = sbuf([P, S], F32, "wgs_sb", "wgs_slot")
+        wgs_sb = reused.tile([P, S], F32, name="wgs_sb", align_bytes=64, offset=0)
         nc.sync.dma_start(out=wgs_sb[:], in_=wgs)
-        for lo in range(0, S, BANK):
-            part = entries(idx, lo, lo + BANK)
-            nc.vector.tensor_copy(v_w[1][:, lo : lo + BANK], tab_w[1][:].bitcast(U32).indirect(part))
+        w1_sc_rest = reused.tile([P, PASSES, H - P], U8, name="w1_sc_rest", align_bytes=64, offset=4 * S)
+        nc.gpsimd.memset(w1_sc_rest[:].bitcast(I32), 0)
+        load_w1_scales(w1_sc_rest, slice(P, H))
+        for lo, hi in ((0, FIRST), (FIRST, S)):
+            nc.vector.tensor_copy(v_w[1][:, lo:hi], tab_w[1][:].bitcast(U32).indirect(entries(idx, lo, hi)))
         w1_rest = sbuf([P, PASSES, 2 * (H - P)], U8, "w1_rest", "weights_slot")
         nc.sync.dma_start(out=w1_rest[:].bitcast(I32), in_=w1_view[:, :, 2 * P :].bitcast(I32))
         load_page(1)
 
         h_sb = {}
 
+        used_banks = []
+
+        def next_bank(shape, name):
+            used_banks.append(name)
+            return banks.tile(shape, F32, name=name, tag=f"bank{len(used_banks) % 4}")
+
         def first_product(c):
             h_sb[c] = sbuf([P, S], F32, f"h{c}", "row_slot1" if c == 0 else None)
-            for half in range(S // BANK):
-                cols = slice(half * BANK, (half + 1) * BANK)
-                h_sum = banks.tile([P, BANK], F32, name="h_sum", tag=f"bank{(2 * c + half) % 4}")
-                for a in range(PASSES):
-                    if c == 0:
-                        w1_codes = w1_first[:, a, :]
-                    else:
-                        w1_codes = w1_rest[:, a, 2 * P * (c - 1) : 2 * P * c]
-                    nc.tensor.matmul_mx(
-                        out=h_sum[:],
-                        lhsT=w1_codes.bitcast(FP4X4),
-                        lhsT_scale=w1_sc[:, a, c * P : (c + 1) * P],
-                        rhs=v_w[a][:, cols].bitcast(FP8X4),
-                        rhs_scale=v_sc[a][:, cols],
-                        start=(a == 0),
-                        stop=(a == PASSES - 1),
-                    )
-                nc.scalar.copy(out=h_sb[c][:, cols], in_=h_sum[:])
+            if c == 0:
+                parts = [(0, FIRST, P), (FIRST, FIRST + BANK, BANK), (FIRST + BANK, S, P)]
+            else:
+                parts = [(0, BANK, BANK), (BANK, S, BANK)]
+            for lo, hi, width in parts:
+                h_sum = next_bank([P, hi - lo], "h_sum")
+                for at in range(lo, hi, width):
+                    for a in range(PASSES):
+                        if c == 0:
+                            w1_codes, w1_scale = w1_first[:, a, :], w1_sc_first[:, a, :]
+                        else:
+                            w1_codes = w1_rest[:, a, 2 * P * (c - 1) : 2 * P * c]
+                            w1_scale = w1_sc_rest[:, a, P * (c - 1) : P * c]
+                        nc.tensor.matmul_mx(
+                            out=h_sum[:, at - lo : at - lo + width],
+                            lhsT=w1_codes.bitcast(FP4X4),
+                            lhsT_scale=w1_scale,
+                            rhs=v_w[a][:, at : at + width].bitcast(FP8X4),
+                            rhs_scale=v_sc[a][:, at : at + width],
+                            start=(a == 0),
+                            stop=(a == PASSES - 1),
+                        )
+                nc.scalar.copy(out=h_sb[c][:, lo:hi], in_=h_sum[:])
 
         first_product(0)
         first_product(1)
@@ -147,6 +170,10 @@ def tile_list_fetal_slice_mosaic_kernel(
         with nc.allow_non_contiguous_dma(reason="one value of the bias for each partition and row tile"):
             nc.sync.dma_start(out=bias_sb[:, 0, 0:PACK], in_=bias[0 : STEADY * P].rearrange("(c p) -> p c", p=P))
         nc.sync.dma_start(out=bias_sb[:, 1, 0:PACK], in_=bias[STEADY * P :].rearrange("(p t) -> p t", t=PACK))
+        ident_f32 = sbuf([P, P], F32, "ident_f32")
+        make_identity(nc, ident_f32[:])
+        ident_bf = sbuf([P, P], BF16, "ident_bf")
+        nc.scalar.activation(out=ident_bf[:], in_=ident_f32[:], func=IDENTITY)
         neg_bias = sbuf([P, ROW_TILES], F32, "neg_bias")
         nc.scalar.activation(
             out=neg_bias[:].rearrange("p (g t) -> p g t", t=PACK), in_=bias_sb[:, :, 0:PACK], func=IDENTITY, scale=-1.0
@@ -157,14 +184,14 @@ def tile_list_fetal_slice_mosaic_kernel(
         def upper_product():
             for b in range(S // P):
                 cols = slice(b * P, (b + 1) * P)
-                h_sum = banks.tile([P, BANK], F32, name="h_sum", tag=f"bank{b % 4}")
+                h_sum = next_bank([P, BANK], "h_sum")
                 for a in range(PASSES):
                     nc.tensor.matmul_mx(
                         out=h_sum[:],
                         lhsT=v_w[a][:, cols].bitcast(FP8X4),
                         lhsT_scale=v_sc[a][:, cols],
                         rhs=w1_rest[:, a, 2 * (upper - P) :].bitcast(FP4X4),
-                        rhs_scale=w1_sc[:, a, upper:],
+                        rhs_scale=w1_sc_rest[:, a, upper - P :],
                         start=(a == 0),
                         stop=(a == PASSES - 1),
                     )
@@ -173,7 +200,10 @@ def tile_list_fetal_slice_mosaic_kernel(
         wgs_dealt = {}
 
         def load_wgs_dealt(t, slot):
-            wgs_dealt[t] = sbuf([P, S], F32, f"wgs_dealt{t}", slot)
+            if slot:
+                wgs_dealt[t] = sbuf([P, S], F32, f"wgs_dealt{t}", slot)
+            else:
+                wgs_dealt[t] = reused.tile([P, S], F32, name=f"wgs_dealt{t}", align_bytes=64, offset=0)
             for quad in range(QUADRANTS):
                 nc.sync.dma_start(
                     out=wgs_dealt[t][QUADRANT * quad : QUADRANT * (quad + 1), :],
@@ -307,8 +337,8 @@ def tile_list_fetal_slice_mosaic_kernel(
             engine_copy(out=result, in_=sums[(span, pair)][:])
             nc.sync.dma_start(out=out_view[:, 2 * pair : 2 * pair + 2, lo:hi], in_=result)
 
-        scatter(0, 0, BANK, wgs_first)
-        scatter(0, BANK, S, wgs_sb)
+        scatter(0, 0, FIRST, wgs_first)
+        scatter(0, FIRST, S, wgs_sb)
         x = sbuf([P, M], F32, "x0", "row_slot2")
         gather(0, x[:], 0, M)
         for c in range(1, STEADY + 1):
@@ -325,7 +355,7 @@ def tile_list_fetal_slice_mosaic_kernel(
                 gather(c, x[:], 0, M)
             if c == 2:
                 upper_product()
-            load_wgs_dealt(c - 1, f"h{c}" if c < STEADY else "wgs_slot")
+            load_wgs_dealt(c - 1, f"h{c}" if c < STEADY else None)
             if c >= 2:
                 turn_h_back(c - 2)
             if 2 <= c < 2 + PASSES:
@@ -346,29 +376,28 @@ def tile_list_fetal_slice_mosaic_kernel(
             lo, hi = piece * PIECE, (piece + 1) * PIECE
             for i in range(late):
                 gather(STEADY + i, x[:, i, :], lo, hi)
-            last_piece = hi == M
-            if piece < 2:
-                z = sbuf([P, late, PIECE], BF16, f"z_late{piece}")
-            else:
-                z = ending.tile([P, late, PIECE], BF16, name=f"z_late{piece}", offset=1024 * (piece + 1))
             mine = [s for s, (at, end) in enumerate(SPANS) if lo <= at and end <= hi]
             woven = {}
             for s in mine:
                 at, end = SPANS[s]
+                if s >= 2:
+                    z = ending.tile(
+                        [P, late, end - at], BF16, name=f"z_late{s}", align_bytes=64, offset=(3584, 4096, 5120)[s - 2]
+                    )
+                else:
+                    z = sbuf([P, late, end - at], BF16, f"z_late{s}")
                 for i in range(late):
-                    floored(z[:, i, at - lo : end - lo], x[:, i, at - lo : end - lo], STEADY + i, at, end)
+                    floored(z[:, i, :], x[:, i, at - lo : end - lo], STEADY + i, at, end)
                 woven[s] = sbuf([P, end - at, PACK], BF16, f"woven1_{at}")
-                nc.scalar.copy(out=woven[s][:], in_=z[:, :, at - lo : end - lo].rearrange("p t m -> p m t"))
-            if last_piece:
-                result = sbuf([P, 2, PIECE], F32, "result_before_last", "h4")
-                store(piece - 1, 0, nc.vector.tensor_copy, result[:])
-                result = ending.tile([P, 2, PIECE], F32, name="result_before_last1", offset=4096)
-                store(piece - 1, 1, nc.scalar.copy, result[:])
-            elif piece > 0:
+                weave = nc.vector.tensor_copy if end == M else nc.scalar.copy
+                weave(out=woven[s][:], in_=z[:].rearrange("p t m -> p m t"))
+            if piece > 0:
                 if piece == 1:
                     result = sbuf([P, 2, 2, PIECE], F32, "result0", "z_late1")
+                elif piece == 2:
+                    result = ending.tile([P, 2, 2, PIECE], F32, name="result1", align_bytes=64, offset=0)
                 else:
-                    result = ending.tile([P, 2, 2, PIECE], F32, name="result1", offset=0)
+                    result = sbuf([P, 2, 2, PIECE], F32, "result2", f"floor{STEADY - 1}")
                 for pair in range(2):
                     store(piece - 1, pair, nc.scalar.copy, result[:, pair, :, :])
             for s in mine:

@@ -58,6 +58,8 @@ def tile_list_fetal_slice_mosaic_kernel(
         def entries(listed, lo, hi):
             return listed[:, lo // PER_COLUMN : hi // PER_COLUMN]
 
+        w1_sc_first = sbuf([P, PASSES, P], U8, "w1_sc_first")
+        nc.vector.memset(w1_sc_first[:].bitcast(I32), 0)
         nc.sync.dma_start(idx[:], offs)
         tab_sc = sbuf([P, T], U8, "tab_sc", "page_slot0")
         rows_by_parity = tab_scales.rearrange("a (h o r) c -> o (a h) r c", o=2, r=PACK)
@@ -70,8 +72,6 @@ def tile_list_fetal_slice_mosaic_kernel(
         nc.vector.memset(tab_sc[HALF:P, :].bitcast(I32), 0)
         v_sc_both = sbuf([P, PASSES, S], U8, "v_sc")
         v_sc = [v_sc_both[:, a, :] for a in range(PASSES)]
-        w1_sc_first = sbuf([P, PASSES, P], U8, "w1_sc_first")
-        nc.vector.memset(w1_sc_first[:].bitcast(I32), 0)
 
         def load_w1_scales(planes, cols):
             for quad in range(QUADRANTS):
@@ -86,7 +86,6 @@ def tile_list_fetal_slice_mosaic_kernel(
         def load_words(a):
             nc.sync.dma_start(out=tab_w[a][:], in_=tab_words[a].rearrange("p t i -> p (t i)").bitcast(I32))
 
-        load_words(0)
         nc.sync.dma_start(idx2[:], offs2)
         nc.sync.dma_start(idx3[:], offs3)
         w1_view = w1_words.rearrange("a p c -> p a c")
@@ -94,8 +93,9 @@ def tile_list_fetal_slice_mosaic_kernel(
         nc.sync.dma_start(out=w1_first[:].bitcast(I32), in_=w1_view[:, :, 0 : 2 * P].bitcast(I32))
         wgs_first = sbuf([P, FIRST], F32, "wgs_first", "page_slot2")
         nc.sync.dma_start(out=wgs_first[:], in_=wgs[:, 0:FIRST])
-        load_words(1)
+        load_words(0)
         load_w1_scales(w1_sc_first, slice(0, P))
+        load_words(1)
         pages = {}
 
         def load_page(c):

@@ -32,6 +32,7 @@ HALF = P // 2
 SCALE_ROW = 16
 SLOTS = 3
 FIRST = 256
+ROW_OFFSETS = {"row_slot0": 0, "bias": 4096, "across": 3712}
 STEADY = 4
 SPANS = [(0, PIECE), (PIECE, 2 * PIECE), (2 * PIECE, 3 * PIECE), (3 * PIECE, M - P), (M - P, M)]
 
@@ -45,10 +46,13 @@ def tile_list_fetal_slice_mosaic_kernel(
         keep = ctx.enter_context(tc.tile_pool(name="keep", bufs=1))
         ending = ctx.enter_context(tc.tile_pool(name="ending", bufs=1))
         reused = ctx.enter_context(tc.tile_pool(name="reused", bufs=1))
+        rows_pool = ctx.enter_context(tc.tile_pool(name="rows_pool", bufs=1))
         banks = ctx.enter_context(tc.psum_pool(name="banks", bufs=1))
         turns = ctx.enter_context(tc.psum_pool(name="turns", bufs=2))
 
         def sbuf(shape, dtype, name, tag=None):
+            if tag in ROW_OFFSETS:
+                return rows_pool.tile(shape, dtype, name=name, align_bytes=64, offset=ROW_OFFSETS[tag])
             return keep.tile(shape, dtype, name=name, tag=tag or name, align_bytes=64)
 
         idx = lists.tile([P, S // PER_COLUMN], U16, name="idx")
@@ -89,7 +93,7 @@ def tile_list_fetal_slice_mosaic_kernel(
         nc.sync.dma_start(idx2[:], offs2)
         nc.sync.dma_start(idx3[:], offs3)
         w1_view = w1_words.rearrange("a p c -> p a c")
-        w1_first = sbuf([P, PASSES, 2 * P], U8, "w1_first", "row_slot0")
+        w1_first = sbuf([P, PASSES, 2 * P], U8, "w1_first", "across")
         nc.sync.dma_start(out=w1_first[:].bitcast(I32), in_=w1_view[:, :, 0 : 2 * P].bitcast(I32))
         wgs_first = sbuf([P, FIRST], F32, "wgs_first", "page_slot2")
         nc.sync.dma_start(out=wgs_first[:], in_=wgs[:, 0:FIRST])
@@ -166,7 +170,7 @@ def tile_list_fetal_slice_mosaic_kernel(
 
         first_product(0)
         first_product(1)
-        bias_sb = sbuf([P, PASSES, 2 * PACK], F32, "bias_sb", "row_slot0")
+        bias_sb = sbuf([P, PASSES, 4 * PACK], F32, "bias_sb", "bias")
         with nc.allow_non_contiguous_dma(reason="one value of the bias for each partition and row tile"):
             nc.sync.dma_start(out=bias_sb[:, 0, 0:PACK], in_=bias[0 : STEADY * P].rearrange("(c p) -> p c", p=P))
         nc.sync.dma_start(out=bias_sb[:, 1, 0:PACK], in_=bias[STEADY * P :].rearrange("(p t) -> p t", t=PACK))
@@ -213,7 +217,7 @@ def tile_list_fetal_slice_mosaic_kernel(
         def turn_h_back(t):
             h_sb[STEADY + t] = sbuf([P, S], F32, f"h{STEADY + t}")
             for half in range(S // BANK):
-                back = turns.tile([P, BANK // P, P], F32, name="back", tag="back")
+                back = turns.tile([P, BANK // P, P], F32, name="back", tag="back" if t < PACK - 1 else "turned")
                 for b in range(BANK // P):
                     nc.tensor.transpose(back[:, b, :], h_turned[:, half * BANK // P + b, t, :], ident_f32[:])
                 nc.scalar.copy(
@@ -235,7 +239,7 @@ def tile_list_fetal_slice_mosaic_kernel(
         w2_sc = sbuf([P, PASSES, N], U8, "w2_sc")
 
         def prepare_w2(g):
-            w2_rows = sbuf([P, PACK, N], F32, f"w2_rows{g}", f"floor{g + 1}")
+            w2_rows = sbuf([P, PACK, N], F32, f"w2_rows{g}", ("floor2", "h4")[g])
             rows = w2[g * P * PACK : (g + 1) * P * PACK, :]
             nc.sync.dma_start(out=w2_rows[:], in_=rows.rearrange("(p t) n -> p t n", t=PACK))
             w2_bf = sbuf([P, N, PACK], BF16, f"w2_bf{g}")
@@ -313,11 +317,11 @@ def tile_list_fetal_slice_mosaic_kernel(
             half_start = lo // BANK * BANK
             moving = [z_codes[(0, half_start)][:, lo - half_start : hi - half_start], z_codes[(1, lo)][:]]
             for pair in range(N // (2 * P)):
-                bank = (2 * span + pair) % 8
+                bank = 2 * (0, 1, 2, 1, 0)[span] + pair
                 if bank < 4:
                     out_sum = banks.tile([P, 2, hi - lo], F32, name="out_sum", tag=f"bank{bank}")
                 else:
-                    out_sum = turns.tile([P, 2, hi - lo], F32, name="out_sum", tag="turned" if bank < 6 else "back")
+                    out_sum = turns.tile([P, 2, hi - lo], F32, name="out_sum", tag="turned")
                 for g in range(PASSES):
                     for j in range(2):
                         n_cols = slice((2 * pair + j) * P, (2 * pair + j + 1) * P)
@@ -342,30 +346,32 @@ def tile_list_fetal_slice_mosaic_kernel(
         x = sbuf([P, M], F32, "x0", "row_slot2")
         gather(0, x[:], 0, M)
         for c in range(1, STEADY + 1):
-            load_floors(c - 1, 1)
+            if c != 2:
+                load_floors(c - 1, 1)
             load_page(c + 1)
-            if c + 1 < STEADY:
-                first_product(c + 1)
+            if c == 1:
+                first_product(2)
             scatter(c, 0, S, wgs_sb if c < STEADY else wgs_dealt[0])
-            z = sbuf([P, 1, M], BF16, f"z{c - 1}", f"z_slot{c % 2}")
+            z = sbuf([P, 1, M], BF16, f"z{c - 1}")
             floored(z[:, 0, :], x[:], c - 1, 0, M)
-            turn(c - 1, 1, z, 0, M)
             if c < STEADY:
                 x = sbuf([P, M], F32, f"x{c}", f"row_slot{c - 1}")
                 gather(c, x[:], 0, M)
-            if c == 2:
+            if c == 1:
+                load_floors(1, 1)
+                first_product(3)
                 upper_product()
+                for t in range(PACK):
+                    turn_h_back(t)
+            turn(c - 1, 1, z, 0, M)
             load_wgs_dealt(c - 1, f"h{c}" if c < STEADY else None)
-            if c >= 2:
-                turn_h_back(c - 2)
-            if 2 <= c < 2 + PASSES:
-                prepare_w2(c - 2)
             if c == TILES_A_PASS:
                 for lo, hi in spans[0]:
                     weave_and_quantise(0, lo, hi)
         for c in range(STEADY + 2, ROW_TILES):
             load_page(c)
-        turn_h_back(PACK - 1)
+        for g in range(PASSES):
+            prepare_w2(g)
         late = ROW_TILES - STEADY
         load_floors(STEADY, late)
         for c in range(STEADY + 1, ROW_TILES):
@@ -378,6 +384,7 @@ def tile_list_fetal_slice_mosaic_kernel(
                 gather(STEADY + i, x[:, i, :], lo, hi)
             mine = [s for s, (at, end) in enumerate(SPANS) if lo <= at and end <= hi]
             woven = {}
+            planes = {}
             for s in mine:
                 at, end = SPANS[s]
                 if s >= 2:
@@ -388,16 +395,19 @@ def tile_list_fetal_slice_mosaic_kernel(
                     z = sbuf([P, late, end - at], BF16, f"z_late{s}")
                 for i in range(late):
                     floored(z[:, i, :], x[:, i, at - lo : end - lo], STEADY + i, at, end)
+                planes[s] = z
+            for s in mine:
+                at, end = SPANS[s]
                 woven[s] = sbuf([P, end - at, PACK], BF16, f"woven1_{at}")
-                weave = nc.vector.tensor_copy if end == M else nc.scalar.copy
-                weave(out=woven[s][:], in_=z[:].rearrange("p t m -> p m t"))
+                weave = nc.vector.tensor_copy if hi == M else nc.scalar.copy
+                weave(out=woven[s][:], in_=planes[s][:].rearrange("p t m -> p m t"))
             if piece > 0:
                 if piece == 1:
                     result = sbuf([P, 2, 2, PIECE], F32, "result0", "z_late1")
                 elif piece == 2:
                     result = ending.tile([P, 2, 2, PIECE], F32, name="result1", align_bytes=64, offset=0)
                 else:
-                    result = sbuf([P, 2, 2, PIECE], F32, "result2", f"floor{STEADY - 1}")
+                    result = sbuf([P, 2, 2, PIECE], F32, "result2", "h7")
                 for pair in range(2):
                     store(piece - 1, pair, nc.scalar.copy, result[:, pair, :, :])
             for s in mine:

@@ -74,6 +74,8 @@ def tile_list_fetal_slice_mosaic_kernel(
             )
             nc.vector.memset(tab_sc[base : base + SCALE_ROW, :].bitcast(I32), 0)
         nc.vector.memset(tab_sc[HALF:P, :].bitcast(I32), 0)
+        zero_word = sbuf([P, 1, 1], I32, "zero_word")
+        nc.vector.memset(zero_word[:], 0)
         v_sc_both = sbuf([P, PASSES, S], U8, "v_sc")
         v_sc = [v_sc_both[:, a, :] for a in range(PASSES)]
 
@@ -126,7 +128,7 @@ def tile_list_fetal_slice_mosaic_kernel(
         wgs_sb = reused.tile([P, S], F32, name="wgs_sb", align_bytes=64, offset=0)
         nc.sync.dma_start(out=wgs_sb[:], in_=wgs)
         w1_sc_rest = reused.tile([P, PASSES, H - P], U8, name="w1_sc_rest", align_bytes=64, offset=4 * S)
-        nc.gpsimd.memset(w1_sc_rest[:].bitcast(I32), 0)
+        nc.scalar.copy(out=w1_sc_rest[:].bitcast(U32), in_=zero_word[:].bitcast(U32).to_broadcast([P, PASSES, (H - P) // 4]))
         load_w1_scales(w1_sc_rest, slice(P, H))
         for lo, hi in ((0, FIRST), (FIRST, S)):
             nc.vector.tensor_copy(v_w[1][:, lo:hi], tab_w[1][:].bitcast(U32).indirect(entries(idx, lo, hi)))

@@ -33,6 +33,7 @@ SCALE_ROW = 16
 SLOTS = 3
 FIRST = 256
 ROW_OFFSETS = {"row_slot0": 0, "bias": 4096, "across": 3712}
+AHEAD = 3
 STEADY = 4
 SPANS = [(0, PIECE), (PIECE, 2 * PIECE), (2 * PIECE, 3 * PIECE), (3 * PIECE, M - P), (M - P, M)]
 
@@ -231,10 +232,10 @@ def tile_list_fetal_slice_mosaic_kernel(
         def load_floors(c, count):
             rows = sbuf([P, count, M], F32, f"low{c}", f"row_slot{c % SLOTS}" if count == 1 else f"floor{c - 1}")
             nc.sync.dma_start(out=rows[:], in_=low[c * P : (c + count) * P, :].rearrange("(p i) m -> p i m", p=P))
+            floor[c] = sbuf([P, count, M], F32, f"floor{c}")
             for i in range(count):
-                floor[c + i] = sbuf([P, M], F32, f"floor{c + i}")
                 nc.scalar.activation(
-                    out=floor[c + i][:], in_=rows[:, i, :], func=IDENTITY, bias=neg_bias[:, c + i : c + i + 1]
+                    out=floor[c][:, i, :], in_=rows[:, i, :], func=IDENTITY, bias=neg_bias[:, c + i : c + i + 1]
                 )
 
         w2_codes = sbuf([P, PASSES, N], U32, "w2_codes")
@@ -261,9 +262,9 @@ def tile_list_fetal_slice_mosaic_kernel(
             nc.vector.tensor_copy(x, pages[c][:].indirect(entries(idx3, lo, hi)))
 
         def floored(z, x, c, lo, hi):
-            nc.vector.scalar_tensor_tensor(z, x, neg_bias[:, c : c + 1], floor[c][:, lo:hi], ALU.add, ALU.max)
+            nc.vector.scalar_tensor_tensor(z, x, neg_bias[:, c : c + 1], floor[c][:, 0, lo:hi], ALU.add, ALU.max)
 
-        spans = {0: [(0, BANK), (BANK, M)]}
+        spans = {0: [(0, BANK), (BANK, M - PIECE), (M - PIECE, M)]}
         z_t = {}
         for g in range(1):
             for lo, hi in spans[g]:
@@ -290,7 +291,7 @@ def tile_list_fetal_slice_mosaic_kernel(
         z_codes = {}
         z_sc = [sbuf([P, M], U8, f"z_sc{g}") for g in range(PASSES)]
 
-        def weave_and_quantise(g, lo, hi):
+        def weave_lower(g, lo, hi):
             woven = sbuf([P, (hi - lo) * PACK], BF16, f"woven{g}_{lo}")
             step = min(PIECE, hi - lo)
             blocks = step // P
@@ -304,10 +305,10 @@ def tile_list_fetal_slice_mosaic_kernel(
                     out=pairs.rearrange("p (b m u) -> p b m u", b=blocks, u=2),
                     in_=back[:].rearrange("p b u m -> p b m u"),
                 )
-            quantise(g, lo, hi, woven[:])
+            return woven
 
-        def quantise(g, lo, hi, woven):
-            z_codes[(g, lo)] = sbuf([P, hi - lo], U32, f"z_codes{g}_{lo}")
+        def quantise(g, lo, hi, woven, slot=None):
+            z_codes[(g, lo)] = sbuf([P, hi - lo], U32, f"z_codes{g}_{lo}", slot)
             nc.vector.quantize_mx(out=z_codes[(g, lo)][:].bitcast(FP8X4), scales=z_sc[g][:, lo:hi], in_=woven)
 
         out_view = out.rearrange("(j p) m -> p j m", p=P)
@@ -316,8 +317,8 @@ def tile_list_fetal_slice_mosaic_kernel(
 
         def product(span):
             lo, hi = SPANS[span]
-            half_start = lo // BANK * BANK
-            moving = [z_codes[(0, half_start)][:, lo - half_start : hi - half_start], z_codes[(1, lo)][:]]
+            at = max(first for first, end in spans[0] if first <= lo)
+            moving = [z_codes[(0, at)][:, lo - at : hi - at], z_codes[(1, lo)][:]]
             for pair in range(N // (2 * P)):
                 bank = 2 * (0, 1, 2, 1, 0)[span] + pair
                 if bank < 4:
@@ -368,8 +369,9 @@ def tile_list_fetal_slice_mosaic_kernel(
             turn(c - 1, 1, z, 0, M)
             load_wgs_dealt(c - 1, f"h{c}" if c < STEADY else None)
             if c == TILES_A_PASS:
-                for lo, hi in spans[0]:
-                    weave_and_quantise(0, lo, hi)
+                woven_lower = {lo: weave_lower(0, lo, hi) for lo, hi in spans[0]}
+                for lo, hi in spans[0][:-1]:
+                    quantise(0, lo, hi, woven_lower[lo][:])
         for c in range(STEADY + 2, ROW_TILES):
             load_page(c)
         for g in range(PASSES):
@@ -379,44 +381,62 @@ def tile_list_fetal_slice_mosaic_kernel(
         for c in range(STEADY + 1, ROW_TILES):
             scatter(c, 0, S, wgs_dealt[c - STEADY])
 
-        x = sbuf([P, late, PIECE], F32, "x_late", f"floor{STEADY - 1}")
-        for piece in range(M // PIECE):
+        picked = sbuf([P, PACK, PIECE], F32, "picked", f"floor{STEADY - 1}")
+        shifted = sbuf([P, 2, PACK, PIECE], F32, "shifted")
+        pieces = M // PIECE
+
+        def pick(piece, t, lo, hi):
+            cols = slice(lo - piece * PIECE, hi - piece * PIECE)
+            c = STEADY + t
+            gather(c, picked[:, t, cols], lo, hi)
+            nc.scalar.activation(
+                out=shifted[:, piece % 2, t, cols], in_=picked[:, t, cols], func=IDENTITY, bias=neg_bias[:, c : c + 1]
+            )
+
+        def floored_woven(span):
+            lo, hi = SPANS[span]
+            piece = lo // PIECE
+            woven = sbuf([P, hi - lo, PACK], BF16, f"woven1_{lo}")
+            nc.vector.tensor_tensor(
+                woven[:].rearrange("p (c i) t -> p c t i", i=PACK),
+                shifted[:, piece % 2, :, lo - piece * PIECE : hi - piece * PIECE].rearrange("p t (c i) -> p c t i", i=PACK),
+                floor[STEADY][:, :, lo:hi].rearrange("p t (c i) -> p c t i", i=PACK),
+                ALU.max,
+            )
+            return woven[:].rearrange("p m t -> p (m t)")
+
+        def finish(span):
+            lo, hi = SPANS[span]
+            quantise(1, lo, hi, floored_woven(span))
+            product(span)
+
+        def store_piece(span):
+            result = sbuf([P, 2, 2, PIECE], F32, f"result{span}", ("h5", "h6", "h7")[span])
+            for pair in range(2):
+                store(span, pair, nc.scalar.copy, result[:, pair, :, :])
+
+        for piece in range(pieces):
             lo, hi = piece * PIECE, (piece + 1) * PIECE
-            for i in range(late):
-                gather(STEADY + i, x[:, i, :], lo, hi)
-            mine = [s for s, (at, end) in enumerate(SPANS) if lo <= at and end <= hi]
-            woven = {}
-            planes = {}
-            for s in mine:
-                at, end = SPANS[s]
-                if s >= 2:
-                    z = ending.tile(
-                        [P, late, end - at], BF16, name=f"z_late{s}", align_bytes=64, offset=(3584, 4096, 5120)[s - 2]
-                    )
-                else:
-                    z = sbuf([P, late, end - at], BF16, f"z_late{s}")
-                for i in range(late):
-                    floored(z[:, i, :], x[:, i, at - lo : end - lo], STEADY + i, at, end)
-                planes[s] = z
-            for s in mine:
-                at, end = SPANS[s]
-                woven[s] = sbuf([P, end - at, PACK], BF16, f"woven1_{at}")
-                weave = nc.vector.tensor_copy if hi == M else nc.scalar.copy
-                weave(out=woven[s][:], in_=planes[s][:].rearrange("p t m -> p m t"))
+            for t in range(AHEAD):
+                pick(piece, t, lo, hi)
             if piece > 0:
-                if piece == 1:
-                    result = sbuf([P, 2, 2, PIECE], F32, "result0", "z_late1")
-                elif piece == 2:
-                    result = ending.tile([P, 2, 2, PIECE], F32, name="result1", align_bytes=64, offset=0)
-                else:
-                    result = sbuf([P, 2, 2, PIECE], F32, "result2", "h7")
-                for pair in range(2):
-                    store(piece - 1, pair, nc.scalar.copy, result[:, pair, :, :])
-            for s in mine:
-                quantise(1, *SPANS[s], woven[s][:].rearrange("p m t -> p (m t)"))
-            for s in mine:
-                product(s)
-        for s in mine:
+                finish(piece - 1)
+            if piece < pieces - 1:
+                pick(piece, AHEAD, lo, hi)
+            else:
+                pick(piece, AHEAD, lo, hi - P)
+                pick(piece, AHEAD, hi - P, hi)
+            if piece > 0:
+                store_piece(piece - 1)
+        lo, hi = spans[0][-1]
+        quantise(0, lo, hi, woven_lower[lo][:], "row_slot2")
+        last_spans = (pieces - 1, pieces)
+        woven = {s: floored_woven(s) for s in last_spans}
+        for s in last_spans:
+            quantise(1, *SPANS[s], woven[s])
+        for s in last_spans:
+            product(s)
+        for s in last_spans:
             for pair, engine_copy in enumerate((nc.scalar.copy, nc.vector.tensor_copy)):
-                result = sbuf([P, 2, P], F32, f"result{s}_{pair}", f"h{5 + pair}" if s == 3 else None)
+                result = sbuf([P, 2, P], F32, f"result{s}_{pair}")
                 store(s, pair, engine_copy, result[:])

@@ -131,7 +131,7 @@ def tile_list_fetal_slice_mosaic_kernel(
         w1_sc_rest = reused.tile([P, PASSES, H - P], U8, name="w1_sc_rest", align_bytes=64, offset=4 * S)
         nc.scalar.copy(out=w1_sc_rest[:].bitcast(U32), in_=zero_word[:].bitcast(U32).to_broadcast([P, PASSES, (H - P) // 4]))
         load_w1_scales(w1_sc_rest, slice(P, H))
-        for lo, hi in ((0, FIRST), (FIRST, S)):
+        for lo, hi in ((0, FIRST), (FIRST, FIRST + BANK), (FIRST + BANK, S)):
             nc.vector.tensor_copy(v_w[1][:, lo:hi], tab_w[1][:].bitcast(U32).indirect(entries(idx, lo, hi)))
         w1_rest = sbuf([P, PASSES, 2 * (H - P)], U8, "w1_rest", "weights_slot")
         nc.sync.dma_start(out=w1_rest[:].bitcast(I32), in_=w1_view[:, :, 2 * P :].bitcast(I32))
@@ -405,11 +405,6 @@ def tile_list_fetal_slice_mosaic_kernel(
             )
             return woven[:].rearrange("p m t -> p (m t)")
 
-        def finish(span):
-            lo, hi = SPANS[span]
-            quantise(1, lo, hi, floored_woven(span))
-            product(span)
-
         def store_piece(span):
             result = sbuf([P, 2, 2, PIECE], F32, f"result{span}", ("h5", "h6", "h7")[span])
             for pair in range(2):
@@ -420,13 +415,15 @@ def tile_list_fetal_slice_mosaic_kernel(
             for t in range(AHEAD):
                 pick(piece, t, lo, hi)
             if piece > 0:
-                finish(piece - 1)
+                woven = floored_woven(piece - 1)
             if piece < pieces - 1:
                 pick(piece, AHEAD, lo, hi)
             else:
                 pick(piece, AHEAD, lo, hi - P)
                 pick(piece, AHEAD, hi - P, hi)
             if piece > 0:
+                quantise(1, *SPANS[piece - 1], woven)
+                product(piece - 1)
                 store_piece(piece - 1)
         lo, hi = spans[0][-1]
         quantise(0, lo, hi, woven_lower[lo][:], "row_slot2")

@@ -32,6 +32,7 @@ HALF = P // 2
 SCALE_ROW = 16
 SLOTS = 3
 FIRST = 256
+FIRST_PARTS = [(0, FIRST), (FIRST, BANK), (BANK, S)]
 ROW_OFFSETS = {"row_slot0": 0, "bias": 4096, "across": 3712}
 AHEAD = 3
 STEADY = 4
@@ -116,14 +117,19 @@ def tile_list_fetal_slice_mosaic_kernel(
 
         picked_sc = sbuf([P, S], U8, "picked_sc", "weights_slot")
         nc.vector.tensor_copy(picked_sc[:], tab_sc[:].indirect(idx[:]))
-        for a in range(PASSES):
-            for h in range(2):
-                first = SCALE_ROW + PACK * (2 * a + h)
-                nc.sync.dma_start(
-                    out=v_sc_both[HALF * h : HALF * (h + 1), a, :].bitcast(I32),
-                    in_=picked_sc[first : first + HALF, :].bitcast(I32),
-                )
+
+        def move_scale_rows(lo, hi):
+            for a in range(PASSES):
+                for h in range(2):
+                    first = SCALE_ROW + PACK * (2 * a + h)
+                    nc.sync.dma_start(
+                        out=v_sc_both[HALF * h : HALF * (h + 1), a, lo:hi].bitcast(I32),
+                        in_=picked_sc[first : first + HALF, lo:hi].bitcast(I32),
+                    )
+
+        move_scale_rows(0, FIRST)
         load_page(0)
+        move_scale_rows(FIRST, S)
         v_w = [sbuf([P, S], U32, "v_w0"), sbuf([P, S], U32, "v_w1")]
         nc.vector.tensor_copy(v_w[0][:], tab_w[0][:].bitcast(U32).indirect(idx[:]))
         wgs_sb = reused.tile([P, S], F32, name="wgs_sb", align_bytes=64, offset=0)
@@ -131,7 +137,7 @@ def tile_list_fetal_slice_mosaic_kernel(
         w1_sc_rest = reused.tile([P, PASSES, H - P], U8, name="w1_sc_rest", align_bytes=64, offset=4 * S)
         nc.scalar.copy(out=w1_sc_rest[:].bitcast(U32), in_=zero_word[:].bitcast(U32).to_broadcast([P, PASSES, (H - P) // 4]))
         load_w1_scales(w1_sc_rest, slice(P, H))
-        for lo, hi in ((0, FIRST), (FIRST, FIRST + BANK), (FIRST + BANK, S)):
+        for lo, hi in FIRST_PARTS:
             nc.vector.tensor_copy(v_w[1][:, lo:hi], tab_w[1][:].bitcast(U32).indirect(entries(idx, lo, hi)))
         w1_rest = sbuf([P, PASSES, 2 * (H - P)], U8, "w1_rest", "weights_slot")
         nc.sync.dma_start(out=w1_rest[:].bitcast(I32), in_=w1_view[:, :, 2 * P :].bitcast(I32))
@@ -148,7 +154,7 @@ def tile_list_fetal_slice_mosaic_kernel(
         def first_product(c):
             h_sb[c] = sbuf([P, S], F32, f"h{c}", "row_slot1" if c == 0 else None)
             if c == 0:
-                parts = [(0, FIRST, P), (FIRST, FIRST + BANK, BANK), (FIRST + BANK, S, P)]
+                parts = [(lo, hi, P if lo == 0 else hi - lo) for lo, hi in FIRST_PARTS]
             else:
                 parts = [(0, BANK, BANK), (BANK, S, BANK)]
             for lo, hi, width in parts:
@@ -344,8 +350,8 @@ def tile_list_fetal_slice_mosaic_kernel(
             engine_copy(out=result, in_=sums[(span, pair)][:])
             nc.sync.dma_start(out=out_view[:, 2 * pair : 2 * pair + 2, lo:hi], in_=result)
 
-        scatter(0, 0, FIRST, wgs_first)
-        scatter(0, FIRST, S, wgs_sb)
+        for lo, hi in FIRST_PARTS:
+            scatter(0, lo, hi, wgs_first if lo == 0 else wgs_sb)
         x = sbuf([P, M], F32, "x0", "row_slot2")
         gather(0, x[:], 0, M)
         for c in range(1, STEADY + 1):

@@ -78,8 +78,10 @@ def tile_list_fetal_slice_mosaic_kernel(
         nc.vector.memset(tab_sc[HALF:P, :].bitcast(I32), 0)
         zero_word = sbuf([P, 1, 1], I32, "zero_word")
         nc.vector.memset(zero_word[:], 0)
-        v_sc_both = sbuf([P, PASSES, S], U8, "v_sc")
-        v_sc = [v_sc_both[:, a, :] for a in range(PASSES)]
+        v_sc_half = [sbuf([P, PASSES, BANK], U8, "v_sc0")]
+
+        def v_scale(a, lo, hi):
+            return v_sc_half[lo // BANK][:, a, lo % BANK : lo % BANK + hi - lo]
 
         def load_w1_scales(planes, cols):
             for quad in range(QUADRANTS):
@@ -123,17 +125,21 @@ def tile_list_fetal_slice_mosaic_kernel(
                 for h in range(2):
                     first = SCALE_ROW + PACK * (2 * a + h)
                     nc.sync.dma_start(
-                        out=v_sc_both[HALF * h : HALF * (h + 1), a, lo:hi].bitcast(I32),
+                        out=v_scale(a, lo, hi)[HALF * h : HALF * (h + 1), :].bitcast(I32),
                         in_=picked_sc[first : first + HALF, lo:hi].bitcast(I32),
                     )
 
         move_scale_rows(0, FIRST)
         load_page(0)
-        move_scale_rows(FIRST, S)
+        move_scale_rows(FIRST, BANK)
         v_w = [sbuf([P, S], U32, "v_w0"), sbuf([P, S], U32, "v_w1")]
         nc.vector.tensor_copy(v_w[0][:], tab_w[0][:].bitcast(U32).indirect(idx[:]))
         wgs_sb = reused.tile([P, S], F32, name="wgs_sb", align_bytes=64, offset=0)
-        nc.sync.dma_start(out=wgs_sb[:], in_=wgs)
+        nc.sync.dma_start(out=wgs_sb[:, FIRST:BANK], in_=wgs[:, FIRST:BANK])
+        v_sc_half.append(reused.tile([P, PASSES, BANK], U8, name="v_sc1", align_bytes=64, offset=6 * S))
+        move_scale_rows(BANK, S)
+        nc.sync.dma_start(out=wgs_sb[:, BANK:S], in_=wgs[:, BANK:S])
+        nc.sync.dma_start(out=wgs_sb[:, 0:FIRST], in_=wgs[:, 0:FIRST])
         w1_sc_rest = reused.tile([P, PASSES, H - P], U8, name="w1_sc_rest", align_bytes=64, offset=4 * S)
         nc.scalar.copy(out=w1_sc_rest[:].bitcast(U32), in_=zero_word[:].bitcast(U32).to_broadcast([P, PASSES, (H - P) // 4]))
         load_w1_scales(w1_sc_rest, slice(P, H))
@@ -171,7 +177,7 @@ def tile_list_fetal_slice_mosaic_kernel(
                             lhsT=w1_codes.bitcast(FP4X4),
                             lhsT_scale=w1_scale,
                             rhs=v_w[a][:, at : at + width].bitcast(FP8X4),
-                            rhs_scale=v_sc[a][:, at : at + width],
+                            rhs_scale=v_scale(a, at, at + width),
                             start=(a == 0),
                             stop=(a == PASSES - 1),
                         )
@@ -202,7 +208,7 @@ def tile_list_fetal_slice_mosaic_kernel(
                     nc.tensor.matmul_mx(
                         out=h_sum[:],
                         lhsT=v_w[a][:, cols].bitcast(FP8X4),
-                        lhsT_scale=v_sc[a][:, cols],
+                        lhsT_scale=v_scale(a, cols.start, cols.stop),
                         rhs=w1_rest[:, a, 2 * (upper - P) :].bitcast(FP4X4),
                         rhs_scale=w1_sc_rest[:, a, upper - P :],
                         start=(a == 0),

@@ -34,7 +34,7 @@ SLOTS = 3
 FIRST = 256
 FIRST_PARTS = [(0, FIRST), (FIRST, BANK), (BANK, S)]
 ROW_OFFSETS = {"row_slot0": 0, "bias": 4096, "across": 3712}
-AHEAD = 3
+AHEAD = 1
 STEADY = 4
 SPANS = [(0, PIECE), (PIECE, 2 * PIECE), (2 * PIECE, 3 * PIECE), (3 * PIECE, M - P), (M - P, M)]
 
@@ -393,16 +393,18 @@ def tile_list_fetal_slice_mosaic_kernel(
         for c in range(STEADY + 1, ROW_TILES):
             scatter(c, 0, S, wgs_dealt[c - STEADY])
 
-        picked = sbuf([P, PACK, PIECE], F32, "picked", f"floor{STEADY - 1}")
-        shifted = sbuf([P, 2, PACK, PIECE], F32, "shifted")
+        bias_wide = sbuf([P, PACK, PIECE], F32, "bias_wide")
+        nc.scalar.copy(out=bias_wide[:], in_=bias_sb[:, 1, 0:PACK].unsqueeze(2).to_broadcast([P, PACK, PIECE]))
+        shifted = sbuf([P, 2, PACK, PIECE], F32, "shifted", f"floor{STEADY - 1}")
         pieces = M // PIECE
 
         def pick(piece, t, lo, hi):
             cols = slice(lo - piece * PIECE, hi - piece * PIECE)
-            c = STEADY + t
-            gather(c, picked[:, t, cols], lo, hi)
-            nc.scalar.activation(
-                out=shifted[:, piece % 2, t, cols], in_=picked[:, t, cols], func=IDENTITY, bias=neg_bias[:, c : c + 1]
+            nc.vector.tensor_tensor(
+                shifted[:, piece % 2, t, cols],
+                pages[STEADY + t][:].indirect(entries(idx3, lo, hi)),
+                bias_wide[:, t, cols],
+                ALU.subtract,
             )
 
         def floored_woven(span):
@@ -428,15 +430,12 @@ def tile_list_fetal_slice_mosaic_kernel(
                 pick(piece, t, lo, hi)
             if piece > 0:
                 woven = floored_woven(piece - 1)
-            if piece < pieces - 1:
-                pick(piece, AHEAD, lo, hi)
-            else:
-                pick(piece, AHEAD, lo, hi - P)
-                pick(piece, AHEAD, hi - P, hi)
-            if piece > 0:
-                quantise(1, *SPANS[piece - 1], woven)
-                product(piece - 1)
-                store_piece(piece - 1)
+            for t in range(AHEAD, PACK):
+                pick(piece, t, lo, hi)
+                if piece > 0 and t == AHEAD:
+                    quantise(1, *SPANS[piece - 1], woven)
+                    product(piece - 1)
+                    store_piece(piece - 1)
         lo, hi = spans[0][-1]
         quantise(0, lo, hi, woven_lower[lo][:], "row_slot2")
         last_spans = (pieces - 1, pieces)

@@ -271,10 +271,18 @@ def tile_list_fetal_slice_mosaic_kernel(
             )
 
         def gather(c, x, lo, hi):
-            nc.vector.tensor_copy(x, pages[c][:].indirect(entries(idx3, lo, hi)))
+            if c == 0:
+                nc.vector.tensor_copy(x, pages[c][:].indirect(entries(idx3, lo, hi)))
+                return
+            bias_row = sbuf([P, M], F32, f"bias_row{c}", f"bias_row{c % 2}")
+            nc.scalar.copy(out=bias_row[:], in_=bias_sb[:, 0, c : c + 1].to_broadcast([P, M]))
+            nc.vector.tensor_tensor(x, pages[c][:].indirect(entries(idx3, lo, hi)), bias_row[:], ALU.subtract)
 
         def floored(z, x, c, lo, hi):
-            nc.vector.scalar_tensor_tensor(z, x, neg_bias[:, c : c + 1], floor[c][:, 0, lo:hi], ALU.add, ALU.max)
+            if c == 0:
+                nc.vector.scalar_tensor_tensor(z, x, neg_bias[:, 0:1], floor[0][:, 0, lo:hi], ALU.add, ALU.max)
+                return
+            nc.vector.tensor_tensor(z, x, floor[c][:, 0, lo:hi], ALU.max)
 
         spans = {0: [(0, BANK), (BANK, M - PIECE), (M - PIECE, M)]}
         z_t = {}
@@ -437,7 +445,7 @@ def tile_list_fetal_slice_mosaic_kernel(
                     product(piece - 1)
                     store_piece(piece - 1)
         lo, hi = spans[0][-1]
-        quantise(0, lo, hi, woven_lower[lo][:], "row_slot2")
+        quantise(0, lo, hi, woven_lower[lo][:], "page_slot0")
         last_spans = (pieces - 1, pieces)
         woven = {s: floored_woven(s) for s in last_spans}
         for s in last_spans:

@@ -36,7 +36,8 @@ FIRST_PARTS = [(0, FIRST), (FIRST, BANK), (BANK, S)]
 ROW_OFFSETS = {"row_slot0": 0, "bias": 4096, "across": 3712}
 AHEAD = 1
 STEADY = 4
-SPANS = [(0, PIECE), (PIECE, 2 * PIECE), (2 * PIECE, 3 * PIECE), (3 * PIECE, M - P), (M - P, M)]
+PIECES = [(0, BANK), (BANK, M - PIECE), (M - PIECE, M)]
+SPANS = [(0, BANK), (BANK, M - PIECE), (M - PIECE, M - P), (M - P, M)]
 
 
 def tile_list_fetal_slice_mosaic_kernel(
@@ -335,34 +336,40 @@ def tile_list_fetal_slice_mosaic_kernel(
 
         sums = {}
 
+        def groups(span):
+            lo, hi = SPANS[span]
+            size = 1 if hi - lo == BANK else 2
+            return [range(j, j + size) for j in range(0, N // P, size)]
+
         def product(span):
             lo, hi = SPANS[span]
             at = max(first for first, end in spans[0] if first <= lo)
             moving = [z_codes[(0, at)][:, lo - at : hi - at], z_codes[(1, lo)][:]]
-            for pair in range(N // (2 * P)):
-                bank = 2 * (0, 1, 2, 1, 0)[span] + pair
-                if bank < 4:
-                    out_sum = banks.tile([P, 2, hi - lo], F32, name="out_sum", tag=f"bank{bank}")
+            for number, group in enumerate(groups(span)):
+                if span in (1, 2):
+                    out_sum = turns.tile([P, len(group), hi - lo], F32, name="out_sum", tag=("turned", "back")[span - 1])
                 else:
-                    out_sum = turns.tile([P, 2, hi - lo], F32, name="out_sum", tag="turned")
+                    out_sum = banks.tile([P, len(group), hi - lo], F32, name="out_sum", tag=f"bank{number}")
                 for g in range(PASSES):
-                    for j in range(2):
-                        n_cols = slice((2 * pair + j) * P, (2 * pair + j + 1) * P)
+                    for j in group:
+                        n_cols = slice(j * P, (j + 1) * P)
                         nc.tensor.matmul_mx(
-                            out=out_sum[:, j, :],
+                            out=out_sum[:, j - group[0], :],
                             lhsT=w2_codes[:, g, n_cols].bitcast(FP8X4),
                             lhsT_scale=w2_sc[:, g, n_cols],
                             rhs=moving[g].bitcast(FP8X4),
                             rhs_scale=z_sc[g][:, lo:hi],
-                            start=(g == 0 and j == 0),
-                            stop=(g == PASSES - 1 and j == 1),
+                            start=(g == 0 and j == group[0]),
+                            stop=(g == PASSES - 1 and j == group[-1]),
                         )
-                sums[(span, pair)] = out_sum
+                sums[(span, number)] = out_sum
 
-        def store(span, pair, engine_copy, result):
+        def store(span, engine_copies):
             lo, hi = SPANS[span]
-            engine_copy(out=result, in_=sums[(span, pair)][:])
-            nc.sync.dma_start(out=out_view[:, 2 * pair : 2 * pair + 2, lo:hi], in_=result)
+            for number, group in enumerate(groups(span)):
+                result = sbuf([P, len(group), hi - lo], F32, f"result{span}_{number}", (f"z{number}", f"h{5 + number}", None, None)[span])
+                engine_copies[number % 2](out=result[:], in_=sums[(span, number)][:])
+                nc.sync.dma_start(out=out_view[:, group[0] : group[-1] + 1, lo:hi], in_=result[:])
 
         for lo, hi in FIRST_PARTS:
             scatter(0, lo, hi, wgs_first if lo == 0 else wgs_sb)
@@ -401,58 +408,48 @@ def tile_list_fetal_slice_mosaic_kernel(
         for c in range(STEADY + 1, ROW_TILES):
             scatter(c, 0, S, wgs_dealt[c - STEADY])
 
-        bias_wide = sbuf([P, PACK, PIECE], F32, "bias_wide")
-        nc.scalar.copy(out=bias_wide[:], in_=bias_sb[:, 1, 0:PACK].unsqueeze(2).to_broadcast([P, PACK, PIECE]))
-        shifted = sbuf([P, 2, PACK, PIECE], F32, "shifted", f"floor{STEADY - 1}")
-        pieces = M // PIECE
+        bias_wide = sbuf([P, PACK, BANK], F32, "bias_wide")
+        nc.scalar.copy(out=bias_wide[:], in_=bias_sb[:, 1, 0:PACK].unsqueeze(2).to_broadcast([P, PACK, BANK]))
+        shifted = sbuf([P, PACK, M], F32, "shifted", f"floor{STEADY - 1}")
 
-        def pick(piece, t, lo, hi):
-            cols = slice(lo - piece * PIECE, hi - piece * PIECE)
+        def pick(piece, t):
+            lo, hi = PIECES[piece]
             nc.vector.tensor_tensor(
-                shifted[:, piece % 2, t, cols],
+                shifted[:, t, lo:hi],
                 pages[STEADY + t][:].indirect(entries(idx3, lo, hi)),
-                bias_wide[:, t, cols],
+                bias_wide[:, t, 0 : hi - lo],
                 ALU.subtract,
             )
 
         def floored_woven(span):
             lo, hi = SPANS[span]
-            piece = lo // PIECE
             woven = sbuf([P, hi - lo, PACK], BF16, f"woven1_{lo}")
             nc.vector.tensor_tensor(
                 woven[:].rearrange("p (c i) t -> p c t i", i=PACK),
-                shifted[:, piece % 2, :, lo - piece * PIECE : hi - piece * PIECE].rearrange("p t (c i) -> p c t i", i=PACK),
+                shifted[:, :, lo:hi].rearrange("p t (c i) -> p c t i", i=PACK),
                 floor[STEADY][:, :, lo:hi].rearrange("p t (c i) -> p c t i", i=PACK),
                 ALU.max,
             )
             return woven[:].rearrange("p m t -> p (m t)")
 
-        def store_piece(span):
-            result = sbuf([P, 2, 2, PIECE], F32, f"result{span}", ("h5", "h6", "h7")[span])
-            for pair in range(2):
-                store(span, pair, nc.scalar.copy, result[:, pair, :, :])
-
-        for piece in range(pieces):
-            lo, hi = piece * PIECE, (piece + 1) * PIECE
-            for t in range(AHEAD):
-                pick(piece, t, lo, hi)
+        for piece in range(len(PIECES)):
+            pick(piece, 0)
             if piece > 0:
                 woven = floored_woven(piece - 1)
-            for t in range(AHEAD, PACK):
-                pick(piece, t, lo, hi)
-                if piece > 0 and t == AHEAD:
-                    quantise(1, *SPANS[piece - 1], woven)
-                    product(piece - 1)
-                    store_piece(piece - 1)
+            pick(piece, 1)
+            if piece > 0:
+                quantise(1, *SPANS[piece - 1], woven)
+                product(piece - 1)
+                store(piece - 1, (nc.scalar.copy, nc.scalar.copy))
+            pick(piece, 2)
+            pick(piece, 3)
         lo, hi = spans[0][-1]
         quantise(0, lo, hi, woven_lower[lo][:], "page_slot0")
-        last_spans = (pieces - 1, pieces)
+        last_spans = (len(SPANS) - 2, len(SPANS) - 1)
         woven = {s: floored_woven(s) for s in last_spans}
         for s in last_spans:
             quantise(1, *SPANS[s], woven[s])
         for s in last_spans:
             product(s)
         for s in last_spans:
-            for pair, engine_copy in enumerate((nc.scalar.copy, nc.vector.tensor_copy)):
-                result = sbuf([P, 2, P], F32, f"result{s}_{pair}")
-                store(s, pair, engine_copy, result[:])
+            store(s, (nc.scalar.copy, nc.vector.tensor_copy))

@@ -16,28 +16,42 @@ FP8X4 = mybir.dt.float8_e4m3fn_x4
 FP4X4 = mybir.dt.float4_e2m1fn_x4
 ALU = mybir.AluOpType
 IDENTITY = mybir.ActivationFunctionType.Identity
+COPY = mybir.ActivationFunctionType.Copy
+SIGN = mybir.ActivationFunctionType.Sign
 
 P = 128
 PACK = 4
+RUN = 2
 QUADRANT = 32
 QUADRANTS = P // QUADRANT
 PER_COLUMN = 16
 BANK = 512
 PASSES = 2
 ROW_TILES = H // P
-TILES_A_PASS = ROW_TILES // PASSES
-LAST = ROW_TILES - 1
+LOWER = ROW_TILES // PASSES
+UPPER_ROW = LOWER * P
 PIECE = 256
 HALF = P // 2
 SCALE_ROW = 16
-SLOTS = 3
-FIRST = 256
-FIRST_PARTS = [(0, FIRST), (FIRST, BANK), (BANK, S)]
-ROW_OFFSETS = {"row_slot0": 0, "bias": 4096, "across": 3712}
-AHEAD = 1
-STEADY = 4
+FIRST = BANK
+FIRST_PARTS = [(0, FIRST), (FIRST, S)]
+HEAD_TILES = 2
 PIECES = [(0, BANK), (BANK, M - PIECE), (M - PIECE, M)]
 SPANS = [(0, BANK), (BANK, M - PIECE), (M - PIECE, M - P), (M - P, M)]
+
+ROW = 4 * M
+EDGE = 64
+REGIONS = [
+    ("dealt0", ROW), ("page1", 2 * ROW), ("keep1", ROW), ("page2", 2 * ROW), ("wgs", ROW + EDGE), ("page3", 2 * ROW), ("keep2", ROW),
+    ("page5", 2 * ROW), ("keep0", ROW), ("page4", 2 * ROW),
+    ("spare", ROW), ("drop0", ROW), ("dealt1", ROW), ("dealt2", ROW),
+    ("floors", 4 * ROW), ("page0", 2 * ROW), ("h1", ROW), ("h0", ROW),
+    ("x3", ROW), ("drop1", ROW), ("low3", ROW),
+    ("x1", ROW), ("bias", 4 * EDGE), ("low0", ROW), ("x2", ROW), ("w2_codes", ROW), ("raw4", ROW), ("last", 2 * ROW),
+    ("h4", ROW), ("h5", ROW), ("h6", ROW), ("z_t0", ROW), ("h7", ROW), ("h2", ROW), ("z_t1", ROW),
+    ("gap0", ROW), ("gap1", ROW), ("h3", ROW), ("w2_bf", 2 * ROW),
+]
+START = {name: sum(size for other, size in REGIONS[:i]) for i, (name, size) in enumerate(REGIONS)}
 
 
 def tile_list_fetal_slice_mosaic_kernel(
@@ -47,16 +61,17 @@ def tile_list_fetal_slice_mosaic_kernel(
     with ExitStack() as ctx:
         lists = ctx.enter_context(tc.tile_pool(name="lists", bufs=1))
         keep = ctx.enter_context(tc.tile_pool(name="keep", bufs=1))
-        ending = ctx.enter_context(tc.tile_pool(name="ending", bufs=1))
-        reused = ctx.enter_context(tc.tile_pool(name="reused", bufs=1))
-        rows_pool = ctx.enter_context(tc.tile_pool(name="rows_pool", bufs=1))
+        placed = ctx.enter_context(tc.tile_pool(name="placed", bufs=1))
         banks = ctx.enter_context(tc.psum_pool(name="banks", bufs=1))
-        turns = ctx.enter_context(tc.psum_pool(name="turns", bufs=2))
 
-        def sbuf(shape, dtype, name, tag=None):
-            if tag in ROW_OFFSETS:
-                return rows_pool.tile(shape, dtype, name=name, align_bytes=64, offset=ROW_OFFSETS[tag])
-            return keep.tile(shape, dtype, name=name, tag=tag or name, align_bytes=64)
+        def own(shape, dtype, name):
+            return keep.tile(shape, dtype, name=name, align_bytes=64)
+
+        def place(shape, dtype, name, region, shift=0):
+            return placed.tile(shape, dtype, name=name, align_bytes=64, offset=START[region] + shift)
+
+        def bank(shape, tag):
+            return banks.tile(shape, F32, name=tag, tag=tag)
 
         idx = lists.tile([P, S // PER_COLUMN], U16, name="idx")
         idx2 = lists.tile([P, S // PER_COLUMN], U16, name="idx2")
@@ -65,10 +80,11 @@ def tile_list_fetal_slice_mosaic_kernel(
         def entries(listed, lo, hi):
             return listed[:, lo // PER_COLUMN : hi // PER_COLUMN]
 
-        w1_sc_first = sbuf([P, PASSES, P], U8, "w1_sc_first")
+        head = HEAD_TILES * P
+        w1_sc_first = place([P, PASSES, head], U8, "w1_sc_first", "bias")
         nc.vector.memset(w1_sc_first[:].bitcast(I32), 0)
         nc.sync.dma_start(idx[:], offs)
-        tab_sc = sbuf([P, T], U8, "tab_sc", "page_slot0")
+        tab_sc = place([P, T], U8, "tab_sc", "page0")
         rows_by_parity = tab_scales.rearrange("a (h o r) c -> o (a h) r c", o=2, r=PACK)
         for o in range(2):
             base = QUADRANT * o
@@ -77,12 +93,12 @@ def tile_list_fetal_slice_mosaic_kernel(
             )
             nc.vector.memset(tab_sc[base : base + SCALE_ROW, :].bitcast(I32), 0)
         nc.vector.memset(tab_sc[HALF:P, :].bitcast(I32), 0)
-        zero_word = sbuf([P, 1, 1], I32, "zero_word")
+        zero_word = own([P, 1, 1], I32, "zero_word")
         nc.vector.memset(zero_word[:], 0)
-        v_sc_half = [sbuf([P, PASSES, BANK], U8, "v_sc0")]
+        v_sc = own([P, PASSES, S], U8, "v_sc")
 
         def v_scale(a, lo, hi):
-            return v_sc_half[lo // BANK][:, a, lo % BANK : lo % BANK + hi - lo]
+            return v_sc[:, a, lo:hi]
 
         def load_w1_scales(planes, cols):
             for quad in range(QUADRANTS):
@@ -92,7 +108,7 @@ def tile_list_fetal_slice_mosaic_kernel(
                     in_=rows.rearrange("a r c -> r a c").bitcast(I32),
                 )
 
-        tab_w = [reused.tile([P, T], I32, name="tab_w0", align_bytes=64, offset=0), sbuf([P, T], I32, "tab_w1", "page_slot1")]
+        tab_w = [place([P, T], I32, "tab_w0", "page2", 2 * EDGE), place([P, T], I32, "tab_w1", "keep0", -ROW // 2)]
 
         def load_words(a):
             nc.sync.dma_start(out=tab_w[a][:], in_=tab_words[a].rearrange("p t i -> p (t i)").bitcast(I32))
@@ -100,25 +116,33 @@ def tile_list_fetal_slice_mosaic_kernel(
         nc.sync.dma_start(idx2[:], offs2)
         nc.sync.dma_start(idx3[:], offs3)
         w1_view = w1_words.rearrange("a p c -> p a c")
-        w1_first = sbuf([P, PASSES, 2 * P], U8, "w1_first", "across")
-        nc.sync.dma_start(out=w1_first[:].bitcast(I32), in_=w1_view[:, :, 0 : 2 * P].bitcast(I32))
-        wgs_first = sbuf([P, FIRST], F32, "wgs_first", "page_slot2")
+        w1_first = place([P, PASSES, 2 * head], U8, "w1_first", "dealt2", -2 * head)
+        nc.sync.dma_start(out=w1_first[:].bitcast(I32), in_=w1_view[:, :, 0 : 2 * head].bitcast(I32))
+        wgs_first = place([P, FIRST], F32, "wgs_first", "page1", -2 * FIRST)
         nc.sync.dma_start(out=wgs_first[:], in_=wgs[:, 0:FIRST])
         load_words(0)
-        load_w1_scales(w1_sc_first, slice(0, P))
+        load_w1_scales(w1_sc_first, slice(0, head))
         load_words(1)
+
+        def dealt_rows(rows, t):
+            return rows.rearrange("(a t e) c -> t a e c", t=PACK, e=RUN)[t]
+
+        def load_planes(planes, rows):
+            for e in range(RUN):
+                nc.sync.dma_start(out=planes[e:P:RUN, :, :], in_=rows.rearrange("(a t e) c -> e a t c", t=PACK, e=RUN)[e])
+
         pages = {}
+        page_place = {
+            0: ("page0", 0), 1: ("page1", 0), 2: ("page2", 2 * EDGE), 3: ("page3", -EDGE), 4: ("page4", -EDGE),
+            5: ("page5", EDGE), 6: ("page1", EDGE), 7: ("page2", -EDGE),
+        }
 
         def load_page(c):
-            pages[c] = sbuf([P, T2], F32, f"page{c}", f"page_slot{c % SLOTS}" if c < LAST else "row_slot2")
-            if c < STEADY:
-                rows = page0[c * P : (c + 1) * P, :]
-            else:
-                rows = page0[STEADY * P :, :].rearrange("(p t) c -> t p c", t=PACK)[c - STEADY]
+            pages[c] = place([P, T2], F32, f"page{c}", *page_place[c])
+            rows = page0[c * P : (c + 1) * P, :] if c < LOWER else dealt_rows(page0[UPPER_ROW:, :], c - LOWER)
             nc.sync.dma_start(out=pages[c][:], in_=rows)
 
-
-        picked_sc = sbuf([P, S], U8, "picked_sc", "weights_slot")
+        picked_sc = place([P, S], U8, "picked_sc", "drop0", -S // 2)
         nc.vector.tensor_copy(picked_sc[:], tab_sc[:].indirect(idx[:]))
 
         def move_scale_rows(lo, hi):
@@ -130,49 +154,70 @@ def tile_list_fetal_slice_mosaic_kernel(
                         in_=picked_sc[first : first + HALF, lo:hi].bitcast(I32),
                     )
 
-        move_scale_rows(0, FIRST)
+        move_scale_rows(0, S)
         load_page(0)
-        move_scale_rows(FIRST, BANK)
-        v_w = [sbuf([P, S], U32, "v_w0"), sbuf([P, S], U32, "v_w1")]
+        v_w = [place([P, S], U32, "v_w0", "x1"), place([P, S], U32, "v_w1", "x2")]
         nc.vector.tensor_copy(v_w[0][:], tab_w[0][:].bitcast(U32).indirect(idx[:]))
-        wgs_sb = reused.tile([P, S], F32, name="wgs_sb", align_bytes=64, offset=0)
-        nc.sync.dma_start(out=wgs_sb[:, FIRST:BANK], in_=wgs[:, FIRST:BANK])
-        v_sc_half.append(reused.tile([P, PASSES, BANK], U8, name="v_sc1", align_bytes=64, offset=6 * S))
-        move_scale_rows(BANK, S)
-        nc.sync.dma_start(out=wgs_sb[:, BANK:S], in_=wgs[:, BANK:S])
+        wgs_sb = place([P, S], F32, "wgs_sb", "wgs", EDGE)
+        nc.sync.dma_start(out=wgs_sb[:, FIRST:S], in_=wgs[:, FIRST:S])
         nc.sync.dma_start(out=wgs_sb[:, 0:FIRST], in_=wgs[:, 0:FIRST])
-        w1_sc_rest = reused.tile([P, PASSES, H - P], U8, name="w1_sc_rest", align_bytes=64, offset=4 * S)
-        nc.scalar.copy(out=w1_sc_rest[:].bitcast(U32), in_=zero_word[:].bitcast(U32).to_broadcast([P, PASSES, (H - P) // 4]))
-        load_w1_scales(w1_sc_rest, slice(P, H))
+        rest = H - head
+        w1_sc_rest = place([P, PASSES, rest], U8, "w1_sc_rest", "drop0", -PASSES * rest)
+        nc.scalar.copy(out=w1_sc_rest[:].bitcast(U32), in_=zero_word[:].bitcast(U32).to_broadcast([P, PASSES, rest // 4]))
+        load_w1_scales(w1_sc_rest, slice(head, H))
         for lo, hi in FIRST_PARTS:
             nc.vector.tensor_copy(v_w[1][:, lo:hi], tab_w[1][:].bitcast(U32).indirect(entries(idx, lo, hi)))
-        w1_rest = sbuf([P, PASSES, 2 * (H - P)], U8, "w1_rest", "weights_slot")
-        nc.sync.dma_start(out=w1_rest[:].bitcast(I32), in_=w1_view[:, :, 2 * P :].bitcast(I32))
+        w1_rest = place([P, PASSES, 2 * rest], U8, "w1_rest", "drop0")
+        nc.sync.dma_start(out=w1_rest[:].bitcast(I32), in_=w1_view[:, :, 2 * head :].bitcast(I32))
         load_page(1)
 
-        h_sb = {}
+        wgs_dealt = {}
+        dealt_place = [("dealt0", 0), ("dealt1", 0), ("dealt2", 0), ("dealt0", 0)]
 
+        def load_wgs_dealt(t):
+            wgs_dealt[t] = place([P, S], F32, f"wgs_dealt{t}", *dealt_place[t])
+            for quad in range(QUADRANTS):
+                nc.sync.dma_start(out=wgs_dealt[t][QUADRANT * quad : QUADRANT * (quad + 1), 0:S], in_=dealt_rows(wgs, t))
+
+        load_wgs_dealt(0)
+
+        w1_dealt = place([P, PASSES, PACK, 2 * P], U8, "w1_dealt", "w2_codes")
+        w1_sc_dealt = place([P, PASSES, PACK, P], U8, "w1_sc_dealt", "w2_codes", PASSES * PACK * 2 * P)
+
+        def deal_w1():
+            upper = UPPER_ROW - head
+            nc.scalar.copy(
+                out=w1_dealt[:].bitcast(U32),
+                in_=w1_rest[:, :, 2 * upper :].bitcast(U32).rearrange("p g (a t) -> p g t a", t=PACK),
+            )
+            nc.scalar.copy(
+                out=w1_sc_dealt[:].bitcast(U16),
+                in_=w1_sc_rest[:, :, upper:].bitcast(U16).rearrange("p g (a t) -> p g t a", t=PACK),
+            )
+
+        def w1_tile(c, a):
+            if c < HEAD_TILES:
+                return w1_first[:, a, 2 * P * c : 2 * P * (c + 1)], w1_sc_first[:, a, P * c : P * (c + 1)]
+            if c < LOWER:
+                i = c - HEAD_TILES
+                return w1_rest[:, a, 2 * P * i : 2 * P * (i + 1)], w1_sc_rest[:, a, P * i : P * (i + 1)]
+            return w1_dealt[:, a, c - LOWER, :], w1_sc_dealt[:, a, c - LOWER, :]
+
+        h_sb = {}
         used_banks = []
 
-        def next_bank(shape, name):
-            used_banks.append(name)
-            return banks.tile(shape, F32, name=name, tag=f"bank{len(used_banks) % 4}")
-
         def first_product(c):
-            h_sb[c] = sbuf([P, S], F32, f"h{c}", "row_slot1" if c == 0 else None)
+            h_sb[c] = place([P, S], F32, f"h{c}", {3: "low0", 4: "raw4"}.get(c, f"h{c}"))
             if c == 0:
-                parts = [(lo, hi, P if lo == 0 else hi - lo) for lo, hi in FIRST_PARTS]
+                parts = [(lo, hi, hi - lo) for lo, hi in FIRST_PARTS]
             else:
                 parts = [(0, BANK, BANK), (BANK, S, BANK)]
             for lo, hi, width in parts:
-                h_sum = next_bank([P, hi - lo], "h_sum")
+                used_banks.append(c)
+                h_sum = bank([P, hi - lo], f"bank{len(used_banks) % 4}")
                 for at in range(lo, hi, width):
                     for a in range(PASSES):
-                        if c == 0:
-                            w1_codes, w1_scale = w1_first[:, a, :], w1_sc_first[:, a, :]
-                        else:
-                            w1_codes = w1_rest[:, a, 2 * P * (c - 1) : 2 * P * c]
-                            w1_scale = w1_sc_rest[:, a, P * (c - 1) : P * c]
+                        w1_codes, w1_scale = w1_tile(c, a)
                         nc.tensor.matmul_mx(
                             out=h_sum[:, at - lo : at - lo + width],
                             lhsT=w1_codes.bitcast(FP4X4),
@@ -182,158 +227,227 @@ def tile_list_fetal_slice_mosaic_kernel(
                             start=(a == 0),
                             stop=(a == PASSES - 1),
                         )
-                nc.scalar.copy(out=h_sb[c][:, lo:hi], in_=h_sum[:])
+                if c == 0 and lo == 0:
+                    nc.vector.tensor_tensor(h_sb[c][:, lo:hi], h_sum[:], wgs_first[:], ALU.mult)
+                else:
+                    nc.scalar.copy(out=h_sb[c][:, lo:hi], in_=h_sum[:])
 
-        first_product(0)
-        first_product(1)
-        bias_sb = sbuf([P, PASSES, 4 * PACK], F32, "bias_sb", "bias")
-        with nc.allow_non_contiguous_dma(reason="one value of the bias for each partition and row tile"):
-            nc.sync.dma_start(out=bias_sb[:, 0, 0:PACK], in_=bias[0 : STEADY * P].rearrange("(c p) -> p c", p=P))
-        nc.sync.dma_start(out=bias_sb[:, 1, 0:PACK], in_=bias[STEADY * P :].rearrange("(p t) -> p t", t=PACK))
-        ident_f32 = sbuf([P, P], F32, "ident_f32")
-        make_identity(nc, ident_f32[:])
-        ident_bf = sbuf([P, P], BF16, "ident_bf")
-        nc.scalar.activation(out=ident_bf[:], in_=ident_f32[:], func=IDENTITY)
-        neg_bias = sbuf([P, ROW_TILES], F32, "neg_bias")
-        nc.scalar.activation(
-            out=neg_bias[:].rearrange("p (g t) -> p g t", t=PACK), in_=bias_sb[:, :, 0:PACK], func=IDENTITY, scale=-1.0
-        )
-        h_turned = sbuf([P, S // P, PACK, P], F32, "h_turned")
-        upper = STEADY * P
+        weighed_place = {3: ("h3", 0), 4: ("h4", 0), 5: ("page0", EDGE), 6: ("page0", ROW + EDGE), 7: ("wgs", 0)}
 
-        def upper_product():
-            for b in range(S // P):
-                cols = slice(b * P, (b + 1) * P)
-                h_sum = next_bank([P, BANK], "h_sum")
-                for a in range(PASSES):
-                    nc.tensor.matmul_mx(
-                        out=h_sum[:],
-                        lhsT=v_w[a][:, cols].bitcast(FP8X4),
-                        lhsT_scale=v_scale(a, cols.start, cols.stop),
-                        rhs=w1_rest[:, a, 2 * (upper - P) :].bitcast(FP4X4),
-                        rhs_scale=w1_sc_rest[:, a, upper - P :],
-                        start=(a == 0),
-                        stop=(a == PASSES - 1),
-                    )
-                nc.scalar.copy(out=h_turned[:, b, :, :], in_=h_sum[:].rearrange("j (p t) -> j t p", t=PACK))
+        def weigh(c, lo=0, hi=S):
+            weights = wgs_sb if c < LOWER else wgs_dealt[c - LOWER]
+            plain = h_sb[c]
+            if c in weighed_place:
+                h_sb[c] = place([P, S], F32, f"weighed{c}", *weighed_place[c])
+            nc.gpsimd.tensor_tensor(h_sb[c][:, lo:hi], plain[:, lo:hi], weights[:, lo:hi], ALU.mult)
 
-        wgs_dealt = {}
+        def scatter(c, lo=0, hi=S):
+            nc.vector.tensor_copy(pages[c][:].indirect(entries(idx2, lo, hi)), h_sb[c][:, lo:hi])
 
-        def load_wgs_dealt(t, slot):
-            if slot:
-                wgs_dealt[t] = sbuf([P, S], F32, f"wgs_dealt{t}", slot)
-            else:
-                wgs_dealt[t] = reused.tile([P, S], F32, name=f"wgs_dealt{t}", align_bytes=64, offset=0)
-            for quad in range(QUADRANTS):
-                nc.sync.dma_start(
-                    out=wgs_dealt[t][QUADRANT * quad : QUADRANT * (quad + 1), :],
-                    in_=wgs.rearrange("(q t) j -> t q j", t=PACK)[t],
-                )
+        ident = own([P, P], F32, "ident")
+        make_identity(nc, ident[:])
 
-        def turn_h_back(t):
-            h_sb[STEADY + t] = sbuf([P, S], F32, f"h{STEADY + t}")
-            for half in range(S // BANK):
-                back = turns.tile([P, BANK // P, P], F32, name="back", tag="back" if t < PACK - 1 else "turned")
-                for b in range(BANK // P):
-                    nc.tensor.transpose(back[:, b, :], h_turned[:, half * BANK // P + b, t, :], ident_f32[:])
+        low_sb = {}
+        low_place = [("low0", 0), ("dealt1", 0), ("drop0", 0), ("low3", -EDGE)]
+
+        def load_low(c):
+            low_sb[c] = place([P, M], F32, f"low{c}", *low_place[c])
+            nc.sync.dma_start(out=low_sb[c][:], in_=low[c * P : (c + 1) * P, :])
+
+        x = {}
+
+        def gather(c):
+            nc.vector.tensor_copy(x[c], pages[c][:].indirect(idx3[:]))
+
+        sign, kept, dropped = {}, {}, {}
+        sign_place = [("page4", 0), ("h0", 0), ("h0", ROW // 2), ("h0", 0)]
+        gap_place = ["gap0", "gap0", "gap1", "gap1"]
+        keep_place = [("keep0", 0), ("keep1", 0), ("keep2", -2 * EDGE), ("last", 0)]
+        drop_place = [("drop0", 0), ("drop1", 0), ("dealt2", 0), ("last", ROW)]
+
+        def compare(c):
+            gap = place([P, M], F32, f"gap{c}", gap_place[c])
+            nc.gpsimd.tensor_tensor(gap[:], x[c], low_sb[c][:], ALU.subtract)
+            sign[c] = place([P, M], BF16, f"sign{c}", *sign_place[c])
+            nc.scalar.activation(out=sign[c][:], in_=gap[:], func=SIGN)
+
+        def shares(c):
+            kept[c] = place([P, M], F32, f"keep{c}", *keep_place[c])
+            nc.scalar.activation(out=kept[c][:], in_=sign[c][:], func=COPY, scale=0.5, bias=0.5)
+            dropped[c] = place([P, M], F32, f"drop{c}", *drop_place[c])
+            nc.scalar.activation(out=dropped[c][:], in_=sign[c][:], func=COPY, scale=-0.5, bias=0.5)
+
+        low_part = {}
+
+        def choose(c, lo=0, hi=M):
+            nc.gpsimd.tensor_tensor(x[c][:, lo:hi], x[c][:, lo:hi], kept[c][:, lo:hi], ALU.mult)
+            low_part[c] = place([P, M], F32, "low_part0", "gap1") if c == 0 else low_sb[c]
+            nc.gpsimd.tensor_tensor(low_part[c][:, lo:hi], low_sb[c][:, lo:hi], dropped[c][:, lo:hi], ALU.mult)
+
+        blocks = BANK // P
+        z_t = [place([P, blocks, 2, P], F32, f"z_t{half}", f"z_t{half}") for half in range(M // BANK)]
+        share = P // PACK
+
+        def add_up(c, halves=(0, 1)):
+            for half in halves:
+                z_sum = bank([P, blocks, P], f"sum{half}")
+                for b in range(blocks):
+                    cols = slice(half * BANK + b * P, half * BANK + (b + 1) * P)
+                    terms = [x[c][:, cols], low_part[c][:, cols], bias_blocks[:, c, :]]
+                    for i, term in enumerate(terms):
+                        nc.tensor.matmul(
+                            z_sum[:, b, :], term, ident[:], start=(i == 0), stop=(i == len(terms) - 1), is_transpose=True
+                        )
+                pairs = z_t[half][:, :, :, share * c : share * (c + 1)].bitcast(BF16)
                 nc.scalar.copy(
-                    out=h_sb[STEADY + t][:, half * BANK : (half + 1) * BANK], in_=back[:].rearrange("p b j -> p (b j)")
+                    out=pairs.rearrange("m b u (l e) -> m b u l e", e=2),
+                    in_=z_sum[:].rearrange("m b (l u e) -> m b u l e", u=2, e=2),
                 )
 
-        floor = {}
+        w2_codes = place([P, PASSES, N], U32, "w2_codes", "w2_codes")
+        w2_sc = place([P, PASSES, N], U8, "w2_sc", "drop1", EDGE)
+        w2_bf = {}
 
-        def load_floors(c, count):
-            rows = sbuf([P, count, M], F32, f"low{c}", f"row_slot{c % SLOTS}" if count == 1 else f"floor{c - 1}")
-            nc.sync.dma_start(out=rows[:], in_=low[c * P : (c + count) * P, :].rearrange("(p i) m -> p i m", p=P))
-            floor[c] = sbuf([P, count, M], F32, f"floor{c}")
-            for i in range(count):
-                nc.scalar.activation(
-                    out=floor[c][:, i, :], in_=rows[:, i, :], func=IDENTITY, bias=neg_bias[:, c + i : c + i + 1]
-                )
+        def round_w2(g):
+            w2_rows = place([P, PACK, N], F32, f"w2_rows{g}", ("page5", "page4")[g])
+            rows = w2[g * UPPER_ROW : (g + 1) * UPPER_ROW, :]
+            if g == 0:
+                nc.sync.dma_start(out=w2_rows[:], in_=rows.rearrange("(p t) n -> p t n", t=PACK))
+            else:
+                load_planes(w2_rows, rows)
+            w2_bf[g] = place([P, N, PACK], BF16, f"w2_bf{g}", "w2_bf", ROW * g)
+            nc.scalar.copy(out=w2_bf[g][:], in_=w2_rows[:].rearrange("p t n -> p n t"))
 
-        w2_codes = sbuf([P, PASSES, N], U32, "w2_codes")
-        w2_sc = sbuf([P, PASSES, N], U8, "w2_sc")
-
-        def prepare_w2(g):
-            w2_rows = sbuf([P, PACK, N], F32, f"w2_rows{g}", ("floor2", "h4")[g])
-            rows = w2[g * P * PACK : (g + 1) * P * PACK, :]
-            nc.sync.dma_start(out=w2_rows[:], in_=rows.rearrange("(p t) n -> p t n", t=PACK))
-            w2_bf = sbuf([P, N, PACK], BF16, f"w2_bf{g}")
-            nc.scalar.copy(out=w2_bf[:], in_=w2_rows[:].rearrange("p t n -> p n t"))
+        def quantise_w2(g):
             nc.vector.quantize_mx(
                 out=w2_codes[:, g, :].bitcast(FP8X4),
                 scales=w2_sc[:, g, :],
-                in_=w2_bf[:].rearrange("p n t -> p (n t)"),
+                in_=w2_bf[g][:].rearrange("p n t -> p (n t)"),
             )
 
-        def scatter(c, lo, hi, weights):
-            nc.vector.tensor_tensor(
-                pages[c][:].indirect(entries(idx2, lo, hi)), h_sb[c][:, lo:hi], weights[:, lo:hi], ALU.mult
-            )
+        first_product(0)
+        first_product(1)
+        scatter(0, *FIRST_PARTS[0])
+        for lo, hi in FIRST_PARTS[1:]:
+            weigh(0, lo, hi)
+            scatter(0, lo, hi)
+        weigh(1)
+        scatter(1)
+        bias_sb = place([P, PASSES, 4 * PACK], F32, "bias_sb", "bias")
+        with nc.allow_non_contiguous_dma(reason="one value of the bias for each partition and row tile"):
+            nc.sync.dma_start(out=bias_sb[:, 0, 0:PACK], in_=bias[0:UPPER_ROW].rearrange("(c p) -> p c", p=P))
+            for e in range(RUN):
+                nc.sync.dma_start(
+                    out=bias_sb[e:P:RUN, 1, 0:PACK],
+                    in_=bias[UPPER_ROW:].rearrange("(a t e) -> e a t", t=PACK, e=RUN)[e],
+                )
+        load_wgs_dealt(1)
+        load_wgs_dealt(2)
+        first_product(2)
+        first_product(3)
+        deal_w1()
+        first_product(4)
+        for c in (2, 3, 4):
+            weigh(c)
+        for c in (5, 6, 7):
+            first_product(c)
+        bias_blocks = own([P, LOWER, P], F32, "bias_blocks")
+        nc.scalar.activation(
+            out=bias_blocks[:], in_=bias_sb[:, 0, 0:PACK].unsqueeze(2).to_broadcast([P, LOWER, P]), func=COPY, scale=-1.0
+        )
+        neg_bias = place([P, PACK], F32, "neg_bias", "h0")
+        nc.scalar.activation(out=neg_bias[:], in_=bias_sb[:, 1, 0:PACK], func=COPY, scale=-1.0)
+        for g in range(PASSES):
+            round_w2(g)
+        load_page(2)
+        load_low(0)
+        load_page(3)
+        load_wgs_dealt(3)
+        x0 = place([P, M], F32, "x0", "raw4")
+        x[0] = x0[:]
+        gather(0)
 
-        def gather(c, x, lo, hi):
-            if c == 0:
-                nc.vector.tensor_copy(x, pages[c][:].indirect(entries(idx3, lo, hi)))
-                return
-            bias_row = sbuf([P, M], F32, f"bias_row{c}", f"bias_row{c % 2}")
-            nc.scalar.copy(out=bias_row[:], in_=bias_sb[:, 0, c : c + 1].to_broadcast([P, M]))
-            nc.vector.tensor_tensor(x, pages[c][:].indirect(entries(idx3, lo, hi)), bias_row[:], ALU.subtract)
+        compare(0)
+        shares(0)
+        scatter(2)
+        weigh(5)
+        weigh(6)
+        scatter(3)
+        choose(0)
+        floors = place([P, PACK, M], F32, "floors", "floors", EDGE)
+        load_planes(floors, low[UPPER_ROW:, :])
+        for t in range(PACK):
+            nc.scalar.activation(out=floors[:, t, :], in_=floors[:, t, :], func=IDENTITY, bias=neg_bias[:, t : t + 1])
+        bias_wide = own([P, PACK, BANK], F32, "bias_wide")
+        nc.scalar.copy(out=bias_wide[:], in_=bias_sb[:, 1, 0:PACK].unsqueeze(2).to_broadcast([P, PACK, BANK]))
+        load_low(1)
+        load_page(4)
+        load_low(2)
+        load_page(5)
+        x1 = place([P, M], F32, "x1", "bias", 5 * EDGE - ROW)
+        x2 = place([P, M], F32, "x2", "x2", -EDGE)
+        x[1], x[2] = x1[:], x2[:]
+        gather(1)
+        gather(2)
 
-        def floored(z, x, c, lo, hi):
-            if c == 0:
-                nc.vector.scalar_tensor_tensor(z, x, neg_bias[:, 0:1], floor[0][:, 0, lo:hi], ALU.add, ALU.max)
-                return
-            nc.vector.tensor_tensor(z, x, floor[c][:, 0, lo:hi], ALU.max)
+        compare(1)
+        shares(1)
+        compare(2)
+        weigh(7)
+        add_up(0)
+        scatter(4)
+        scatter(5)
+        choose(1)
+        load_page(6)
+        load_low(3)
+        load_page(7)
+        x3 = place([P, M], F32, "x3", "x3", EDGE)
+        x[3] = x3[:]
+        gather(3)
+        for g in range(PASSES):
+            quantise_w2(g)
 
-        spans = {0: [(0, BANK), (BANK, M - PIECE), (M - PIECE, M)]}
-        z_t = {}
-        for g in range(1):
-            for lo, hi in spans[g]:
-                z_t[(g, lo)] = sbuf([P, (hi - lo) // P, 2, P], F32, f"z_t{g}_{lo}")
-        share = P // PACK
+        compare(3)
+        shares(2)
+        shares(3)
+        add_up(1)
+        scatter(6)
+        scatter(7)
+        choose(2)
+        choose(3, 0, BANK)
+        choose(3, BANK, M)
+        add_up(2)
 
-        def turn(c, count, z, lo, hi):
-            g, within = divmod(c, TILES_A_PASS)
-            blocks = (hi - lo) // P
-            turned = turns.tile([P, count, blocks, P], BF16, name="turned", tag="turned")
-            for i in range(count):
-                for b in range(blocks):
-                    nc.tensor.transpose(turned[:, i, b, :], z[:, i, b * P : (b + 1) * P], ident_bf[:])
-            for at, end in spans[g]:
-                if lo <= at and end <= hi:
-                    words = turned[:, :, (at - lo) // P : (end - lo) // P, :].bitcast(F32)
-                    nc.scalar.copy(
-                        out=z_t[(g, at)][:, :, :, share * within : share * (within + count)].rearrange(
-                            "m b u (i l) -> m i b u l", i=count
-                        ),
-                        in_=words.rearrange("m i b (l u) -> m i b u l", u=2),
-                    )
+        z_sc = [own([P, M], U8, f"z_sc{g}") for g in range(PASSES)]
+        woven_lower = {}
 
-        z_codes = {}
-        z_sc = [sbuf([P, M], U8, f"z_sc{g}") for g in range(PASSES)]
-
-        def weave_lower(g, lo, hi):
-            woven = sbuf([P, (hi - lo) * PACK], BF16, f"woven{g}_{lo}")
-            step = min(PIECE, hi - lo)
-            blocks = step // P
-            for at in range(0, hi - lo, step):
-                back = turns.tile([P, blocks, 2, P], F32, name="back", tag="back")
-                for b in range(blocks):
+        def weave_lower(lo, hi):
+            woven_lower[lo] = place([P, (hi - lo) * PACK], BF16, f"woven0_{lo}", "w2_bf", lo * PACK * 2)
+            for at in range(lo, hi, PIECE):
+                back = bank([P, PIECE // P, 2, P], f"back{at // PIECE % 2}")
+                for b in range(PIECE // P):
                     for u in range(2):
-                        nc.tensor.transpose(back[:, b, u, :], z_t[(g, lo)][:, at // P + b, u, :], ident_f32[:])
-                pairs = woven[:, at * PACK : (at + step) * PACK].bitcast(F32)
+                        nc.tensor.transpose(back[:, b, u, :], z_t[at // BANK][:, at % BANK // P + b, u, :], ident[:])
+                pairs = woven_lower[lo][:, (at - lo) * PACK : (at - lo + PIECE) * PACK].bitcast(F32)
                 nc.scalar.copy(
-                    out=pairs.rearrange("p (b m u) -> p b m u", b=blocks, u=2),
+                    out=pairs.rearrange("p (b m u) -> p b m u", b=PIECE // P, u=2),
                     in_=back[:].rearrange("p b u m -> p b m u"),
                 )
-            return woven
 
-        def quantise(g, lo, hi, woven, slot=None):
-            z_codes[(g, lo)] = sbuf([P, hi - lo], U32, f"z_codes{g}_{lo}", slot)
+        add_up(3, (0,))
+        weave_lower(*PIECES[0])
+        add_up(3, (1,))
+        for lo, hi in PIECES[1:]:
+            weave_lower(lo, hi)
+
+        z_codes = {}
+
+        def quantise(g, lo, hi, woven):
+            region, shift = (("raw4", 0), ("spare", 0))[g]
+            z_codes[(g, lo)] = place([P, hi - lo], U32, f"z_codes{g}_{lo}", region, shift + 4 * lo)
             nc.vector.quantize_mx(out=z_codes[(g, lo)][:].bitcast(FP8X4), scales=z_sc[g][:, lo:hi], in_=woven)
 
         out_view = out.rearrange("(j p) m -> p j m", p=P)
-
         sums = {}
 
         def groups(span):
@@ -343,13 +457,10 @@ def tile_list_fetal_slice_mosaic_kernel(
 
         def product(span):
             lo, hi = SPANS[span]
-            at = max(first for first, end in spans[0] if first <= lo)
+            at = max(first for first, end in PIECES if first <= lo)
             moving = [z_codes[(0, at)][:, lo - at : hi - at], z_codes[(1, lo)][:]]
             for number, group in enumerate(groups(span)):
-                if span in (1, 2):
-                    out_sum = turns.tile([P, len(group), hi - lo], F32, name="out_sum", tag=("turned", "back")[span - 1])
-                else:
-                    out_sum = banks.tile([P, len(group), hi - lo], F32, name="out_sum", tag=f"bank{number}")
+                out_sum = bank([P, len(group), hi - lo], ("bank", "sum", "back", "bank")[span] + str(number))
                 for g in range(PASSES):
                     for j in group:
                         n_cols = slice(j * P, (j + 1) * P)
@@ -364,70 +475,41 @@ def tile_list_fetal_slice_mosaic_kernel(
                         )
                 sums[(span, number)] = out_sum
 
+        result_place = [("page3", -EDGE), ("h3", 0), ("dealt1", 0), ("dealt1", ROW // 2)]
+
         def store(span, engine_copies):
             lo, hi = SPANS[span]
+            region, shift = result_place[span]
             for number, group in enumerate(groups(span)):
-                result = sbuf([P, len(group), hi - lo], F32, f"result{span}_{number}", (f"z{number}", f"h{5 + number}", None, None)[span])
+                size = 4 * len(group) * (hi - lo)
+                result = place([P, len(group), hi - lo], F32, f"result{span}_{number}", region, shift + number * size)
                 engine_copies[number % 2](out=result[:], in_=sums[(span, number)][:])
                 nc.sync.dma_start(out=out_view[:, group[0] : group[-1] + 1, lo:hi], in_=result[:])
 
-        for lo, hi in FIRST_PARTS:
-            scatter(0, lo, hi, wgs_first if lo == 0 else wgs_sb)
-        x = sbuf([P, M], F32, "x0", "row_slot2")
-        gather(0, x[:], 0, M)
-        for c in range(1, STEADY + 1):
-            if c != 2:
-                load_floors(c - 1, 1)
-            load_page(c + 1)
-            if c == 1:
-                first_product(2)
-            scatter(c, 0, S, wgs_sb if c < STEADY else wgs_dealt[0])
-            z = sbuf([P, 1, M], BF16, f"z{c - 1}")
-            floored(z[:, 0, :], x[:], c - 1, 0, M)
-            if c < STEADY:
-                x = sbuf([P, M], F32, f"x{c}", f"row_slot{c - 1}")
-                gather(c, x[:], 0, M)
-            if c == 1:
-                load_floors(1, 1)
-                first_product(3)
-                upper_product()
-                for t in range(PACK):
-                    turn_h_back(t)
-            turn(c - 1, 1, z, 0, M)
-            load_wgs_dealt(c - 1, f"h{c}" if c < STEADY else None)
-            if c == TILES_A_PASS:
-                woven_lower = {lo: weave_lower(0, lo, hi) for lo, hi in spans[0]}
-                for lo, hi in spans[0][:-1]:
-                    quantise(0, lo, hi, woven_lower[lo][:])
-        for c in range(STEADY + 2, ROW_TILES):
-            load_page(c)
-        for g in range(PASSES):
-            prepare_w2(g)
-        late = ROW_TILES - STEADY
-        load_floors(STEADY, late)
-        for c in range(STEADY + 1, ROW_TILES):
-            scatter(c, 0, S, wgs_dealt[c - STEADY])
-
-        bias_wide = sbuf([P, PACK, BANK], F32, "bias_wide")
-        nc.scalar.copy(out=bias_wide[:], in_=bias_sb[:, 1, 0:PACK].unsqueeze(2).to_broadcast([P, PACK, BANK]))
-        shifted = sbuf([P, PACK, M], F32, "shifted", f"floor{STEADY - 1}")
+        shifted_place = [("last", 0), ("z_t0", 0), ("z_t1", 0)]
+        shifted = [
+            place([P, PACK, hi - lo], F32, f"shifted{piece}", *shifted_place[piece]) for piece, (lo, hi) in enumerate(PIECES)
+        ]
 
         def pick(piece, t):
             lo, hi = PIECES[piece]
             nc.vector.tensor_tensor(
-                shifted[:, t, lo:hi],
-                pages[STEADY + t][:].indirect(entries(idx3, lo, hi)),
+                shifted[piece][:, t, :],
+                pages[LOWER + t][:].indirect(entries(idx3, lo, hi)),
                 bias_wide[:, t, 0 : hi - lo],
                 ALU.subtract,
             )
 
         def floored_woven(span):
             lo, hi = SPANS[span]
-            woven = sbuf([P, hi - lo, PACK], BF16, f"woven1_{lo}")
+            piece = min(span, len(PIECES) - 1)
+            at = PIECES[piece][0]
+            region, shift = ("low3", -EDGE) if span == 0 else ("dealt2", (lo - BANK) * PACK * 2)
+            woven = place([P, hi - lo, PACK], BF16, f"woven1_{lo}", region, shift)
             nc.vector.tensor_tensor(
                 woven[:].rearrange("p (c i) t -> p c t i", i=PACK),
-                shifted[:, :, lo:hi].rearrange("p t (c i) -> p c t i", i=PACK),
-                floor[STEADY][:, :, lo:hi].rearrange("p t (c i) -> p c t i", i=PACK),
+                shifted[piece][:, :, lo - at : hi - at].rearrange("p t (c i) -> p c t i", i=PACK),
+                floors[:, :, lo:hi].rearrange("p t (c i) -> p c t i", i=PACK),
                 ALU.max,
             )
             return woven[:].rearrange("p m t -> p (m t)")
@@ -438,13 +520,14 @@ def tile_list_fetal_slice_mosaic_kernel(
                 woven = floored_woven(piece - 1)
             pick(piece, 1)
             if piece > 0:
+                quantise(0, *PIECES[piece - 1], woven_lower[PIECES[piece - 1][0]][:])
                 quantise(1, *SPANS[piece - 1], woven)
                 product(piece - 1)
                 store(piece - 1, (nc.scalar.copy, nc.scalar.copy))
             pick(piece, 2)
             pick(piece, 3)
-        lo, hi = spans[0][-1]
-        quantise(0, lo, hi, woven_lower[lo][:], "page_slot0")
+        lo, hi = PIECES[-1]
+        quantise(0, lo, hi, woven_lower[lo][:])
         last_spans = (len(SPANS) - 2, len(SPANS) - 1)
         woven = {s: floored_woven(s) for s in last_spans}
         for s in last_spans:

@@ -42,14 +42,14 @@ SPANS = [(0, BANK), (BANK, M - PIECE), (M - PIECE, M - P), (M - P, M)]
 ROW = 4 * M
 EDGE = 64
 REGIONS = [
-    ("dealt0", ROW), ("page1", 2 * ROW), ("keep1", ROW), ("page2", 2 * ROW), ("wgs", ROW + EDGE), ("page3", 2 * ROW), ("keep2", ROW),
+    ("weighed6", ROW), ("page1", 2 * ROW), ("keep1", ROW), ("page2", 2 * ROW), ("raw2", ROW + EDGE), ("page3", 2 * ROW),
     ("page5", 2 * ROW), ("keep0", ROW), ("page4", 2 * ROW),
-    ("spare", ROW), ("drop0", ROW), ("dealt1", ROW), ("dealt2", ROW),
+    ("spare", ROW), ("drop0", ROW), ("low2", ROW), ("low_part0", ROW),
     ("floors", 4 * ROW), ("page0", 2 * ROW), ("h1", ROW), ("h0", ROW),
     ("x3", ROW), ("drop1", ROW), ("low3", ROW),
-    ("x1", ROW), ("bias", 4 * EDGE), ("low0", ROW), ("x2", ROW), ("w2_codes", ROW), ("raw4", ROW), ("last", 2 * ROW),
-    ("h4", ROW), ("h5", ROW), ("h6", ROW), ("z_t0", ROW), ("h7", ROW), ("h2", ROW), ("z_t1", ROW),
-    ("gap0", ROW), ("gap1", ROW), ("h3", ROW), ("w2_bf", 2 * ROW),
+    ("x1", ROW), ("bias", 4 * EDGE), ("low0", ROW), ("x2", ROW), ("w2_codes", ROW), ("wgs", ROW), ("last", 2 * ROW),
+    ("dealt2", ROW), ("h5", ROW), ("dealt3", ROW), ("h6", ROW), ("z_t0", ROW), ("h7", ROW), ("h2", ROW), ("z_t1", ROW),
+    ("h3", ROW), ("w2_bf", 2 * ROW),
 ]
 START = {name: sum(size for other, size in REGIONS[:i]) for i, (name, size) in enumerate(REGIONS)}
 
@@ -108,7 +108,7 @@ def tile_list_fetal_slice_mosaic_kernel(
                     in_=rows.rearrange("a r c -> r a c").bitcast(I32),
                 )
 
-        tab_w = [place([P, T], I32, "tab_w0", "page2", 2 * EDGE), place([P, T], I32, "tab_w1", "keep0", -ROW // 2)]
+        tab_w = [place([P, T], I32, "tab_w0", "w2_codes"), place([P, T], I32, "tab_w1", "page1")]
 
         def load_words(a):
             nc.sync.dma_start(out=tab_w[a][:], in_=tab_words[a].rearrange("p t i -> p (t i)").bitcast(I32))
@@ -116,9 +116,9 @@ def tile_list_fetal_slice_mosaic_kernel(
         nc.sync.dma_start(idx2[:], offs2)
         nc.sync.dma_start(idx3[:], offs3)
         w1_view = w1_words.rearrange("a p c -> p a c")
-        w1_first = place([P, PASSES, 2 * head], U8, "w1_first", "dealt2", -2 * head)
+        w1_first = place([P, PASSES, 2 * head], U8, "w1_first", "page4", -2 * head)
         nc.sync.dma_start(out=w1_first[:].bitcast(I32), in_=w1_view[:, :, 0 : 2 * head].bitcast(I32))
-        wgs_first = place([P, FIRST], F32, "wgs_first", "page1", -2 * FIRST)
+        wgs_first = place([P, FIRST], F32, "wgs_first", "floors", EDGE + ROW - 2 * FIRST)
         nc.sync.dma_start(out=wgs_first[:], in_=wgs[:, 0:FIRST])
         load_words(0)
         load_w1_scales(w1_sc_first, slice(0, head))
@@ -158,7 +158,7 @@ def tile_list_fetal_slice_mosaic_kernel(
         load_page(0)
         v_w = [place([P, S], U32, "v_w0", "x1"), place([P, S], U32, "v_w1", "x2")]
         nc.vector.tensor_copy(v_w[0][:], tab_w[0][:].bitcast(U32).indirect(idx[:]))
-        wgs_sb = place([P, S], F32, "wgs_sb", "wgs", EDGE)
+        wgs_sb = place([P, S], F32, "wgs_sb", "wgs")
         nc.sync.dma_start(out=wgs_sb[:, FIRST:S], in_=wgs[:, FIRST:S])
         nc.sync.dma_start(out=wgs_sb[:, 0:FIRST], in_=wgs[:, 0:FIRST])
         rest = H - head
@@ -172,7 +172,8 @@ def tile_list_fetal_slice_mosaic_kernel(
         load_page(1)
 
         wgs_dealt = {}
-        dealt_place = [("dealt0", 0), ("dealt1", 0), ("dealt2", 0), ("dealt0", 0)]
+
+        dealt_place = [("floors", EDGE), ("floors", EDGE + ROW), ("dealt2", EDGE), ("dealt3", -EDGE)]
 
         def load_wgs_dealt(t):
             wgs_dealt[t] = place([P, S], F32, f"wgs_dealt{t}", *dealt_place[t])
@@ -180,6 +181,7 @@ def tile_list_fetal_slice_mosaic_kernel(
                 nc.sync.dma_start(out=wgs_dealt[t][QUADRANT * quad : QUADRANT * (quad + 1), 0:S], in_=dealt_rows(wgs, t))
 
         load_wgs_dealt(0)
+        load_wgs_dealt(1)
 
         w1_dealt = place([P, PASSES, PACK, 2 * P], U8, "w1_dealt", "w2_codes")
         w1_sc_dealt = place([P, PASSES, PACK, P], U8, "w1_sc_dealt", "w2_codes", PASSES * PACK * 2 * P)
@@ -207,7 +209,7 @@ def tile_list_fetal_slice_mosaic_kernel(
         used_banks = []
 
         def first_product(c):
-            h_sb[c] = place([P, S], F32, f"h{c}", {3: "low0", 4: "raw4"}.get(c, f"h{c}"))
+            h_sb[c] = place([P, S], F32, f"h{c}", *{2: ("raw2", EDGE), 3: ("low0", 0), 4: ("floors", EDGE + 2 * ROW)}.get(c, (f"h{c}", 0)))
             if c == 0:
                 parts = [(lo, hi, hi - lo) for lo, hi in FIRST_PARTS]
             else:
@@ -232,7 +234,9 @@ def tile_list_fetal_slice_mosaic_kernel(
                 else:
                     nc.scalar.copy(out=h_sb[c][:, lo:hi], in_=h_sum[:])
 
-        weighed_place = {3: ("h3", 0), 4: ("h4", 0), 5: ("page0", EDGE), 6: ("page0", ROW + EDGE), 7: ("wgs", 0)}
+        weighed_place = {
+            2: ("h2", 0), 3: ("h3", 0), 4: ("page0", EDGE), 5: ("page0", ROW + EDGE), 6: ("weighed6", EDGE), 7: ("raw2", 0),
+        }
 
         def weigh(c, lo=0, hi=S):
             weights = wgs_sb if c < LOWER else wgs_dealt[c - LOWER]
@@ -246,45 +250,57 @@ def tile_list_fetal_slice_mosaic_kernel(
 
         ident = own([P, P], F32, "ident")
         make_identity(nc, ident[:])
+        ident_bf = own([P, P], BF16, "ident_bf")
 
         low_sb = {}
-        low_place = [("low0", 0), ("dealt1", 0), ("drop0", 0), ("low3", -EDGE)]
+        low_place = [("low0", 0), ("spare", EDGE), ("low2", -EDGE), ("low_part0", 0)]
 
         def load_low(c):
             low_sb[c] = place([P, M], F32, f"low{c}", *low_place[c])
             nc.sync.dma_start(out=low_sb[c][:], in_=low[c * P : (c + 1) * P, :])
+            nc.scalar.activation(out=low_sb[c][:], in_=low_sb[c][:], func=COPY, scale=-1.0)
 
         x = {}
 
         def gather(c):
             nc.vector.tensor_copy(x[c], pages[c][:].indirect(idx3[:]))
 
-        sign, kept, dropped = {}, {}, {}
+        kept, dropped = {}, {}
+        blocks = BANK // P
         sign_place = [("page4", 0), ("h0", 0), ("h0", ROW // 2), ("h0", 0)]
-        gap_place = ["gap0", "gap0", "gap1", "gap1"]
-        keep_place = [("keep0", 0), ("keep1", 0), ("keep2", -2 * EDGE), ("last", 0)]
-        drop_place = [("drop0", 0), ("drop1", 0), ("dealt2", 0), ("last", ROW)]
+        keep_place = [("keep0", 0), ("keep1", 0), ("dealt2", 0), ("last", 0)]
+        drop_place = [("drop0", 0), ("drop1", 0), ("dealt3", 0), ("last", ROW)]
+
+        def add_turned(total, terms):
+            for i, term in enumerate(terms):
+                nc.tensor.matmul(total, term, ident[:], start=(i == 0), stop=(i == len(terms) - 1), is_transpose=True)
 
         def compare(c):
-            gap = place([P, M], F32, f"gap{c}", gap_place[c])
-            nc.gpsimd.tensor_tensor(gap[:], x[c], low_sb[c][:], ALU.subtract)
-            sign[c] = place([P, M], BF16, f"sign{c}", *sign_place[c])
-            nc.scalar.activation(out=sign[c][:], in_=gap[:], func=SIGN)
-
-        def shares(c):
+            sign = place([P, M // P, P], BF16, f"sign{c}", *sign_place[c])
             kept[c] = place([P, M], F32, f"keep{c}", *keep_place[c])
-            nc.scalar.activation(out=kept[c][:], in_=sign[c][:], func=COPY, scale=0.5, bias=0.5)
             dropped[c] = place([P, M], F32, f"drop{c}", *drop_place[c])
-            nc.scalar.activation(out=dropped[c][:], in_=sign[c][:], func=COPY, scale=-0.5, bias=0.5)
+            for half in range(M // BANK):
+                gap = bank([P, blocks, P], f"bank{half}")
+                for b in range(blocks):
+                    cols = slice(half * BANK + b * P, half * BANK + (b + 1) * P)
+                    add_turned(gap[:, b, :], [x[c][:, cols], low_sb[c][:, cols]])
+                nc.scalar.activation(out=sign[:, half * blocks : (half + 1) * blocks, :], in_=gap[:], func=SIGN)
+            for half in range(M // BANK):
+                back = banks.tile([P, BANK], BF16, name="sign_back", tag=f"bank{2 + half}")
+                for b in range(blocks):
+                    nc.tensor.transpose(back[:, b * P : (b + 1) * P], sign[:, half * blocks + b, :], ident_bf[:])
+                cols = slice(half * BANK, (half + 1) * BANK)
+                nc.scalar.activation(out=kept[c][:, cols], in_=back[:], func=COPY, scale=0.5, bias=0.5)
+                nc.scalar.activation(out=dropped[c][:, cols], in_=back[:], func=COPY, scale=0.5, bias=-0.5)
 
-        low_part = {}
+        x_part, low_part = {}, {}
 
         def choose(c, lo=0, hi=M):
-            nc.gpsimd.tensor_tensor(x[c][:, lo:hi], x[c][:, lo:hi], kept[c][:, lo:hi], ALU.mult)
-            low_part[c] = place([P, M], F32, "low_part0", "gap1") if c == 0 else low_sb[c]
+            x_part[c] = place([P, M], F32, "x_part2", "page3", -EDGE)[:] if c == 2 else x[c]
+            nc.gpsimd.tensor_tensor(x_part[c][:, lo:hi], x[c][:, lo:hi], kept[c][:, lo:hi], ALU.mult)
+            low_part[c] = place([P, M], F32, "low_part0", "low_part0") if c == 0 else low_sb[c]
             nc.gpsimd.tensor_tensor(low_part[c][:, lo:hi], low_sb[c][:, lo:hi], dropped[c][:, lo:hi], ALU.mult)
 
-        blocks = BANK // P
         z_t = [place([P, blocks, 2, P], F32, f"z_t{half}", f"z_t{half}") for half in range(M // BANK)]
         share = P // PACK
 
@@ -293,11 +309,7 @@ def tile_list_fetal_slice_mosaic_kernel(
                 z_sum = bank([P, blocks, P], f"sum{half}")
                 for b in range(blocks):
                     cols = slice(half * BANK + b * P, half * BANK + (b + 1) * P)
-                    terms = [x[c][:, cols], low_part[c][:, cols], bias_blocks[:, c, :]]
-                    for i, term in enumerate(terms):
-                        nc.tensor.matmul(
-                            z_sum[:, b, :], term, ident[:], start=(i == 0), stop=(i == len(terms) - 1), is_transpose=True
-                        )
+                    add_turned(z_sum[:, b, :], [x_part[c][:, cols], low_part[c][:, cols], bias_blocks[:, c, :]])
                 pairs = z_t[half][:, :, :, share * c : share * (c + 1)].bitcast(BF16)
                 nc.scalar.copy(
                     out=pairs.rearrange("m b u (l e) -> m b u l e", e=2),
@@ -309,7 +321,7 @@ def tile_list_fetal_slice_mosaic_kernel(
         w2_bf = {}
 
         def round_w2(g):
-            w2_rows = place([P, PACK, N], F32, f"w2_rows{g}", ("page5", "page4")[g])
+            w2_rows = place([P, PACK, N], F32, f"w2_rows{g}", "page4", 2 * ROW * (g - 1))
             rows = w2[g * UPPER_ROW : (g + 1) * UPPER_ROW, :]
             if g == 0:
                 nc.sync.dma_start(out=w2_rows[:], in_=rows.rearrange("(p t) n -> p t n", t=PACK))
@@ -341,16 +353,13 @@ def tile_list_fetal_slice_mosaic_kernel(
                     out=bias_sb[e:P:RUN, 1, 0:PACK],
                     in_=bias[UPPER_ROW:].rearrange("(a t e) -> e a t", t=PACK, e=RUN)[e],
                 )
-        load_wgs_dealt(1)
-        load_wgs_dealt(2)
-        first_product(2)
-        first_product(3)
-        deal_w1()
-        first_product(4)
-        for c in (2, 3, 4):
-            weigh(c)
-        for c in (5, 6, 7):
+        for c in (2, 3):
             first_product(c)
+            weigh(c)
+        deal_w1()
+        for c in range(LOWER, ROW_TILES):
+            first_product(c)
+        nc.scalar.copy(out=ident_bf[:], in_=ident[:])
         bias_blocks = own([P, LOWER, P], F32, "bias_blocks")
         nc.scalar.activation(
             out=bias_blocks[:], in_=bias_sb[:, 0, 0:PACK].unsqueeze(2).to_broadcast([P, LOWER, P]), func=COPY, scale=-1.0
@@ -362,28 +371,28 @@ def tile_list_fetal_slice_mosaic_kernel(
         load_page(2)
         load_low(0)
         load_page(3)
-        load_wgs_dealt(3)
-        x0 = place([P, M], F32, "x0", "raw4")
+        x0 = place([P, M], F32, "x0", "wgs")
         x[0] = x0[:]
         gather(0)
 
         compare(0)
-        shares(0)
         scatter(2)
+        weigh(4)
         weigh(5)
-        weigh(6)
         scatter(3)
         choose(0)
         floors = place([P, PACK, M], F32, "floors", "floors", EDGE)
-        load_planes(floors, low[UPPER_ROW:, :])
         for t in range(PACK):
+            nc.sync.dma_start(out=floors[:, t, :], in_=dealt_rows(low[UPPER_ROW:, :], t))
             nc.scalar.activation(out=floors[:, t, :], in_=floors[:, t, :], func=IDENTITY, bias=neg_bias[:, t : t + 1])
         bias_wide = own([P, PACK, BANK], F32, "bias_wide")
         nc.scalar.copy(out=bias_wide[:], in_=bias_sb[:, 1, 0:PACK].unsqueeze(2).to_broadcast([P, PACK, BANK]))
-        load_low(1)
+        load_wgs_dealt(2)
+        load_wgs_dealt(3)
         load_page(4)
-        load_low(2)
+        load_low(1)
         load_page(5)
+        load_low(2)
         x1 = place([P, M], F32, "x1", "bias", 5 * EDGE - ROW)
         x2 = place([P, M], F32, "x2", "x2", -EDGE)
         x[1], x[2] = x1[:], x2[:]
@@ -391,15 +400,15 @@ def tile_list_fetal_slice_mosaic_kernel(
         gather(2)
 
         compare(1)
-        shares(1)
-        compare(2)
+        weigh(6)
         weigh(7)
         add_up(0)
         scatter(4)
         scatter(5)
         choose(1)
-        load_page(6)
+        compare(2)
         load_low(3)
+        load_page(6)
         load_page(7)
         x3 = place([P, M], F32, "x3", "x3", EDGE)
         x[3] = x3[:]
@@ -408,8 +417,6 @@ def tile_list_fetal_slice_mosaic_kernel(
             quantise_w2(g)
 
         compare(3)
-        shares(2)
-        shares(3)
         add_up(1)
         scatter(6)
         scatter(7)
@@ -443,7 +450,7 @@ def tile_list_fetal_slice_mosaic_kernel(
         z_codes = {}
 
         def quantise(g, lo, hi, woven):
-            region, shift = (("raw4", 0), ("spare", 0))[g]
+            region, shift = (("wgs", 0), ("spare", 0))[g]
             z_codes[(g, lo)] = place([P, hi - lo], U32, f"z_codes{g}_{lo}", region, shift + 4 * lo)
             nc.vector.quantize_mx(out=z_codes[(g, lo)][:].bitcast(FP8X4), scales=z_sc[g][:, lo:hi], in_=woven)
 
@@ -475,7 +482,7 @@ def tile_list_fetal_slice_mosaic_kernel(
                         )
                 sums[(span, number)] = out_sum
 
-        result_place = [("page3", -EDGE), ("h3", 0), ("dealt1", 0), ("dealt1", ROW // 2)]
+        result_place = [("page0", EDGE), ("h3", 0), ("low3", 0), ("low3", ROW // 2)]
 
         def store(span, engine_copies):
             lo, hi = SPANS[span]
@@ -504,7 +511,7 @@ def tile_list_fetal_slice_mosaic_kernel(
             lo, hi = SPANS[span]
             piece = min(span, len(PIECES) - 1)
             at = PIECES[piece][0]
-            region, shift = ("low3", -EDGE) if span == 0 else ("dealt2", (lo - BANK) * PACK * 2)
+            region, shift = ("low_part0", 0) if span == 0 else ("h6", (lo - BANK) * PACK * 2)
             woven = place([P, hi - lo, PACK], BF16, f"woven1_{lo}", region, shift)
             nc.vector.tensor_tensor(
                 woven[:].rearrange("p (c i) t -> p c t i", i=PACK),

@@ -42,14 +42,13 @@ SPANS = [(0, BANK), (BANK, M - PIECE), (M - PIECE, M - P), (M - P, M)]
 ROW = 4 * M
 EDGE = 64
 REGIONS = [
-    ("weighed6", ROW), ("page1", 2 * ROW), ("keep1", ROW), ("page2", 2 * ROW), ("raw2", ROW + EDGE), ("page3", 2 * ROW),
-    ("page5", 2 * ROW), ("keep0", ROW), ("page4", 2 * ROW),
-    ("spare", ROW), ("drop0", ROW), ("low2", ROW), ("low_part0", ROW),
-    ("floors", 4 * ROW), ("page0", 2 * ROW), ("h1", ROW), ("h0", ROW),
-    ("x3", ROW), ("drop1", ROW), ("low3", ROW),
-    ("x1", ROW), ("bias", 4 * EDGE), ("low0", ROW), ("x2", ROW), ("w2_codes", ROW), ("wgs", ROW), ("last", 2 * ROW),
-    ("dealt2", ROW), ("h5", ROW), ("dealt3", ROW), ("h6", ROW), ("z_t0", ROW), ("h7", ROW), ("h2", ROW), ("z_t1", ROW),
-    ("h3", ROW), ("w2_bf", 2 * ROW),
+    ("page0", 2 * ROW), ("page1", 2 * ROW), ("page2", 2 * ROW), ("bias", ROW // 4), ("page3", 2 * ROW),
+    ("dealt0", ROW), ("dealt1", ROW), ("dealt2", ROW), ("dealt3", ROW + 2 * EDGE), ("h7", ROW), ("x3", ROW),
+    ("shares0", 2 * ROW), ("shares1", 2 * ROW), ("shares2", 2 * ROW), ("shares3", 2 * ROW), ("w2_sc", ROW // 4),
+    ("low0", ROW), ("low1", ROW), ("scales", ROW // 2), ("low2", ROW), ("low3", ROW), ("floors", 4 * ROW),
+    ("w2_codes", ROW), ("wgs", ROW),
+    ("h0", ROW), ("h1", ROW), ("h2", ROW), ("h3", ROW), ("h4", ROW), ("h5", ROW), ("h6", ROW), ("weighed7", ROW),
+    ("z_t0", ROW), ("z_t1", ROW), ("w2_bf", 2 * ROW),
 ]
 START = {name: sum(size for other, size in REGIONS[:i]) for i, (name, size) in enumerate(REGIONS)}
 
@@ -81,7 +80,7 @@ def tile_list_fetal_slice_mosaic_kernel(
             return listed[:, lo // PER_COLUMN : hi // PER_COLUMN]
 
         head = HEAD_TILES * P
-        w1_sc_first = place([P, PASSES, head], U8, "w1_sc_first", "bias")
+        w1_sc_first = place([P, PASSES, head], U8, "w1_sc_first", "dealt3", -head)
         nc.vector.memset(w1_sc_first[:].bitcast(I32), 0)
         nc.sync.dma_start(idx[:], offs)
         tab_sc = place([P, T], U8, "tab_sc", "page0")
@@ -108,7 +107,7 @@ def tile_list_fetal_slice_mosaic_kernel(
                     in_=rows.rearrange("a r c -> r a c").bitcast(I32),
                 )
 
-        tab_w = [place([P, T], I32, "tab_w0", "w2_codes"), place([P, T], I32, "tab_w1", "page1")]
+        tab_w = [place([P, T], I32, "tab_w0", "w2_codes"), place([P, T], I32, "tab_w1", "page1", ROW)]
 
         def load_words(a):
             nc.sync.dma_start(out=tab_w[a][:], in_=tab_words[a].rearrange("p t i -> p (t i)").bitcast(I32))
@@ -116,9 +115,9 @@ def tile_list_fetal_slice_mosaic_kernel(
         nc.sync.dma_start(idx2[:], offs2)
         nc.sync.dma_start(idx3[:], offs3)
         w1_view = w1_words.rearrange("a p c -> p a c")
-        w1_first = place([P, PASSES, 2 * head], U8, "w1_first", "page4", -2 * head)
+        w1_first = place([P, PASSES, 2 * head], U8, "w1_first", "dealt1", -2 * head)
         nc.sync.dma_start(out=w1_first[:].bitcast(I32), in_=w1_view[:, :, 0 : 2 * head].bitcast(I32))
-        wgs_first = place([P, FIRST], F32, "wgs_first", "floors", EDGE + ROW - 2 * FIRST)
+        wgs_first = place([P, FIRST], F32, "wgs_first", "bias")
         nc.sync.dma_start(out=wgs_first[:], in_=wgs[:, 0:FIRST])
         load_words(0)
         load_w1_scales(w1_sc_first, slice(0, head))
@@ -127,22 +126,14 @@ def tile_list_fetal_slice_mosaic_kernel(
         def dealt_rows(rows, t):
             return rows.rearrange("(a t e) c -> t a e c", t=PACK, e=RUN)[t]
 
-        def load_planes(planes, rows):
-            for e in range(RUN):
-                nc.sync.dma_start(out=planes[e:P:RUN, :, :], in_=rows.rearrange("(a t e) c -> e a t c", t=PACK, e=RUN)[e])
-
         pages = {}
-        page_place = {
-            0: ("page0", 0), 1: ("page1", 0), 2: ("page2", 2 * EDGE), 3: ("page3", -EDGE), 4: ("page4", -EDGE),
-            5: ("page5", EDGE), 6: ("page1", EDGE), 7: ("page2", -EDGE),
-        }
 
         def load_page(c):
-            pages[c] = place([P, T2], F32, f"page{c}", *page_place[c])
+            pages[c] = place([P, T2], F32, f"page{c}", f"page{c % LOWER}" if c < ROW_TILES - 1 else "shares0")
             rows = page0[c * P : (c + 1) * P, :] if c < LOWER else dealt_rows(page0[UPPER_ROW:, :], c - LOWER)
             nc.sync.dma_start(out=pages[c][:], in_=rows)
 
-        picked_sc = place([P, S], U8, "picked_sc", "drop0", -S // 2)
+        picked_sc = place([P, S], U8, "picked_sc", "low2", -S // 2)
         nc.vector.tensor_copy(picked_sc[:], tab_sc[:].indirect(idx[:]))
 
         def move_scale_rows(lo, hi):
@@ -156,35 +147,31 @@ def tile_list_fetal_slice_mosaic_kernel(
 
         move_scale_rows(0, S)
         load_page(0)
-        v_w = [place([P, S], U32, "v_w0", "x1"), place([P, S], U32, "v_w1", "x2")]
+        v_w = [place([P, S], U32, f"v_w{a}", f"low{a}") for a in range(PASSES)]
         nc.vector.tensor_copy(v_w[0][:], tab_w[0][:].bitcast(U32).indirect(idx[:]))
         wgs_sb = place([P, S], F32, "wgs_sb", "wgs")
         nc.sync.dma_start(out=wgs_sb[:, FIRST:S], in_=wgs[:, FIRST:S])
         nc.sync.dma_start(out=wgs_sb[:, 0:FIRST], in_=wgs[:, 0:FIRST])
         rest = H - head
-        w1_sc_rest = place([P, PASSES, rest], U8, "w1_sc_rest", "drop0", -PASSES * rest)
+        w1_sc_rest = place([P, PASSES, rest], U8, "w1_sc_rest", "low2", -PASSES * rest)
         nc.scalar.copy(out=w1_sc_rest[:].bitcast(U32), in_=zero_word[:].bitcast(U32).to_broadcast([P, PASSES, rest // 4]))
         load_w1_scales(w1_sc_rest, slice(head, H))
         for lo, hi in FIRST_PARTS:
             nc.vector.tensor_copy(v_w[1][:, lo:hi], tab_w[1][:].bitcast(U32).indirect(entries(idx, lo, hi)))
-        w1_rest = place([P, PASSES, 2 * rest], U8, "w1_rest", "drop0")
+        w1_rest = place([P, PASSES, 2 * rest], U8, "w1_rest", "low2")
         nc.sync.dma_start(out=w1_rest[:].bitcast(I32), in_=w1_view[:, :, 2 * head :].bitcast(I32))
-        load_page(1)
+        for c in range(1, LOWER):
+            load_page(c)
 
         wgs_dealt = {}
 
-        dealt_place = [("floors", EDGE), ("floors", EDGE + ROW), ("dealt2", EDGE), ("dealt3", -EDGE)]
-
         def load_wgs_dealt(t):
-            wgs_dealt[t] = place([P, S], F32, f"wgs_dealt{t}", *dealt_place[t])
+            wgs_dealt[t] = place([P, S], F32, f"wgs_dealt{t}", f"dealt{t}")
             for quad in range(QUADRANTS):
                 nc.sync.dma_start(out=wgs_dealt[t][QUADRANT * quad : QUADRANT * (quad + 1), 0:S], in_=dealt_rows(wgs, t))
 
-        load_wgs_dealt(0)
-        load_wgs_dealt(1)
-
-        w1_dealt = place([P, PASSES, PACK, 2 * P], U8, "w1_dealt", "w2_codes")
-        w1_sc_dealt = place([P, PASSES, PACK, P], U8, "w1_sc_dealt", "w2_codes", PASSES * PACK * 2 * P)
+        w1_dealt = place([P, PASSES, PACK, 2 * P], U8, "w1_dealt", "low3")
+        w1_sc_dealt = place([P, PASSES, PACK, P], U8, "w1_sc_dealt", "low3", PASSES * PACK * 2 * P)
 
         def deal_w1():
             upper = UPPER_ROW - head
@@ -209,7 +196,7 @@ def tile_list_fetal_slice_mosaic_kernel(
         used_banks = []
 
         def first_product(c):
-            h_sb[c] = place([P, S], F32, f"h{c}", *{2: ("raw2", EDGE), 3: ("low0", 0), 4: ("floors", EDGE + 2 * ROW)}.get(c, (f"h{c}", 0)))
+            h_sb[c] = place([P, S], F32, f"h{c}", f"h{c}")
             if c == 0:
                 parts = [(lo, hi, hi - lo) for lo, hi in FIRST_PARTS]
             else:
@@ -234,15 +221,11 @@ def tile_list_fetal_slice_mosaic_kernel(
                 else:
                     nc.scalar.copy(out=h_sb[c][:, lo:hi], in_=h_sum[:])
 
-        weighed_place = {
-            2: ("h2", 0), 3: ("h3", 0), 4: ("page0", EDGE), 5: ("page0", ROW + EDGE), 6: ("weighed6", EDGE), 7: ("raw2", 0),
-        }
-
         def weigh(c, lo=0, hi=S):
             weights = wgs_sb if c < LOWER else wgs_dealt[c - LOWER]
             plain = h_sb[c]
-            if c in weighed_place:
-                h_sb[c] = place([P, S], F32, f"weighed{c}", *weighed_place[c])
+            if c == ROW_TILES - 1:
+                h_sb[c] = place([P, S], F32, f"weighed{c}", f"weighed{c}")
             nc.gpsimd.tensor_tensor(h_sb[c][:, lo:hi], plain[:, lo:hi], weights[:, lo:hi], ALU.mult)
 
         def scatter(c, lo=0, hi=S):
@@ -253,32 +236,32 @@ def tile_list_fetal_slice_mosaic_kernel(
         ident_bf = own([P, P], BF16, "ident_bf")
 
         low_sb = {}
-        low_place = [("low0", 0), ("spare", EDGE), ("low2", -EDGE), ("low_part0", 0)]
 
         def load_low(c):
-            low_sb[c] = place([P, M], F32, f"low{c}", *low_place[c])
+            low_sb[c] = place([P, M], F32, f"low{c}", f"low{c}")
             nc.sync.dma_start(out=low_sb[c][:], in_=low[c * P : (c + 1) * P, :])
             nc.scalar.activation(out=low_sb[c][:], in_=low_sb[c][:], func=COPY, scale=-1.0)
 
         x = {}
 
+        x_place = [("dealt2", EDGE), ("dealt3", EDGE), ("h7", -EDGE), ("x3", -EDGE)]
+
         def gather(c):
+            x[c] = place([P, M], F32, f"x{c}", *x_place[c])[:]
             nc.vector.tensor_copy(x[c], pages[c][:].indirect(idx3[:]))
 
         kept, dropped = {}, {}
         blocks = BANK // P
-        sign_place = [("page4", 0), ("h0", 0), ("h0", ROW // 2), ("h0", 0)]
-        keep_place = [("keep0", 0), ("keep1", 0), ("dealt2", 0), ("last", 0)]
-        drop_place = [("drop0", 0), ("drop1", 0), ("dealt3", 0), ("last", ROW)]
 
         def add_turned(total, terms):
             for i, term in enumerate(terms):
                 nc.tensor.matmul(total, term, ident[:], start=(i == 0), stop=(i == len(terms) - 1), is_transpose=True)
 
         def compare(c):
-            sign = place([P, M // P, P], BF16, f"sign{c}", *sign_place[c])
-            kept[c] = place([P, M], F32, f"keep{c}", *keep_place[c])
-            dropped[c] = place([P, M], F32, f"drop{c}", *drop_place[c])
+            sign = place([P, M // P, P], BF16, f"sign{c}", "floors", c * ROW)
+            shift = EDGE if c == LOWER - 1 else 0
+            kept[c] = place([P, M], F32, f"keep{c}", f"shares{c}", shift)
+            dropped[c] = place([P, M], F32, f"drop{c}", f"shares{c}", ROW + shift)
             for half in range(M // BANK):
                 gap = bank([P, blocks, P], f"bank{half}")
                 for b in range(blocks):
@@ -296,9 +279,9 @@ def tile_list_fetal_slice_mosaic_kernel(
         x_part, low_part = {}, {}
 
         def choose(c, lo=0, hi=M):
-            x_part[c] = place([P, M], F32, "x_part2", "page3", -EDGE)[:] if c == 2 else x[c]
+            x_part[c] = place([P, M], F32, "x_part0", "page3")[:] if c == 0 else x[c]
             nc.gpsimd.tensor_tensor(x_part[c][:, lo:hi], x[c][:, lo:hi], kept[c][:, lo:hi], ALU.mult)
-            low_part[c] = place([P, M], F32, "low_part0", "low_part0") if c == 0 else low_sb[c]
+            low_part[c] = place([P, M], F32, "low_part0", "page3", ROW) if c == 0 else low_sb[c]
             nc.gpsimd.tensor_tensor(low_part[c][:, lo:hi], low_sb[c][:, lo:hi], dropped[c][:, lo:hi], ALU.mult)
 
         z_t = [place([P, blocks, 2, P], F32, f"z_t{half}", f"z_t{half}") for half in range(M // BANK)]
@@ -317,25 +300,18 @@ def tile_list_fetal_slice_mosaic_kernel(
                 )
 
         w2_codes = place([P, PASSES, N], U32, "w2_codes", "w2_codes")
-        w2_sc = place([P, PASSES, N], U8, "w2_sc", "drop1", EDGE)
-        w2_bf = {}
+        w2_sc = place([P, PASSES, N], U8, "w2_sc", "w2_sc")
+        w2_bf = place([P, PASSES, N, PACK], BF16, "w2_bf", "w2_bf")
 
         def round_w2(g):
-            w2_rows = place([P, PACK, N], F32, f"w2_rows{g}", "page4", 2 * ROW * (g - 1))
+            w2_rows = place([P, PACK, N], F32, f"w2_rows{g}", f"shares{g + 1}")
             rows = w2[g * UPPER_ROW : (g + 1) * UPPER_ROW, :]
             if g == 0:
                 nc.sync.dma_start(out=w2_rows[:], in_=rows.rearrange("(p t) n -> p t n", t=PACK))
             else:
-                load_planes(w2_rows, rows)
-            w2_bf[g] = place([P, N, PACK], BF16, f"w2_bf{g}", "w2_bf", ROW * g)
-            nc.scalar.copy(out=w2_bf[g][:], in_=w2_rows[:].rearrange("p t n -> p n t"))
-
-        def quantise_w2(g):
-            nc.vector.quantize_mx(
-                out=w2_codes[:, g, :].bitcast(FP8X4),
-                scales=w2_sc[:, g, :],
-                in_=w2_bf[g][:].rearrange("p n t -> p (n t)"),
-            )
+                for t in range(PACK):
+                    nc.sync.dma_start(out=w2_rows[:, t, :], in_=dealt_rows(rows, t))
+            nc.scalar.copy(out=w2_bf[:, g, :, :], in_=w2_rows[:].rearrange("p t n -> p n t"))
 
         first_product(0)
         first_product(1)
@@ -353,83 +329,54 @@ def tile_list_fetal_slice_mosaic_kernel(
                     out=bias_sb[e:P:RUN, 1, 0:PACK],
                     in_=bias[UPPER_ROW:].rearrange("(a t e) -> e a t", t=PACK, e=RUN)[e],
                 )
-        for c in (2, 3):
+        for t in range(PACK):
+            load_wgs_dealt(t)
+        for c in range(HEAD_TILES, LOWER):
             first_product(c)
             weigh(c)
+            scatter(c)
         deal_w1()
         for c in range(LOWER, ROW_TILES):
             first_product(c)
+            weigh(c)
         nc.scalar.copy(out=ident_bf[:], in_=ident[:])
         bias_blocks = own([P, LOWER, P], F32, "bias_blocks")
         nc.scalar.activation(
             out=bias_blocks[:], in_=bias_sb[:, 0, 0:PACK].unsqueeze(2).to_broadcast([P, LOWER, P]), func=COPY, scale=-1.0
         )
-        neg_bias = place([P, PACK], F32, "neg_bias", "h0")
+        neg_bias = own([P, PACK], F32, "neg_bias")
         nc.scalar.activation(out=neg_bias[:], in_=bias_sb[:, 1, 0:PACK], func=COPY, scale=-1.0)
-        for g in range(PASSES):
-            round_w2(g)
-        load_page(2)
-        load_low(0)
-        load_page(3)
-        x0 = place([P, M], F32, "x0", "wgs")
-        x[0] = x0[:]
-        gather(0)
+        for c in range(LOWER):
+            load_low(c)
+        bias_wide = own([P, PACK, BANK], F32, "bias_wide")
+        nc.scalar.copy(out=bias_wide[:], in_=bias_sb[:, 1, 0:PACK].unsqueeze(2).to_broadcast([P, PACK, BANK]))
 
-        compare(0)
-        scatter(2)
-        weigh(4)
-        weigh(5)
-        scatter(3)
-        choose(0)
-        floors = place([P, PACK, M], F32, "floors", "floors", EDGE)
+        for c in range(LOWER):
+            gather(c)
+        for c in range(LOWER):
+            compare(c)
+        for c in range(LOWER):
+            choose(c)
+            load_page(LOWER + c)
+            scatter(LOWER + c)
+            add_up(c)
+        floors = place([P, PACK, M], F32, "floors", "floors")
         for t in range(PACK):
             nc.sync.dma_start(out=floors[:, t, :], in_=dealt_rows(low[UPPER_ROW:, :], t))
             nc.scalar.activation(out=floors[:, t, :], in_=floors[:, t, :], func=IDENTITY, bias=neg_bias[:, t : t + 1])
-        bias_wide = own([P, PACK, BANK], F32, "bias_wide")
-        nc.scalar.copy(out=bias_wide[:], in_=bias_sb[:, 1, 0:PACK].unsqueeze(2).to_broadcast([P, PACK, BANK]))
-        load_wgs_dealt(2)
-        load_wgs_dealt(3)
-        load_page(4)
-        load_low(1)
-        load_page(5)
-        load_low(2)
-        x1 = place([P, M], F32, "x1", "bias", 5 * EDGE - ROW)
-        x2 = place([P, M], F32, "x2", "x2", -EDGE)
-        x[1], x[2] = x1[:], x2[:]
-        gather(1)
-        gather(2)
-
-        compare(1)
-        weigh(6)
-        weigh(7)
-        add_up(0)
-        scatter(4)
-        scatter(5)
-        choose(1)
-        compare(2)
-        load_low(3)
-        load_page(6)
-        load_page(7)
-        x3 = place([P, M], F32, "x3", "x3", EDGE)
-        x[3] = x3[:]
-        gather(3)
         for g in range(PASSES):
-            quantise_w2(g)
-
-        compare(3)
-        add_up(1)
-        scatter(6)
-        scatter(7)
-        choose(2)
-        choose(3, 0, BANK)
-        choose(3, BANK, M)
-        add_up(2)
+            round_w2(g)
+        nc.vector.quantize_mx(
+            out=w2_codes[:].rearrange("p g n -> p (g n)").bitcast(FP8X4),
+            scales=w2_sc[:].rearrange("p g n -> p (g n)"),
+            in_=w2_bf[:].rearrange("p g n t -> p (g n t)"),
+        )
 
         z_sc = [own([P, M], U8, f"z_sc{g}") for g in range(PASSES)]
         woven_lower = {}
 
         def weave_lower(lo, hi):
-            woven_lower[lo] = place([P, (hi - lo) * PACK], BF16, f"woven0_{lo}", "w2_bf", lo * PACK * 2)
+            woven_lower[lo] = place([P, (hi - lo) * PACK], BF16, f"woven0_{lo}", "h0", lo * PACK * 2)
             for at in range(lo, hi, PIECE):
                 back = bank([P, PIECE // P, 2, P], f"back{at // PIECE % 2}")
                 for b in range(PIECE // P):
@@ -441,16 +388,13 @@ def tile_list_fetal_slice_mosaic_kernel(
                     in_=back[:].rearrange("p b u m -> p b m u"),
                 )
 
-        add_up(3, (0,))
-        weave_lower(*PIECES[0])
-        add_up(3, (1,))
-        for lo, hi in PIECES[1:]:
+        for lo, hi in PIECES:
             weave_lower(lo, hi)
 
         z_codes = {}
 
         def quantise(g, lo, hi, woven):
-            region, shift = (("wgs", 0), ("spare", 0))[g]
+            region, shift = (("wgs", 0), ("h2", 0))[g]
             z_codes[(g, lo)] = place([P, hi - lo], U32, f"z_codes{g}_{lo}", region, shift + 4 * lo)
             nc.vector.quantize_mx(out=z_codes[(g, lo)][:].bitcast(FP8X4), scales=z_sc[g][:, lo:hi], in_=woven)
 
@@ -482,7 +426,7 @@ def tile_list_fetal_slice_mosaic_kernel(
                         )
                 sums[(span, number)] = out_sum
 
-        result_place = [("page0", EDGE), ("h3", 0), ("low3", 0), ("low3", ROW // 2)]
+        result_place = [("w2_bf", 0), ("h3", 0), ("h4", 0), ("h4", ROW // 2)]
 
         def store(span, engine_copies):
             lo, hi = SPANS[span]
@@ -493,7 +437,7 @@ def tile_list_fetal_slice_mosaic_kernel(
                 engine_copies[number % 2](out=result[:], in_=sums[(span, number)][:])
                 nc.sync.dma_start(out=out_view[:, group[0] : group[-1] + 1, lo:hi], in_=result[:])
 
-        shifted_place = [("last", 0), ("z_t0", 0), ("z_t1", 0)]
+        shifted_place = [("shares3", 0), ("z_t0", 0), ("z_t1", 0)]
         shifted = [
             place([P, PACK, hi - lo], F32, f"shifted{piece}", *shifted_place[piece]) for piece, (lo, hi) in enumerate(PIECES)
         ]
@@ -511,7 +455,7 @@ def tile_list_fetal_slice_mosaic_kernel(
             lo, hi = SPANS[span]
             piece = min(span, len(PIECES) - 1)
             at = PIECES[piece][0]
-            region, shift = ("low_part0", 0) if span == 0 else ("h6", (lo - BANK) * PACK * 2)
+            region, shift = ("low3", 0) if span == 0 else ("h5", (lo - BANK) * PACK * 2)
             woven = place([P, hi - lo, PACK], BF16, f"woven1_{lo}", region, shift)
             nc.vector.tensor_tensor(
                 woven[:].rearrange("p (c i) t -> p c t i", i=PACK),

@@ -145,8 +145,9 @@ def tile_list_fetal_slice_mosaic_kernel(
                         in_=picked_sc[first : first + HALF, lo:hi].bitcast(I32),
                     )
 
-        move_scale_rows(0, S)
+        move_scale_rows(0, FIRST)
         load_page(0)
+        move_scale_rows(FIRST, S)
         v_w = [place([P, S], U32, f"v_w{a}", f"low{a}") for a in range(PASSES)]
         nc.vector.tensor_copy(v_w[0][:], tab_w[0][:].bitcast(U32).indirect(idx[:]))
         wgs_sb = place([P, S], F32, "wgs_sb", "wgs")

@@ -42,11 +42,11 @@ SPANS = [(0, BANK), (BANK, M - PIECE), (M - PIECE, M - P), (M - P, M)]
 ROW = 4 * M
 EDGE = 64
 REGIONS = [
-    ("page0", 2 * ROW), ("page1", 2 * ROW), ("page2", 2 * ROW), ("bias", ROW // 4), ("page3", 2 * ROW),
+    ("page0", 2 * ROW), ("page1", 2 * ROW), ("wgs", ROW), ("page2", 2 * ROW), ("bias", ROW // 4), ("page3", 2 * ROW),
     ("dealt0", ROW), ("dealt1", ROW), ("dealt2", ROW), ("dealt3", ROW + 2 * EDGE), ("h7", ROW), ("x3", ROW),
     ("shares0", 2 * ROW), ("shares1", 2 * ROW), ("shares2", 2 * ROW), ("shares3", 2 * ROW), ("w2_sc", ROW // 4),
     ("low0", ROW), ("low1", ROW), ("scales", ROW // 2), ("low2", ROW), ("low3", ROW), ("floors", 4 * ROW),
-    ("w2_codes", ROW), ("wgs", ROW),
+    ("w2_codes", ROW),
     ("h0", ROW), ("h1", ROW), ("h2", ROW), ("h3", ROW), ("h4", ROW), ("h5", ROW), ("h6", ROW), ("weighed7", ROW),
     ("z_t0", ROW), ("z_t1", ROW), ("w2_bf", 2 * ROW),
 ]
@@ -107,7 +107,7 @@ def tile_list_fetal_slice_mosaic_kernel(
                     in_=rows.rearrange("a r c -> r a c").bitcast(I32),
                 )
 
-        tab_w = [place([P, T], I32, "tab_w0", "w2_codes"), place([P, T], I32, "tab_w1", "page1", ROW)]
+        tab_w = [place([P, T], I32, "tab_w0", "page1", ROW), place([P, T], I32, "tab_w1", "page2", ROW)]
 
         def load_words(a):
             nc.sync.dma_start(out=tab_w[a][:], in_=tab_words[a].rearrange("p t i -> p (t i)").bitcast(I32))
@@ -117,7 +117,7 @@ def tile_list_fetal_slice_mosaic_kernel(
         w1_view = w1_words.rearrange("a p c -> p a c")
         w1_first = place([P, PASSES, 2 * head], U8, "w1_first", "dealt1", -2 * head)
         nc.sync.dma_start(out=w1_first[:].bitcast(I32), in_=w1_view[:, :, 0 : 2 * head].bitcast(I32))
-        wgs_first = place([P, FIRST], F32, "wgs_first", "bias")
+        wgs_first = place([P, FIRST], F32, "wgs_first", "w2_codes")
         nc.sync.dma_start(out=wgs_first[:], in_=wgs[:, 0:FIRST])
         load_words(0)
         load_w1_scales(w1_sc_first, slice(0, head))
@@ -150,6 +150,7 @@ def tile_list_fetal_slice_mosaic_kernel(
         move_scale_rows(FIRST, S)
         v_w = [place([P, S], U32, f"v_w{a}", f"low{a}") for a in range(PASSES)]
         nc.vector.tensor_copy(v_w[0][:], tab_w[0][:].bitcast(U32).indirect(idx[:]))
+        load_page(1)
         wgs_sb = place([P, S], F32, "wgs_sb", "wgs")
         nc.sync.dma_start(out=wgs_sb[:, FIRST:S], in_=wgs[:, FIRST:S])
         nc.sync.dma_start(out=wgs_sb[:, 0:FIRST], in_=wgs[:, 0:FIRST])
@@ -161,7 +162,7 @@ def tile_list_fetal_slice_mosaic_kernel(
             nc.vector.tensor_copy(v_w[1][:, lo:hi], tab_w[1][:].bitcast(U32).indirect(entries(idx, lo, hi)))
         w1_rest = place([P, PASSES, 2 * rest], U8, "w1_rest", "low2")
         nc.sync.dma_start(out=w1_rest[:].bitcast(I32), in_=w1_view[:, :, 2 * head :].bitcast(I32))
-        for c in range(1, LOWER):
+        for c in range(HEAD_TILES, LOWER):
             load_page(c)
 
         wgs_dealt = {}
@@ -223,7 +224,7 @@ def tile_list_fetal_slice_mosaic_kernel(
                     nc.scalar.copy(out=h_sb[c][:, lo:hi], in_=h_sum[:])
 
         def weigh(c, lo=0, hi=S):
-            weights = wgs_sb if c < LOWER else wgs_dealt[c - LOWER]
+            weights = wgs_first if hi == FIRST else wgs_sb if c < LOWER else wgs_dealt[c - LOWER]
             plain = h_sb[c]
             if c == ROW_TILES - 1:
                 h_sb[c] = place([P, S], F32, f"weighed{c}", f"weighed{c}")
@@ -236,12 +237,16 @@ def tile_list_fetal_slice_mosaic_kernel(
         make_identity(nc, ident[:])
         ident_bf = own([P, P], BF16, "ident_bf")
 
-        low_sb = {}
+        low_sb, bias_row = {}, {}
 
         def load_low(c):
             low_sb[c] = place([P, M], F32, f"low{c}", f"low{c}")
             nc.sync.dma_start(out=low_sb[c][:], in_=low[c * P : (c + 1) * P, :])
-            nc.scalar.activation(out=low_sb[c][:], in_=low_sb[c][:], func=COPY, scale=-1.0)
+            nc.scalar.activation(
+                out=low_sb[c][:], in_=low_sb[c][:], func=IDENTITY, scale=-1.0, bias=bias_sb[:, 0, c : c + 1]
+            )
+            bias_row[c] = place([P, M], F32, f"bias_row{c}", f"shares{c}", ROW)
+            nc.scalar.copy(out=bias_row[c][:], in_=bias_sb[:, 0, c : c + 1].to_broadcast([P, M]))
 
         x = {}
 
@@ -249,7 +254,7 @@ def tile_list_fetal_slice_mosaic_kernel(
 
         def gather(c):
             x[c] = place([P, M], F32, f"x{c}", *x_place[c])[:]
-            nc.vector.tensor_copy(x[c], pages[c][:].indirect(idx3[:]))
+            nc.vector.tensor_tensor(x[c], pages[c][:].indirect(idx3[:]), bias_row[c][:], ALU.subtract)
 
         kept, dropped = {}, {}
         blocks = BANK // P
@@ -293,7 +298,7 @@ def tile_list_fetal_slice_mosaic_kernel(
                 z_sum = bank([P, blocks, P], f"sum{half}")
                 for b in range(blocks):
                     cols = slice(half * BANK + b * P, half * BANK + (b + 1) * P)
-                    add_turned(z_sum[:, b, :], [x_part[c][:, cols], low_part[c][:, cols], bias_blocks[:, c, :]])
+                    add_turned(z_sum[:, b, :], [x_part[c][:, cols], low_part[c][:, cols]])
                 pairs = z_t[half][:, :, :, share * c : share * (c + 1)].bitcast(BF16)
                 nc.scalar.copy(
                     out=pairs.rearrange("m b u (l e) -> m b u l e", e=2),
@@ -316,12 +321,11 @@ def tile_list_fetal_slice_mosaic_kernel(
 
         first_product(0)
         first_product(1)
-        scatter(0, *FIRST_PARTS[0])
-        for lo, hi in FIRST_PARTS[1:]:
-            weigh(0, lo, hi)
-            scatter(0, lo, hi)
-        weigh(1)
-        scatter(1)
+        for lo, hi in FIRST_PARTS:
+            for c in range(HEAD_TILES):
+                if (c, lo) != (0, 0):
+                    weigh(c, lo, hi)
+                scatter(c, lo, hi)
         bias_sb = place([P, PASSES, 4 * PACK], F32, "bias_sb", "bias")
         with nc.allow_non_contiguous_dma(reason="one value of the bias for each partition and row tile"):
             nc.sync.dma_start(out=bias_sb[:, 0, 0:PACK], in_=bias[0:UPPER_ROW].rearrange("(c p) -> p c", p=P))
@@ -341,10 +345,6 @@ def tile_list_fetal_slice_mosaic_kernel(
             first_product(c)
             weigh(c)
         nc.scalar.copy(out=ident_bf[:], in_=ident[:])
-        bias_blocks = own([P, LOWER, P], F32, "bias_blocks")
-        nc.scalar.activation(
-            out=bias_blocks[:], in_=bias_sb[:, 0, 0:PACK].unsqueeze(2).to_broadcast([P, LOWER, P]), func=COPY, scale=-1.0
-        )
         neg_bias = own([P, PACK], F32, "neg_bias")
         nc.scalar.activation(out=neg_bias[:], in_=bias_sb[:, 1, 0:PACK], func=COPY, scale=-1.0)
         for c in range(LOWER):

@@ -116,12 +116,13 @@ def tile_list_fetal_slice_mosaic_kernel(
         nc.sync.dma_start(idx3[:], offs3)
         w1_view = w1_words.rearrange("a p c -> p a c")
         w1_first = place([P, PASSES, 2 * head], U8, "w1_first", "dealt1", -2 * head)
-        nc.sync.dma_start(out=w1_first[:].bitcast(I32), in_=w1_view[:, :, 0 : 2 * head].bitcast(I32))
-        wgs_first = place([P, FIRST], F32, "wgs_first", "w2_codes")
-        nc.sync.dma_start(out=wgs_first[:], in_=wgs[:, 0:FIRST])
+        for a in range(PASSES):
+            nc.sync.dma_start(out=w1_first[:, a, :].bitcast(I32), in_=w1_view[:, a, 0 : 2 * head].bitcast(I32))
         load_words(0)
         load_w1_scales(w1_sc_first, slice(0, head))
         load_words(1)
+        wgs_first = place([P, FIRST], F32, "wgs_first", "w2_codes")
+        nc.sync.dma_start(out=wgs_first[:], in_=wgs[:, 0:FIRST])
 
         def dealt_rows(rows, t):
             return rows.rearrange("(a t e) c -> t a e c", t=PACK, e=RUN)[t]

from contextlib import ExitStack

import concourse.mybir as mybir
from concourse.masks import make_identity

K, T, S, H, T2, M, N = 1024, 2048, 1024, 1024, 2048, 1024, 512
FLOPS = 2 * K * H * S + 2 * H * N * M

F32 = mybir.dt.float32
BF16 = mybir.dt.bfloat16
I32 = mybir.dt.int32
U32 = mybir.dt.uint32
U16 = mybir.dt.uint16
U8 = mybir.dt.uint8
FP8X4 = mybir.dt.float8_e4m3fn_x4
FP4X4 = mybir.dt.float4_e2m1fn_x4
ALU = mybir.AluOpType
IDENTITY = mybir.ActivationFunctionType.Identity
COPY = mybir.ActivationFunctionType.Copy
SIGN = mybir.ActivationFunctionType.Sign

P = 128
PACK = 4
RUN = 2
QUADRANT = 32
QUADRANTS = P // QUADRANT
PER_COLUMN = 16
BANK = 512
PASSES = 2
ROW_TILES = H // P
LOWER = ROW_TILES // PASSES
UPPER_ROW = LOWER * P
PIECE = 256
HALF = P // 2
SCALE_ROW = 16
FIRST = BANK
FIRST_PARTS = [(0, FIRST), (FIRST, S)]
HEAD_TILES = 2
PIECES = [(0, BANK), (BANK, M - PIECE), (M - PIECE, M)]
SPANS = [(0, BANK), (BANK, M - PIECE), (M - PIECE, M - P), (M - P, M)]

ROW = 4 * M
EDGE = 64
REGIONS = [
    ("page0", 2 * ROW), ("page1", 2 * ROW), ("wgs", ROW), ("page2", 2 * ROW), ("bias", ROW // 4), ("page3", 2 * ROW),
    ("dealt0", ROW), ("dealt1", ROW), ("dealt2", ROW), ("dealt3", ROW + 2 * EDGE), ("h7", ROW), ("x3", ROW),
    ("shares0", 2 * ROW), ("shares1", 2 * ROW), ("shares2", 2 * ROW), ("shares3", 2 * ROW), ("w2_sc", ROW // 4),
    ("low0", ROW), ("low1", ROW), ("scales", ROW // 2), ("low2", ROW), ("low3", ROW), ("floors", 4 * ROW),
    ("w2_codes", ROW),
    ("h0", ROW), ("h1", ROW), ("h2", ROW), ("h3", ROW), ("h4", ROW), ("h5", ROW), ("h6", ROW), ("weighed7", ROW),
    ("z_t0", ROW), ("z_t1", ROW), ("w2_bf", 2 * ROW),
]
START = {name: sum(size for other, size in REGIONS[:i]) for i, (name, size) in enumerate(REGIONS)}


def tile_list_fetal_slice_mosaic_kernel(
    tc, tab_words, tab_scales, offs, w1_words, w1_scales, wgs, page0, offs2, offs3, low, bias, w2, out
):
    nc = tc.nc
    with ExitStack() as ctx:
        lists = ctx.enter_context(tc.tile_pool(name="lists", bufs=1))
        keep = ctx.enter_context(tc.tile_pool(name="keep", bufs=1))
        placed = ctx.enter_context(tc.tile_pool(name="placed", bufs=1))
        banks = ctx.enter_context(tc.psum_pool(name="banks", bufs=1))

        def own(shape, dtype, name):
            return keep.tile(shape, dtype, name=name, align_bytes=64)

        def place(shape, dtype, name, region, shift=0):
            return placed.tile(shape, dtype, name=name, align_bytes=64, offset=START[region] + shift)

        def bank(shape, tag):
            return banks.tile(shape, F32, name=tag, tag=tag)

        idx = lists.tile([P, S // PER_COLUMN], U16, name="idx")
        idx2 = lists.tile([P, S // PER_COLUMN], U16, name="idx2")
        idx3 = lists.tile([P, M // PER_COLUMN], U16, name="idx3")

        def entries(listed, lo, hi):
            return listed[:, lo // PER_COLUMN : hi // PER_COLUMN]

        head = HEAD_TILES * P
        w1_sc_first = place([P, PASSES, head], U8, "w1_sc_first", "dealt3", -head)
        nc.vector.memset(w1_sc_first[:].bitcast(I32), 0)
        nc.sync.dma_start(idx[:], offs)
        tab_sc = place([P, T], U8, "tab_sc", "page0")
        rows_by_parity = tab_scales.rearrange("a (h o r) c -> o (a h) r c", o=2, r=PACK)
        for o in range(2):
            base = QUADRANT * o
            nc.sync.dma_start(
                out=tab_sc[base + SCALE_ROW : base + QUADRANT, :].bitcast(I32), in_=rows_by_parity[o].bitcast(I32)
            )
            nc.vector.memset(tab_sc[base : base + SCALE_ROW, :].bitcast(I32), 0)
        nc.vector.memset(tab_sc[HALF:P, :].bitcast(I32), 0)
        zero_word = own([P, 1, 1], I32, "zero_word")
        nc.vector.memset(zero_word[:], 0)
        v_sc = own([P, PASSES, S], U8, "v_sc")

        def v_scale(a, lo, hi):
            return v_sc[:, a, lo:hi]

        def load_w1_scales(planes, cols):
            for quad in range(QUADRANTS):
                rows = w1_scales[:, PACK * quad : PACK * (quad + 1), cols]
                nc.sync.dma_start(
                    out=planes[QUADRANT * quad : QUADRANT * quad + PACK, :, :].bitcast(I32),
                    in_=rows.rearrange("a r c -> r a c").bitcast(I32),
                )

        tab_w = [place([P, T], I32, "tab_w0", "page1", ROW), place([P, T], I32, "tab_w1", "page2", ROW)]

        def load_words(a):
            nc.sync.dma_start(out=tab_w[a][:], in_=tab_words[a].rearrange("p t i -> p (t i)").bitcast(I32))

        nc.sync.dma_start(idx2[:], offs2)
        nc.sync.dma_start(idx3[:], offs3)
        w1_view = w1_words.rearrange("a p c -> p a c")
        w1_first = place([P, PASSES, 2 * head], U8, "w1_first", "dealt1", -2 * head)
        for a in range(PASSES):
            nc.sync.dma_start(out=w1_first[:, a, :].bitcast(I32), in_=w1_view[:, a, 0 : 2 * head].bitcast(I32))
        load_words(0)
        load_w1_scales(w1_sc_first, slice(0, head))
        load_words(1)
        wgs_first = place([P, FIRST], F32, "wgs_first", "w2_codes")
        nc.sync.dma_start(out=wgs_first[:], in_=wgs[:, 0:FIRST])

        def dealt_rows(rows, t):
            return rows.rearrange("(a t e) c -> t a e c", t=PACK, e=RUN)[t]

        pages = {}

        def load_page(c):
            pages[c] = place([P, T2], F32, f"page{c}", f"page{c % LOWER}" if c < ROW_TILES - 1 else "shares0")
            rows = page0[c * P : (c + 1) * P, :] if c < LOWER else dealt_rows(page0[UPPER_ROW:, :], c - LOWER)
            nc.sync.dma_start(out=pages[c][:], in_=rows)

        picked_sc = place([P, S], U8, "picked_sc", "low2", -S // 2)
        nc.vector.tensor_copy(picked_sc[:], tab_sc[:].indirect(idx[:]))

        def move_scale_rows(lo, hi):
            for a in range(PASSES):
                for h in range(2):
                    first = SCALE_ROW + PACK * (2 * a + h)
                    nc.sync.dma_start(
                        out=v_scale(a, lo, hi)[HALF * h : HALF * (h + 1), :].bitcast(I32),
                        in_=picked_sc[first : first + HALF, lo:hi].bitcast(I32),
                    )

        move_scale_rows(0, FIRST)
        load_page(0)
        move_scale_rows(FIRST, S)
        v_w = [place([P, S], U32, f"v_w{a}", f"low{a}") for a in range(PASSES)]
        nc.vector.tensor_copy(v_w[0][:], tab_w[0][:].bitcast(U32).indirect(idx[:]))
        load_page(1)
        wgs_sb = place([P, S], F32, "wgs_sb", "wgs")
        nc.sync.dma_start(out=wgs_sb[:, FIRST:S], in_=wgs[:, FIRST:S])
        nc.sync.dma_start(out=wgs_sb[:, 0:FIRST], in_=wgs[:, 0:FIRST])
        rest = H - head
        w1_sc_rest = place([P, PASSES, rest], U8, "w1_sc_rest", "low2", -PASSES * rest)
        nc.scalar.copy(out=w1_sc_rest[:].bitcast(U32), in_=zero_word[:].bitcast(U32).to_broadcast([P, PASSES, rest // 4]))
        load_w1_scales(w1_sc_rest, slice(head, H))
        for lo, hi in FIRST_PARTS:
            nc.vector.tensor_copy(v_w[1][:, lo:hi], tab_w[1][:].bitcast(U32).indirect(entries(idx, lo, hi)))
        w1_rest = place([P, PASSES, 2 * rest], U8, "w1_rest", "low2")
        nc.sync.dma_start(out=w1_rest[:].bitcast(I32), in_=w1_view[:, :, 2 * head :].bitcast(I32))
        for c in range(HEAD_TILES, LOWER):
            load_page(c)

        wgs_dealt = {}

        def load_wgs_dealt(t):
            wgs_dealt[t] = place([P, S], F32, f"wgs_dealt{t}", f"dealt{t}")
            for quad in range(QUADRANTS):
                nc.sync.dma_start(out=wgs_dealt[t][QUADRANT * quad : QUADRANT * (quad + 1), 0:S], in_=dealt_rows(wgs, t))

        w1_dealt = place([P, PASSES, PACK, 2 * P], U8, "w1_dealt", "low3")
        w1_sc_dealt = place([P, PASSES, PACK, P], U8, "w1_sc_dealt", "low3", PASSES * PACK * 2 * P)

        def deal_w1():
            upper = UPPER_ROW - head
            nc.scalar.copy(
                out=w1_dealt[:].bitcast(U32),
                in_=w1_rest[:, :, 2 * upper :].bitcast(U32).rearrange("p g (a t) -> p g t a", t=PACK),
            )
            nc.scalar.copy(
                out=w1_sc_dealt[:].bitcast(U16),
                in_=w1_sc_rest[:, :, upper:].bitcast(U16).rearrange("p g (a t) -> p g t a", t=PACK),
            )

        def w1_tile(c, a):
            if c < HEAD_TILES:
                return w1_first[:, a, 2 * P * c : 2 * P * (c + 1)], w1_sc_first[:, a, P * c : P * (c + 1)]
            if c < LOWER:
                i = c - HEAD_TILES
                return w1_rest[:, a, 2 * P * i : 2 * P * (i + 1)], w1_sc_rest[:, a, P * i : P * (i + 1)]
            return w1_dealt[:, a, c - LOWER, :], w1_sc_dealt[:, a, c - LOWER, :]

        h_sb = {}
        used_banks = []

        def first_product(c):
            h_sb[c] = place([P, S], F32, f"h{c}", f"h{c}")
            if c == 0:
                parts = [(lo, hi, hi - lo) for lo, hi in FIRST_PARTS]
            else:
                parts = [(0, BANK, BANK), (BANK, S, BANK)]
            for lo, hi, width in parts:
                used_banks.append(c)
                h_sum = bank([P, hi - lo], f"bank{len(used_banks) % 4}")
                for at in range(lo, hi, width):
                    for a in range(PASSES):
                        w1_codes, w1_scale = w1_tile(c, a)
                        nc.tensor.matmul_mx(
                            out=h_sum[:, at - lo : at - lo + width],
                            lhsT=w1_codes.bitcast(FP4X4),
                            lhsT_scale=w1_scale,
                            rhs=v_w[a][:, at : at + width].bitcast(FP8X4),
                            rhs_scale=v_scale(a, at, at + width),
                            start=(a == 0),
                            stop=(a == PASSES - 1),
                        )
                if c == 0 and lo == 0:
                    nc.vector.tensor_tensor(h_sb[c][:, lo:hi], h_sum[:], wgs_first[:], ALU.mult)
                else:
                    nc.scalar.copy(out=h_sb[c][:, lo:hi], in_=h_sum[:])

        def weigh(c, lo=0, hi=S):
            weights = wgs_first if hi == FIRST else wgs_sb if c < LOWER else wgs_dealt[c - LOWER]
            plain = h_sb[c]
            if c == ROW_TILES - 1:
                h_sb[c] = place([P, S], F32, f"weighed{c}", f"weighed{c}")
            nc.gpsimd.tensor_tensor(h_sb[c][:, lo:hi], plain[:, lo:hi], weights[:, lo:hi], ALU.mult)

        def scatter(c, lo=0, hi=S):
            nc.vector.tensor_copy(pages[c][:].indirect(entries(idx2, lo, hi)), h_sb[c][:, lo:hi])

        ident = own([P, P], F32, "ident")
        make_identity(nc, ident[:])
        ident_bf = own([P, P], BF16, "ident_bf")

        low_sb, bias_row = {}, {}

        def load_low(c):
            low_sb[c] = place([P, M], F32, f"low{c}", f"low{c}")
            nc.sync.dma_start(out=low_sb[c][:], in_=low[c * P : (c + 1) * P, :])
            nc.scalar.activation(
                out=low_sb[c][:], in_=low_sb[c][:], func=IDENTITY, scale=-1.0, bias=bias_sb[:, 0, c : c + 1]
            )
            bias_row[c] = place([P, M], F32, f"bias_row{c}", f"shares{c}", ROW)
            nc.scalar.copy(out=bias_row[c][:], in_=bias_sb[:, 0, c : c + 1].to_broadcast([P, M]))

        x = {}

        x_place = [("dealt2", EDGE), ("dealt3", EDGE), ("h7", -EDGE), ("x3", -EDGE)]

        def gather(c):
            x[c] = place([P, M], F32, f"x{c}", *x_place[c])[:]
            nc.vector.tensor_tensor(x[c], pages[c][:].indirect(idx3[:]), bias_row[c][:], ALU.subtract)

        kept, dropped = {}, {}
        blocks = BANK // P

        def add_turned(total, terms):
            for i, term in enumerate(terms):
                nc.tensor.matmul(total, term, ident[:], start=(i == 0), stop=(i == len(terms) - 1), is_transpose=True)

        def compare(c):
            sign = place([P, M // P, P], BF16, f"sign{c}", "floors", c * ROW)
            shift = EDGE if c == LOWER - 1 else 0
            kept[c] = place([P, M], F32, f"keep{c}", f"shares{c}", shift)
            dropped[c] = place([P, M], F32, f"drop{c}", f"shares{c}", ROW + shift)
            for half in range(M // BANK):
                gap = bank([P, blocks, P], f"bank{half}")
                for b in range(blocks):
                    cols = slice(half * BANK + b * P, half * BANK + (b + 1) * P)
                    add_turned(gap[:, b, :], [x[c][:, cols], low_sb[c][:, cols]])
                nc.scalar.activation(out=sign[:, half * blocks : (half + 1) * blocks, :], in_=gap[:], func=SIGN)
            for half in range(M // BANK):
                back = banks.tile([P, BANK], BF16, name="sign_back", tag=f"bank{2 + half}")
                for b in range(blocks):
                    nc.tensor.transpose(back[:, b * P : (b + 1) * P], sign[:, half * blocks + b, :], ident_bf[:])
                cols = slice(half * BANK, (half + 1) * BANK)
                nc.scalar.activation(out=kept[c][:, cols], in_=back[:], func=COPY, scale=0.5, bias=0.5)
                nc.scalar.activation(out=dropped[c][:, cols], in_=back[:], func=COPY, scale=0.5, bias=-0.5)

        x_part, low_part = {}, {}

        def choose(c, lo=0, hi=M):
            x_part[c] = place([P, M], F32, "x_part0", "page3")[:] if c == 0 else x[c]
            nc.gpsimd.tensor_tensor(x_part[c][:, lo:hi], x[c][:, lo:hi], kept[c][:, lo:hi], ALU.mult)
            low_part[c] = place([P, M], F32, "low_part0", "page3", ROW) if c == 0 else low_sb[c]
            nc.gpsimd.tensor_tensor(low_part[c][:, lo:hi], low_sb[c][:, lo:hi], dropped[c][:, lo:hi], ALU.mult)

        z_t = [place([P, blocks, 2, P], F32, f"z_t{half}", f"z_t{half}") for half in range(M // BANK)]
        share = P // PACK

        def add_up(c, halves=(0, 1)):
            for half in halves:
                z_sum = bank([P, blocks, P], f"sum{half}")
                for b in range(blocks):
                    cols = slice(half * BANK + b * P, half * BANK + (b + 1) * P)
                    add_turned(z_sum[:, b, :], [x_part[c][:, cols], low_part[c][:, cols]])
                pairs = z_t[half][:, :, :, share * c : share * (c + 1)].bitcast(BF16)
                nc.scalar.copy(
                    out=pairs.rearrange("m b u (l e) -> m b u l e", e=2),
                    in_=z_sum[:].rearrange("m b (l u e) -> m b u l e", u=2, e=2),
                )

        w2_codes = place([P, PASSES, N], U32, "w2_codes", "w2_codes")
        w2_sc = place([P, PASSES, N], U8, "w2_sc", "w2_sc")
        w2_bf = place([P, PASSES, N, PACK], BF16, "w2_bf", "w2_bf")

        def round_w2(g):
            w2_rows = place([P, PACK, N], F32, f"w2_rows{g}", f"shares{g + 1}")
            rows = w2[g * UPPER_ROW : (g + 1) * UPPER_ROW, :]
            if g == 0:
                nc.sync.dma_start(out=w2_rows[:], in_=rows.rearrange("(p t) n -> p t n", t=PACK))
            else:
                for t in range(PACK):
                    nc.sync.dma_start(out=w2_rows[:, t, :], in_=dealt_rows(rows, t))
            nc.scalar.copy(out=w2_bf[:, g, :, :], in_=w2_rows[:].rearrange("p t n -> p n t"))

        first_product(0)
        first_product(1)
        for lo, hi in FIRST_PARTS:
            for c in range(HEAD_TILES):
                if (c, lo) != (0, 0):
                    weigh(c, lo, hi)
                scatter(c, lo, hi)
        bias_sb = place([P, PASSES, 4 * PACK], F32, "bias_sb", "bias")
        with nc.allow_non_contiguous_dma(reason="one value of the bias for each partition and row tile"):
            nc.sync.dma_start(out=bias_sb[:, 0, 0:PACK], in_=bias[0:UPPER_ROW].rearrange("(c p) -> p c", p=P))
            for e in range(RUN):
                nc.sync.dma_start(
                    out=bias_sb[e:P:RUN, 1, 0:PACK],
                    in_=bias[UPPER_ROW:].rearrange("(a t e) -> e a t", t=PACK, e=RUN)[e],
                )
        for t in range(PACK):
            load_wgs_dealt(t)
        for c in range(HEAD_TILES, LOWER):
            first_product(c)
            weigh(c)
            scatter(c)
        deal_w1()
        for c in range(LOWER, ROW_TILES):
            first_product(c)
            weigh(c)
        nc.scalar.copy(out=ident_bf[:], in_=ident[:])
        neg_bias = own([P, PACK], F32, "neg_bias")
        nc.scalar.activation(out=neg_bias[:], in_=bias_sb[:, 1, 0:PACK], func=COPY, scale=-1.0)
        for c in range(LOWER):
            load_low(c)
        bias_wide = own([P, PACK, BANK], F32, "bias_wide")
        nc.scalar.copy(out=bias_wide[:], in_=bias_sb[:, 1, 0:PACK].unsqueeze(2).to_broadcast([P, PACK, BANK]))

        for c in range(LOWER):
            gather(c)
        for c in range(LOWER):
            compare(c)
        for c in range(LOWER):
            choose(c)
            load_page(LOWER + c)
            scatter(LOWER + c)
            add_up(c)
        floors = place([P, PACK, M], F32, "floors", "floors")
        for t in range(PACK):
            nc.sync.dma_start(out=floors[:, t, :], in_=dealt_rows(low[UPPER_ROW:, :], t))
            nc.scalar.activation(out=floors[:, t, :], in_=floors[:, t, :], func=IDENTITY, bias=neg_bias[:, t : t + 1])
        for g in range(PASSES):
            round_w2(g)
        nc.vector.quantize_mx(
            out=w2_codes[:].rearrange("p g n -> p (g n)").bitcast(FP8X4),
            scales=w2_sc[:].rearrange("p g n -> p (g n)"),
            in_=w2_bf[:].rearrange("p g n t -> p (g n t)"),
        )

        z_sc = [own([P, M], U8, f"z_sc{g}") for g in range(PASSES)]
        woven_lower = {}

        def weave_lower(lo, hi):
            woven_lower[lo] = place([P, (hi - lo) * PACK], BF16, f"woven0_{lo}", "h0", lo * PACK * 2)
            for at in range(lo, hi, PIECE):
                back = bank([P, PIECE // P, 2, P], f"back{at // PIECE % 2}")
                for b in range(PIECE // P):
                    for u in range(2):
                        nc.tensor.transpose(back[:, b, u, :], z_t[at // BANK][:, at % BANK // P + b, u, :], ident[:])
                pairs = woven_lower[lo][:, (at - lo) * PACK : (at - lo + PIECE) * PACK].bitcast(F32)
                nc.scalar.copy(
                    out=pairs.rearrange("p (b m u) -> p b m u", b=PIECE // P, u=2),
                    in_=back[:].rearrange("p b u m -> p b m u"),
                )

        for lo, hi in PIECES:
            weave_lower(lo, hi)

        z_codes = {}

        def quantise(g, lo, hi, woven):
            region, shift = (("wgs", 0), ("h2", 0))[g]
            z_codes[(g, lo)] = place([P, hi - lo], U32, f"z_codes{g}_{lo}", region, shift + 4 * lo)
            nc.vector.quantize_mx(out=z_codes[(g, lo)][:].bitcast(FP8X4), scales=z_sc[g][:, lo:hi], in_=woven)

        out_view = out.rearrange("(j p) m -> p j m", p=P)
        sums = {}

        def groups(span):
            lo, hi = SPANS[span]
            size = 1 if hi - lo == BANK else 2
            return [range(j, j + size) for j in range(0, N // P, size)]

        def product(span):
            lo, hi = SPANS[span]
            at = max(first for first, end in PIECES if first <= lo)
            moving = [z_codes[(0, at)][:, lo - at : hi - at], z_codes[(1, lo)][:]]
            for number, group in enumerate(groups(span)):
                out_sum = bank([P, len(group), hi - lo], ("bank", "sum", "back", "bank")[span] + str(number))
                for g in range(PASSES):
                    for j in group:
                        n_cols = slice(j * P, (j + 1) * P)
                        nc.tensor.matmul_mx(
                            out=out_sum[:, j - group[0], :],
                            lhsT=w2_codes[:, g, n_cols].bitcast(FP8X4),
                            lhsT_scale=w2_sc[:, g, n_cols],
                            rhs=moving[g].bitcast(FP8X4),
                            rhs_scale=z_sc[g][:, lo:hi],
                            start=(g == 0 and j == group[0]),
                            stop=(g == PASSES - 1 and j == group[-1]),
                        )
                sums[(span, number)] = out_sum

        result_place = [("w2_bf", 0), ("h3", 0), ("h4", 0), ("h4", ROW // 2)]

        def store(span, engine_copies):
            lo, hi = SPANS[span]
            region, shift = result_place[span]
            for number, group in enumerate(groups(span)):
                size = 4 * len(group) * (hi - lo)
                result = place([P, len(group), hi - lo], F32, f"result{span}_{number}", region, shift + number * size)
                engine_copies[number % 2](out=result[:], in_=sums[(span, number)][:])
                nc.sync.dma_start(out=out_view[:, group[0] : group[-1] + 1, lo:hi], in_=result[:])

        shifted_place = [("shares3", 0), ("z_t0", 0), ("z_t1", 0)]
        shifted = [
            place([P, PACK, hi - lo], F32, f"shifted{piece}", *shifted_place[piece]) for piece, (lo, hi) in enumerate(PIECES)
        ]

        def pick(piece, t):
            lo, hi = PIECES[piece]
            nc.vector.tensor_tensor(
                shifted[piece][:, t, :],
                pages[LOWER + t][:].indirect(entries(idx3, lo, hi)),
                bias_wide[:, t, 0 : hi - lo],
                ALU.subtract,
            )

        def floored_woven(span):
            lo, hi = SPANS[span]
            piece = min(span, len(PIECES) - 1)
            at = PIECES[piece][0]
            region, shift = ("low3", 0) if span == 0 else ("h5", (lo - BANK) * PACK * 2)
            woven = place([P, hi - lo, PACK], BF16, f"woven1_{lo}", region, shift)
            nc.vector.tensor_tensor(
                woven[:].rearrange("p (c i) t -> p c t i", i=PACK),
                shifted[piece][:, :, lo - at : hi - at].rearrange("p t (c i) -> p c t i", i=PACK),
                floors[:, :, lo:hi].rearrange("p t (c i) -> p c t i", i=PACK),
                ALU.max,
            )
            return woven[:].rearrange("p m t -> p (m t)")

        for piece in range(len(PIECES)):
            pick(piece, 0)
            if piece > 0:
                woven = floored_woven(piece - 1)
            pick(piece, 1)
            if piece > 0:
                quantise(0, *PIECES[piece - 1], woven_lower[PIECES[piece - 1][0]][:])
                quantise(1, *SPANS[piece - 1], woven)
                product(piece - 1)
                store(piece - 1, (nc.scalar.copy, nc.scalar.copy))
            pick(piece, 2)
            pick(piece, 3)
        lo, hi = PIECES[-1]
        quantise(0, lo, hi, woven_lower[lo][:])
        last_spans = (len(SPANS) - 2, len(SPANS) - 1)
        woven = {s: floored_woven(s) for s in last_spans}
        for s in last_spans:
            quantise(1, *SPANS[s], woven[s])
        for s in last_spans:
            product(s)
        for s in last_spans:
            store(s, (nc.scalar.copy, nc.vector.tensor_copy))
